import numpy as np
import ml_dtypes


def mxq(x, axis, fmt="e4m3"):
    dtype, down = {"e4m3": (ml_dtypes.float8_e4m3fn, 7), "e5m2": (ml_dtypes.float8_e5m2, 14)}[fmt]
    v = np.moveaxis(np.asarray(x, np.float32).astype(ml_dtypes.bfloat16).astype(np.float64), axis, -1)
    blocks = v.reshape(v.shape[:-1] + (-1, 32))
    amax = np.abs(blocks).max(-1, keepdims=True)
    byte = np.maximum(np.where(amax > 0, np.frexp(amax)[1] - 1 + 127, 0) - down, 1)
    scale = np.exp2(byte - 127.0)
    codes = (blocks / scale).astype(np.float32).astype(dtype).astype(np.float64)
    return np.moveaxis((codes * scale).reshape(v.shape), -1, axis)


WIDE = False


def mx_kscale(k):
    if not WIDE:
        return np.ones(k)
    levels = np.array([10, -10, 5, -5, 0])
    if k % 512:
        return np.exp2(np.random.permutation(np.resize(levels, k // 32))).repeat(32)
    a = np.empty((k // 512, 16))
    for p in range(k // 512):
        a[p, :8] = np.random.permutation(np.resize(levels, 8))
        for g in range(8):
            far = levels[np.abs(levels - a[p, g]) >= 10]
            a[p, g + 8] = far[np.random.randint(len(far))]
    return np.exp2(a.ravel()).repeat(32)


BF16 = ml_dtypes.bfloat16


def bf(x):
    return np.asarray(x, np.float32).astype(BF16)


def f64(x):
    return np.asarray(x).astype(np.float64)


E2M1 = np.array([0.0, 0.5, 1.0, 1.5, 2.0, 3.0, 4.0, 6.0, -0.0, -0.5, -1.0, -1.5, -2.0, -3.0, -4.0, -6.0])


def pack_weight(w, fmt):
    k, n = w.shape
    w = f64(bf(w)).reshape(k // 32, 32, n)
    amax = np.abs(w).max(1)
    if fmt == "e4m3":
        byte = np.frexp(amax)[1] - 1 + 127 - 7
    else:
        mant, ex = np.frexp(amax / 6.0)
        byte = np.where(mant > 0.5, ex, ex - 1) + 127
    byte = np.clip(np.where(amax > 0, byte, 1), 1, 254)
    scaled = (w * np.exp2(127.0 - byte)[:, None, :]).reshape(k, n).astype(np.float32)
    by_word = np.ascontiguousarray(scaled.reshape(k // 512, 128, 4, n).transpose(0, 1, 3, 2))
    if fmt == "e4m3":
        words = by_word.astype(ml_dtypes.float8_e4m3fn).view(np.uint8)
    else:
        c = by_word.astype(ml_dtypes.float4_e2m1fn).view(np.uint8) & 0xF
        words = c[..., 0::2] | (c[..., 1::2] << 4)
    return np.ascontiguousarray(words), np.ascontiguousarray(byte.astype(np.uint8).reshape(k // 512, 16, n))


def unpack_weight(words, scales, fmt):
    g, p, n, _ = words.shape
    if fmt == "e4m3":
        vals = np.ascontiguousarray(words).view(ml_dtypes.float8_e4m3fn).astype(np.float64)
    else:
        nib = np.empty((g, p, n, 4), np.uint8)
        nib[..., 0::2] = words & 0xF
        nib[..., 1::2] = words >> 4
        vals = E2M1[nib]
    vals = vals * np.repeat(np.exp2(scales.astype(np.float64) - 127.0), 8, axis=1)[..., None]
    return vals.transpose(0, 1, 3, 2).reshape(g * 512, n)
def pack4(w):
    words, scales = pack_weight(w, "e2m1")
    return words.reshape(words.shape[0], 128, -1), scales


def unpack4(words, scales):
    return unpack_weight(words.reshape(words.shape[0], 128, -1, 2), scales, "e2m1")


B, V, H = 2048, 1024, 512


def draw0():
    c = mx_kscale(H)
    t = mx_kscale(B)
    u = mx_kscale(B)
    v = bf(np.random.uniform(-1.0, 1.0, (B, V)) * u[:, None])
    hp = bf(np.random.uniform(-1.0, 1.0, (B, H)) / u[:, None])
    hf = bf(np.random.uniform(-1.0, 1.0, (B, H)) * c)
    hn = bf(np.random.uniform(-1.0, 1.0, (B, H)) / t[:, None])
    w = np.random.standard_normal((V, H)) * 2.0 / np.sqrt(H) / c
    w_words, w_scales = pack4(w.T)
    return {"v": v,
            "hp": hp,
            "hf": hf,
            "hn": hn,
            "w_words": w_words,
            "w_scales": w_scales,
            "b": bf(0.3 * np.random.standard_normal(V)),
            "s": bf((1.0 + 0.1 * np.random.standard_normal(B)) * t)}


def visible_mean_field(h, w_t, b):
    return np.tanh((mxq(h, 1, "e4m3") @ w_t) + b)


def correlation(vis, hid):
    return mxq(vis, 0, "e4m3").T @ mxq(hid, 0, "e4m3")


def core(v, hp, hf, hn, w_words, w_scales, b, s):
    n_rows = v.shape[0]
    v1 = visible_mean_field(f64(hf), unpack4(w_words, w_scales), f64(b))
    v1s = f64(s)[:, None] * v1
    neg = correlation(v1s, f64(hn))
    pos = correlation(f64(v), f64(hp))
    g = (pos - neg) / np.sqrt(n_rows)
    return g


def e4m3fn_bytes(y):
    return np.clip(np.asarray(y, np.float64), -448.0, 448.0).astype(np.float32).astype(ml_dtypes.float8_e4m3fn).view(np.uint8)


def e4m3fn_values(b):
    return np.asarray(b, np.uint8).view(ml_dtypes.float8_e4m3fn).astype(np.float64)


def setup_inputs():
    d = draw0()
    x0 = np.asarray(d['v']).astype(np.float64)
    s = (np.max(np.abs(x0), axis=(1,), keepdims=True) / 448.0).astype(np.float32)
    out = {}
    for k, v in d.items():
        if k == 'v':
            out['v_bytes'] = e4m3fn_bytes(x0 / s.astype(np.float64))
            out['v_scale'] = s
        else:
            out[k] = v
    return out


def reference(v_bytes, v_scale, hp, hf, hn, w_words, w_scales, b, s):
    return core(e4m3fn_values(v_bytes) * v_scale.astype(np.float64), hp, hf, hn, w_words, w_scales, b, s)

@@ -1,0 +1,426 @@
+from contextlib import ExitStack
+
+import concourse.mybir as mybir
+from concourse.masks import make_identity
+
+B, V, H = 2048, 1024, 512
+FLOPS = 3 * 2 * B * V * H
+
+F32 = mybir.dt.float32
+BF16 = mybir.dt.bfloat16
+U32 = mybir.dt.uint32
+I32 = mybir.dt.int32
+U8 = mybir.dt.uint8
+E4M3 = mybir.dt.float8_e4m3fn
+E4M3X4 = mybir.dt.float8_e4m3fn_x4
+E2M1X4 = mybir.dt.float4_e2m1fn_x4
+ACT = mybir.ActivationFunctionType
+ALU = mybir.AluOpType
+
+P = 128
+G = 4
+MT = V // P
+HALF = MT // 2
+S_SHARE = ((2, 1), (2, 2), (2, 3), (3, 0), (3, 1), (3, 2))
+G_SHARE = ((0, 3),)
+V_OUT = (5, 6)
+STORE_AT = ((0, 13), (1, 13), (2, 14), (3, 14), (4, 15), (5, 15), (6, 15), (7, 15))
+WIDEN_PER_JOB = 4
+GP_COLS = 128
+V1Q = 4
+GP_LATE = (3,)
+S_HP = (2,)
+V_HP = ()
+V_N0 = 0
+HQ_AT = (2, 7, 14)
+WIDEN_AT = {}
+TR_AT = {1: 1, 4: 2, 8: 3}
+HEAD_WIDEN = (0, 0, 0)
+LOADS = ('hf0a', 'hf0b', 'w', 'wsc', 'hn0', 'hf1', 'v0', 'hn1', 'hn3', 'v1', 'hf2', 'hn2', 'hp2', 'v2', 'hp3', 'hp0', 'hf3', 'hp1', 'v3')
+
+
+def tile_persistentmeanfieldisingrbmgradient_w4_kernel(
+    tc, v_bytes, v_scale, hp, hf, hn, w_words, w_scales, b, s, out
+):
+    nc = tc.nc
+    with ExitStack() as ctx:
+        keep = ctx.enter_context(tc.tile_pool(name="keep", bufs=1))
+        ring = ctx.enter_context(tc.tile_pool(name="ring", bufs=4))
+        psum = ctx.enter_context(tc.psum_pool(name="psum", bufs=1))
+
+        def kt(name, shape, dtype):
+            return keep.tile(shape, dtype, name=name, align_bytes=256)
+
+        counts = {"f": 0, "t": 0}
+
+        def bank(kind, shape):
+            i = counts[kind] % 4
+            counts[kind] = counts[kind] + 1
+            nm = kind + str(i)
+            return psum.tile(shape, F32, name=nm, tag=nm)
+
+        def r4(nm):
+            return ring.tile([P, 4, 512], BF16, name=nm, tag="r4", bufs=12, align_bytes=256)
+
+        def grp(nm):
+            return ring.tile([P, 2048], BF16, name=nm, tag="grp", bufs=2, align_bytes=256)
+
+        hf_raw = [r4("hf_raw%d" % g) for g in range(G)]
+        hn_raw = [r4("hn_raw%d" % g) for g in range(G)]
+        hp_raw = [r4("hp_raw%d" % g) for g in range(G)]
+        v_raw = [kt("v_raw%d" % g, [P, 4, V], U8) for g in range(G)]
+        hf_codes = [kt("hf_codes%d" % g, [P, 512], U32) for g in range(G)]
+        hf_sc = [kt("hf_sc%d" % g, [P, 512], U8) for g in range(G)]
+        hn_codes = [kt("hn_codes%d" % g, [P, H], U32) for g in range(G)]
+        hn_sc = [kt("hn_sc%d" % g, [P, H], U8) for g in range(G)]
+        hp_codes = [kt("hp_codes%d" % g, [P, H], U32) for g in range(G)]
+        hp_sc = [kt("hp_sc%d" % g, [P, H], U8) for g in range(G)]
+        v1_codes = [kt("v1_codes%d" % g, [P, V], U32) for g in range(G)]
+        v1_sc = [kt("v1_sc%d" % g, [P, V], U8) for g in range(G)]
+        v_codes = [kt("v_codes%d" % g, [P, V], U32) for g in range(G)]
+        v_sc = [kt("v_sc%d" % g, [P, V], U8) for g in range(G)]
+        w_codes = kt("w_codes", [P, 2 * V], U8)
+        w_sc = kt("w_sc", [P, V], U8)
+        ident = kt("ident", [P, P], F32)
+        b_rows = kt("b_rows", [P, P], BF16)
+        b_rows32 = kt("b_rows32", [P, P], F32)
+        bias = kt("bias", [P, MT], F32)
+        s_bf = kt("s_bf", [P, G, 4], BF16)
+        s_neg = kt("s_neg", [P, G, 4], F32)
+        vs = kt("vs", [P, G, 4], F32)
+        warm = kt("warm", [P, 1], F32)
+
+        with tc.manual_schedule():
+            nc.vector.memset(b_rows[:], 0.0)
+            nc.vector.memset(w_sc[:].bitcast(I32), 0)
+            nc.vector.memset(warm[:], 0.0)
+            make_identity(nc, ident[:])
+            nc.scalar.dma_start(out=b_rows[0:MT, :], in_=b.rearrange("(m c) -> m c", c=P))
+            nc.scalar.dma_start(out=s_bf[:], in_=s.rearrange("(g p t) -> p g t", p=P, t=4))
+            nc.gpsimd.dma_start(out=vs[:], in_=v_scale.rearrange("(g p t) o -> p g (t o)", p=P, t=4))
+            nc.scalar.activation(warm[:], warm[:], ACT.Tanh)
+
+            def rows(x, g):
+                return x.rearrange("(g p t) k -> g p t k", p=P, t=4)[g]
+
+            big = {"hf": (hf_raw, hf), "hn": (hn_raw, hn), "hp": (hp_raw, hp), "v": (v_raw, v_bytes)}
+            for nm in LOADS:
+                if nm == "hf0a":
+                    nc.sync.dma_start(out=hf_raw[0][:, 0:2, :], in_=rows(hf, 0)[:, 0:2, :])
+                elif nm == "hf0b":
+                    nc.sync.dma_start(out=hf_raw[0][:, 2:4, :], in_=rows(hf, 0)[:, 2:4, :])
+                elif nm == "w":
+                    nc.sync.dma_start(out=w_codes[:], in_=w_words[0])
+                elif nm == "wsc":
+                    for q in range(4):
+                        nc.sync.dma_start(
+                            out=w_sc[32 * q : 32 * q + 4, :].bitcast(I32),
+                            in_=w_scales[0][4 * q : 4 * q + 4, :].bitcast(I32),
+                        )
+                else:
+                    dst, x = big[nm[:-1]]
+                    nc.sync.dma_start(out=dst[int(nm[-1])][:], in_=rows(x, int(nm[-1])))
+
+            hf_grp = {}
+
+            tr_bank = {}
+
+            def hf_turn(g, h):
+                if h == 0:
+                    hf_grp[g] = grp("hf_grp%d" % g)
+                bk = bank("t", [P, 2, 2, P])
+                tr_bank[(g, h)] = bk
+                words = hf_raw[g][:].rearrange("p t k -> p (t k)").bitcast(F32)
+                for i in range(2):
+                    for u in range(2):
+                        base = 256 * (2 * h + i)
+                        nc.tensor.transpose(bk[:, i, u, :], words[:, base + u : base + 256 : 2], ident[:])
+
+            def hf_out(g, h):
+                dst = hf_grp[g][:, 1024 * h : 1024 * h + 1024].bitcast(F32).rearrange(
+                    "p (i m u) -> p i m u", i=2, u=2
+                )
+                src = tr_bank[(g, h)][:].rearrange("p i u m -> p i m u")
+                if h == 0:
+                    nc.vector.tensor_copy(out=dst, in_=src)
+                else:
+                    nc.scalar.copy(out=dst, in_=src)
+
+            def hf_quant(g, h):
+                nc.vector.quantize_mx(
+                    out=hf_codes[g][:, 256 * h : 256 * h + 256].bitcast(E4M3X4),
+                    scales=hf_sc[g][:, 256 * h : 256 * h + 256],
+                    in_=hf_grp[g][:, 1024 * h : 1024 * h + 1024],
+                )
+
+            f_bank = {}
+            th = {}
+            t_bank = {}
+            v1_grp = {}
+
+            def field(u):
+                g, m = u // MT, u % MT
+                f_bank[u] = bank("f", [P, 512])
+                nc.tensor.matmul_mx(
+                    out=f_bank[u][:],
+                    lhsT=w_codes[:, 256 * m : 256 * m + 256].bitcast(E2M1X4),
+                    lhsT_scale=w_sc[:, P * m : P * m + P],
+                    rhs=hf_codes[g][:].bitcast(E4M3X4),
+                    rhs_scale=hf_sc[g][:],
+                    start=True,
+                    stop=True,
+                )
+
+            def tanh(u):
+                m = u % MT
+                th[u] = ring.tile([P, 4, P], F32, name="th%d" % u, tag="th", bufs=8)
+                nc.scalar.activation(
+                    th[u][:].rearrange("p t q -> p (t q)"), f_bank[u][:], ACT.Tanh, bias=bias[:, m : m + 1]
+                )
+
+            def turn(u):
+                t_bank[u] = bank("t", [P, 4, P])
+                for t in range(4):
+                    nc.tensor.transpose(t_bank[u][:, t, :], th[u][:, t, :], ident[:])
+
+            def weight(u):
+                g, m = u // MT, u % MT
+                if m == 0:
+                    v1_grp[g] = ring.tile([P, 4096], BF16, name="v1_grp%d" % g, tag="v1_grp", bufs=2, align_bytes=256)
+                nc.vector.tensor_tensor(
+                    out=v1_grp[g][:, 512 * m : 512 * m + 512].rearrange("p (q t) -> p q t", t=4),
+                    in0=t_bank[u][:].rearrange("p t q -> p q t"),
+                    in1=s_neg[:, g, :].unsqueeze(1).to_broadcast([P, P, 4]),
+                    op=ALU.mult,
+                )
+
+            def v1_quant(g, c0, n):
+                nc.vector.quantize_mx(
+                    out=v1_codes[g][:, P * c0 : P * (c0 + n)].bitcast(E4M3X4),
+                    scales=v1_sc[g][:, P * c0 : P * (c0 + n)],
+                    in_=v1_grp[g][:, 512 * c0 : 512 * (c0 + n)],
+                )
+
+            h_grp = {}
+
+            def h_new(nm, g):
+                h_grp[(nm, g)] = ring.tile(
+                    [P, 2048], BF16, name="h_grp_%s%d" % (nm, g), tag="h_grp", bufs=6, align_bytes=256
+                )
+
+            def h_mix_gp(nm, raw, g, c0, n):
+                nc.gpsimd.tensor_scalar(
+                    out=h_grp[(nm, g)][:, 4 * c0 : 4 * (c0 + n)].rearrange("p (c t) -> p c t", t=4),
+                    in0=raw[g][:, :, c0 : c0 + n].rearrange("p t c -> p c t"),
+                    scalar1=1.0,
+                    scalar2=0.0,
+                    op0=ALU.mult,
+                    op1=ALU.add,
+                )
+
+            def mix_views(dst, src):
+                return (
+                    dst.rearrange("p (c i t) -> p c t i", i=4, t=4),
+                    src.rearrange("p t (c i) -> p c t i", i=4),
+                )
+
+            def h_mix_v(nm, raw, g):
+                d, sr = mix_views(h_grp[(nm, g)][:], raw[g][:])
+                nc.vector.tensor_copy(out=d, in_=sr)
+
+            def h_quant(nm, codes, sc, g):
+                nc.vector.quantize_mx(out=codes[g][:].bitcast(E4M3X4), scales=sc[g][:], in_=h_grp[(nm, g)][:])
+
+            v_wide = {}
+            v_grp = {}
+
+            def widen(h, g, t):
+                if t == 0:
+                    v_wide[(h, g)] = r4("v_wide%d_%d" % (h, g))
+                nc.scalar.activation(
+                    v_wide[(h, g)][:, t, :],
+                    v_raw[g][:, t, 512 * h : 512 * h + 512].bitcast(E4M3),
+                    ACT.Copy,
+                    scale=vs[:, g, t : t + 1],
+                )
+
+            def v_mix(mp, g, c):
+                if c == 0:
+                    v_grp[(mp, g)] = ring.tile(
+                        [P, 1024], BF16, name="v_grp%d_%d" % (mp, g), tag="v_grp", bufs=5, align_bytes=256
+                    )
+                c0 = P * (2 * (mp % 2) + c)
+                dst = v_grp[(mp, g)][:, 512 * c : 512 * c + 512]
+                src = v_wide[(mp // 2, g)][:, :, c0 : c0 + P]
+                d, sr = mix_views(dst, src)
+                if c == 1 and (mp, g) in S_SHARE:
+                    nc.scalar.copy(out=d, in_=sr)
+                elif (mp, g) in G_SHARE:
+                    nc.gpsimd.tensor_scalar(
+                        out=dst.rearrange("p (c t) -> p c t", t=4),
+                        in0=src.rearrange("p t c -> p c t"),
+                        scalar1=1.0,
+                        scalar2=0.0,
+                        op0=ALU.mult,
+                        op1=ALU.add,
+                    )
+                else:
+                    nc.vector.tensor_copy(out=d, in_=sr)
+
+            def v_quant(mp, g):
+                c0 = 256 * mp
+                nc.vector.quantize_mx(
+                    out=v_codes[g][:, c0 : c0 + 256].bitcast(E4M3X4),
+                    scales=v_sc[g][:, c0 : c0 + 256],
+                    in_=v_grp[(mp, g)][:],
+                )
+
+            def h_mix_s(nm, raw, g):
+                h_new(nm, g)
+                d, sr = mix_views(h_grp[(nm, g)][:], raw[g][:])
+                nc.scalar.copy(out=d, in_=sr)
+
+            def quant_hn(g):
+                h_quant("n", hn_codes, hn_sc, g)
+
+            def quant_hp(g):
+                h_quant("p", hp_codes, hp_sc, g)
+
+            def mix_gp(nm, raw, g):
+                h_new(nm, g)
+                for c in range(H // GP_COLS):
+                    h_mix_gp(nm, raw, g, GP_COLS * c, GP_COLS)
+
+            if not V_N0:
+                mix_gp("n", hn_raw, 0)
+            mix_gp("n", hn_raw, 1)
+            mix_gp("n", hn_raw, 2)
+            mix_gp("n", hn_raw, 3)
+
+            widen_list = [(h, g, t) for h in range(2) for g in range(G) for t in range(4)]
+            done = [0]
+
+            def widen_some(n):
+                for k in range(n):
+                    if done[0] < len(widen_list):
+                        widen(*widen_list[done[0]])
+                        done[0] = done[0] + 1
+
+            hf_turn(0, 0)
+            hf_turn(0, 1)
+            hf_out(0, 0)
+            hf_out(0, 1)
+            nc.vector.tensor_copy(out=b_rows32[:], in_=b_rows[:])
+            hf_quant(0, 0)
+            b_bank = bank("t", [P, P])
+            nc.tensor.transpose(b_bank[:], b_rows32[:], ident[:])
+            nc.vector.tensor_copy(out=bias[:], in_=b_bank[:, 0:MT])
+            hf_quant(0, 1)
+            nc.vector.tensor_scalar(
+                out=s_neg[:], in0=s_bf[:], scalar1=-1.0, scalar2=None, op0=ALU.mult
+            )
+            widen_some(HEAD_WIDEN[0])
+            for u in range(4):
+                field(u)
+            widen_some(HEAD_WIDEN[1])
+            if V_N0:
+                h_new("n", 0)
+                h_mix_v("n", hn_raw, 0)
+            tanh(0)
+            tanh(1)
+            mix_gp("p", hp_raw, 0)
+            mix_gp("p", hp_raw, 1)
+
+            hq = [(quant_hn, 0), (quant_hn, 1), (quant_hn, 2), (quant_hn, 3), (quant_hp, 0), (quant_hp, 1), (quant_hp, 2), (quant_hp, 3)]
+            nq = 0
+            npairs = G * MT // 2
+            for j in range(npairs):
+                hg = TR_AT.get(j, 0)
+                if hg:
+                    hf_turn(hg, 0)
+                    hf_turn(hg, 1)
+                    hf_out(hg, 0)
+                    hf_out(hg, 1)
+                turn(2 * j)
+                turn(2 * j + 1)
+                if j + 2 < npairs:
+                    field(2 * j + 4)
+                    field(2 * j + 5)
+                if j + 1 < npairs:
+                    tanh(2 * j + 2)
+                    tanh(2 * j + 3)
+                weight(2 * j)
+                if hg:
+                    nc.vector.quantize_mx(
+                        out=hf_codes[hg][:].bitcast(E4M3X4), scales=hf_sc[hg][:], in_=hf_grp[hg][:]
+                    )
+                if V1Q == 8 and j % 4 == 0 and j > 0:
+                    v1_quant(j // 4 - 1, 0, 8)
+                if V1Q == 4 and j % 2 == 0 and j > 0:
+                    v1_quant((j - 2) // 4, 4 * ((j - 2) // 2 % 2), 4)
+                weight(2 * j + 1)
+                if j in HQ_AT:
+                    hq[nq][0](hq[nq][1])
+                    nq = nq + 1
+                widen_some(WIDEN_AT.get(j, 1))
+            for g in GP_LATE:
+                mix_gp("p", hp_raw, g)
+            v1_quant(G - 1, 8 - V1Q, V1Q)
+
+            acc = [bank("f", [P, H]) for m in range(HALF)] + [bank("t", [P, H]) for m in range(HALF)]
+
+            def one_pass(m, codes, sc, rc, rs, g, first, last):
+                c0 = P * m
+                nc.tensor.matmul_mx(
+                    out=acc[m][:],
+                    lhsT=codes[g][:, c0 : c0 + P].bitcast(E4M3X4),
+                    lhsT_scale=sc[g][:, c0 : c0 + P],
+                    rhs=rc[g][:].bitcast(E4M3X4),
+                    rhs_scale=rs[g][:],
+                    start=first,
+                    stop=last,
+                )
+
+            def store(m):
+                res = ring.tile([P, H], F32, name="res%d" % m, tag="th", bufs=8)
+                if m in V_OUT:
+                    nc.vector.tensor_scalar(
+                        out=res[:], in0=acc[m][:], scalar1=float(B) ** -0.5, scalar2=None, op0=ALU.mult
+                    )
+                else:
+                    nc.scalar.activation(res[:], acc[m][:], ACT.Copy, scale=float(B) ** -0.5)
+                nc.sync.dma_start(out=out[P * m : P * m + P, :], in_=res[:])
+
+            while nq < 4:
+                hq[nq][0](hq[nq][1])
+                nq = nq + 1
+            for g in range(G):
+                for h in range(2):
+                    for mm in range(HALF):
+                        one_pass(HALF * h + mm, v1_codes, v1_sc, hn_codes, hn_sc, g, g == 0, False)
+            for g in S_HP:
+                h_mix_s("p", hp_raw, g)
+            jobs = [(mp, g) for mp in range(4) for g in range(G)]
+
+            def mix_job(i):
+                for c in range(2):
+                    v_mix(jobs[i][0], jobs[i][1], c)
+
+            for g in V_HP:
+                h_new("p", g)
+                h_mix_v("p", hp_raw, g)
+            mix_job(0)
+            for i in range(len(jobs)):
+                widen_some(WIDEN_PER_JOB)
+                if i + 1 < len(jobs):
+                    mix_job(i + 1)
+                v_quant(*jobs[i])
+                if nq < len(hq):
+                    hq[nq][0](hq[nq][1])
+                    nq = nq + 1
+                mp, g = jobs[i]
+                for c in range(2):
+                    one_pass(2 * mp + c, v_codes, v_sc, hp_codes, hp_sc, g, False, g == G - 1)
+                for (m, at) in STORE_AT:
+                    if at == i:
+                        store(m)

@@ -20,23 +20,12 @@ ALU = mybir.AluOpType
 P = 128
 G = 4
 MT = V // P
-HALF = MT // 2
-S_SHARE = ((2, 1), (2, 2), (2, 3), (3, 0), (3, 1), (3, 2))
-G_SHARE = ((0, 3),)
-V_OUT = (5, 6)
-STORE_AT = ((0, 13), (1, 13), (2, 14), (3, 14), (4, 15), (5, 15), (6, 15), (7, 15))
-WIDEN_PER_JOB = 4
-GP_COLS = 128
-V1Q = 4
-GP_LATE = (3,)
-S_HP = (2,)
-V_HP = ()
-V_N0 = 0
-HQ_AT = (2, 7, 14)
-WIDEN_AT = {}
-TR_AT = {1: 1, 4: 2, 8: 3}
-HEAD_WIDEN = (0, 0, 0)
-LOADS = ('hf0a', 'hf0b', 'w', 'wsc', 'hn0', 'hf1', 'v0', 'hn1', 'hn3', 'v1', 'hf2', 'hn2', 'hp2', 'v2', 'hp3', 'hp0', 'hf3', 'hp1', 'v3')
+PAIRS = G * MT // 2
+HEAD_WIDEN = 6
+S_MIX = 2
+T_BANKS = 5
+EARLY = 99
+GP_COLS = 768
 
 
 def tile_persistentmeanfieldisingrbmgradient_w4_kernel(
@@ -45,30 +34,29 @@ def tile_persistentmeanfieldisingrbmgradient_w4_kernel(
     nc = tc.nc
     with ExitStack() as ctx:
         keep = ctx.enter_context(tc.tile_pool(name="keep", bufs=1))
-        ring = ctx.enter_context(tc.tile_pool(name="ring", bufs=4))
+        ring = ctx.enter_context(tc.tile_pool(name="ring", bufs=1))
         psum = ctx.enter_context(tc.psum_pool(name="psum", bufs=1))
 
         def kt(name, shape, dtype):
             return keep.tile(shape, dtype, name=name, align_bytes=256)
 
-        counts = {"f": 0, "t": 0}
+        rings = {"t": ["bank%d" % i for i in range(T_BANKS)], "f": ["bank%d" % i for i in range(T_BANKS, 8)]}
 
-        def bank(kind, shape):
-            i = counts[kind] % 4
-            counts[kind] = counts[kind] + 1
-            nm = kind + str(i)
+        def bank(kind, shape, keep_it=False):
+            nm = rings[kind][0]
+            rings[kind].remove(nm)
+            if not keep_it:
+                rings[kind].append(nm)
             return psum.tile(shape, F32, name=nm, tag=nm)
 
-        def r4(nm):
-            return ring.tile([P, 4, 512], BF16, name=nm, tag="r4", bufs=12, align_bytes=256)
+        def rows_tile(name, g):
+            return ring.tile([P, 4, H], BF16, name=name, tag="rows%d" % g, bufs=1, align_bytes=256)
 
-        def grp(nm):
-            return ring.tile([P, 2048], BF16, name=nm, tag="grp", bufs=2, align_bytes=256)
-
-        hf_raw = [r4("hf_raw%d" % g) for g in range(G)]
-        hn_raw = [r4("hn_raw%d" % g) for g in range(G)]
-        hp_raw = [r4("hp_raw%d" % g) for g in range(G)]
+        hf_raw = [rows_tile("hf_raw%d" % g, g) for g in range(G)]
+        h_raw = [kt("h_raw%d" % g, [P, 4, 2 * H], BF16) for g in range(G)]
+        hp_rest = [kt("hp_rest%d" % g, [P, 4 * (2 * H - GP_COLS)], BF16) for g in range(G)]
         v_raw = [kt("v_raw%d" % g, [P, 4, V], U8) for g in range(G)]
+        v_wide = {(0, g): kt("v_wide0_%d" % g, [P, 4, 512], BF16) for g in range(G)}
         hf_codes = [kt("hf_codes%d" % g, [P, 512], U32) for g in range(G)]
         hf_sc = [kt("hf_sc%d" % g, [P, 512], U8) for g in range(G)]
         hn_codes = [kt("hn_codes%d" % g, [P, H], U32) for g in range(G)]
@@ -95,40 +83,52 @@ def tile_persistentmeanfieldisingrbmgradient_w4_kernel(
             nc.vector.memset(w_sc[:].bitcast(I32), 0)
             nc.vector.memset(warm[:], 0.0)
             make_identity(nc, ident[:])
+            nc.scalar.dma_start(out=vs[:], in_=v_scale.rearrange("(g p t) o -> p g (t o)", p=P, t=4))
             nc.scalar.dma_start(out=b_rows[0:MT, :], in_=b.rearrange("(m c) -> m c", c=P))
-            nc.scalar.dma_start(out=s_bf[:], in_=s.rearrange("(g p t) -> p g t", p=P, t=4))
-            nc.gpsimd.dma_start(out=vs[:], in_=v_scale.rearrange("(g p t) o -> p g (t o)", p=P, t=4))
             nc.scalar.activation(warm[:], warm[:], ACT.Tanh)
 
             def rows(x, g):
                 return x.rearrange("(g p t) k -> g p t k", p=P, t=4)[g]
 
-            big = {"hf": (hf_raw, hf), "hn": (hn_raw, hn), "hp": (hp_raw, hp), "v": (v_raw, v_bytes)}
-            for nm in LOADS:
-                if nm == "hf0a":
-                    nc.sync.dma_start(out=hf_raw[0][:, 0:2, :], in_=rows(hf, 0)[:, 0:2, :])
-                elif nm == "hf0b":
-                    nc.sync.dma_start(out=hf_raw[0][:, 2:4, :], in_=rows(hf, 0)[:, 2:4, :])
-                elif nm == "w":
-                    nc.sync.dma_start(out=w_codes[:], in_=w_words[0])
-                elif nm == "wsc":
-                    for q in range(4):
-                        nc.sync.dma_start(
-                            out=w_sc[32 * q : 32 * q + 4, :].bitcast(I32),
-                            in_=w_scales[0][4 * q : 4 * q + 4, :].bitcast(I32),
-                        )
-                else:
-                    dst, x = big[nm[:-1]]
-                    nc.sync.dma_start(out=dst[int(nm[-1])][:], in_=rows(x, int(nm[-1])))
+            def load(dst, x, g):
+                nc.sync.dma_start(out=dst[g][:], in_=rows(x, g))
+
+            def load_half(g, h):
+                nc.sync.dma_start(out=hf_raw[g][:, 2 * h : 2 * h + 2, :], in_=rows(hf, g)[:, 2 * h : 2 * h + 2, :])
+
+            load_half(0, 0)
+            load_half(0, 1)
+            load(v_raw, v_bytes, 0)
+            load_half(1, 0)
+            nc.sync.dma_start(out=w_codes[:], in_=w_words[0])
+            for q in range(4):
+                nc.sync.dma_start(
+                    out=w_sc[32 * q : 32 * q + 4, :].bitcast(I32),
+                    in_=w_scales[0][4 * q : 4 * q + 4, :].bitcast(I32),
+                )
+            load_half(1, 1)
+            nc.sync.dma_start(out=s_bf[:], in_=s.rearrange("(g p t) -> p g t", p=P, t=4))
+            for g in range(G):
+                nc.sync.dma_start(out=h_raw[g][:, :, 0:H], in_=rows(hn, g))
+                nc.sync.dma_start(out=h_raw[g][:, :, H : 2 * H], in_=rows(hp, g))
+                if g + 2 < G:
+                    load(hf_raw, hf, g + 2)
+                if g + 1 < G:
+                    load(v_raw, v_bytes, g + 1)
 
             hf_grp = {}
-
             tr_bank = {}
+
+            def grp(nm):
+                return ring.tile([P, 2048], BF16, name=nm, tag="grp", bufs=2, align_bytes=256)
+
+            def gate(nm):
+                return ring.tile([P, 4 * GP_COLS], BF16, name=nm, tag="gate", bufs=1, align_bytes=256)
 
             def hf_turn(g, h):
                 if h == 0:
-                    hf_grp[g] = grp("hf_grp%d" % g)
-                bk = bank("t", [P, 2, 2, P])
+                    hf_grp[g] = gate("hf_grp1") if g == 1 else grp("hf_grp%d" % g)
+                bk = bank("f" if g > 1 else "t", [P, 2, 2, P])
                 tr_bank[(g, h)] = bk
                 words = hf_raw[g][:].rearrange("p t k -> p (t k)").bitcast(F32)
                 for i in range(2):
@@ -136,22 +136,18 @@ def tile_persistentmeanfieldisingrbmgradient_w4_kernel(
                         base = 256 * (2 * h + i)
                         nc.tensor.transpose(bk[:, i, u, :], words[:, base + u : base + 256 : 2], ident[:])
 
-            def hf_out(g, h):
+            def hf_out(g, h, on_vector):
                 dst = hf_grp[g][:, 1024 * h : 1024 * h + 1024].bitcast(F32).rearrange(
                     "p (i m u) -> p i m u", i=2, u=2
                 )
                 src = tr_bank[(g, h)][:].rearrange("p i u m -> p i m u")
-                if h == 0:
+                if on_vector:
                     nc.vector.tensor_copy(out=dst, in_=src)
                 else:
                     nc.scalar.copy(out=dst, in_=src)
 
-            def hf_quant(g, h):
-                nc.vector.quantize_mx(
-                    out=hf_codes[g][:, 256 * h : 256 * h + 256].bitcast(E4M3X4),
-                    scales=hf_sc[g][:, 256 * h : 256 * h + 256],
-                    in_=hf_grp[g][:, 1024 * h : 1024 * h + 1024],
-                )
+            def quant(codes, sc, c0, n, src):
+                nc.vector.quantize_mx(out=codes[:, c0 : c0 + n].bitcast(E4M3X4), scales=sc[:, c0 : c0 + n], in_=src)
 
             f_bank = {}
             th = {}
@@ -173,7 +169,7 @@ def tile_persistentmeanfieldisingrbmgradient_w4_kernel(
 
             def tanh(u):
                 m = u % MT
-                th[u] = ring.tile([P, 4, P], F32, name="th%d" % u, tag="th", bufs=8)
+                th[u] = ring.tile([P, 4, P], F32, name="th%d" % u, tag="th", bufs=8, align_bytes=256)
                 nc.scalar.activation(
                     th[u][:].rearrange("p t q -> p (t q)"), f_bank[u][:], ACT.Tanh, bias=bias[:, m : m + 1]
                 )
@@ -185,189 +181,97 @@ def tile_persistentmeanfieldisingrbmgradient_w4_kernel(
 
             def weight(u):
                 g, m = u // MT, u % MT
-                if m == 0:
-                    v1_grp[g] = ring.tile([P, 4096], BF16, name="v1_grp%d" % g, tag="v1_grp", bufs=2, align_bytes=256)
+                if m % 4 == 0:
+                    v1_grp[u // 4] = ring.tile(
+                        [P, 2048], BF16, name="v1_grp%d" % (u // 4), tag="v1_grp", bufs=2, align_bytes=256
+                    )
+                c = m % 4
                 nc.vector.tensor_tensor(
-                    out=v1_grp[g][:, 512 * m : 512 * m + 512].rearrange("p (q t) -> p q t", t=4),
+                    out=v1_grp[u // 4][:, 512 * c : 512 * c + 512].rearrange("p (q t) -> p q t", t=4),
                     in0=t_bank[u][:].rearrange("p t q -> p q t"),
                     in1=s_neg[:, g, :].unsqueeze(1).to_broadcast([P, P, 4]),
                     op=ALU.mult,
                 )
 
-            def v1_quant(g, c0, n):
-                nc.vector.quantize_mx(
-                    out=v1_codes[g][:, P * c0 : P * (c0 + n)].bitcast(E4M3X4),
-                    scales=v1_sc[g][:, P * c0 : P * (c0 + n)],
-                    in_=v1_grp[g][:, 512 * c0 : 512 * (c0 + n)],
-                )
+            def v1_quant(g, h):
+                quant(v1_codes[g], v1_sc[g], 512 * h, 512, v1_grp[2 * g + h][:])
 
-            h_grp = {}
-
-            def h_new(nm, g):
-                h_grp[(nm, g)] = ring.tile(
-                    [P, 2048], BF16, name="h_grp_%s%d" % (nm, g), tag="h_grp", bufs=6, align_bytes=256
-                )
-
-            def h_mix_gp(nm, raw, g, c0, n):
+            def mix_gpsimd(dst, src):
                 nc.gpsimd.tensor_scalar(
-                    out=h_grp[(nm, g)][:, 4 * c0 : 4 * (c0 + n)].rearrange("p (c t) -> p c t", t=4),
-                    in0=raw[g][:, :, c0 : c0 + n].rearrange("p t c -> p c t"),
+                    out=dst.rearrange("p (c t) -> p c t", t=4),
+                    in0=src.rearrange("p t c -> p c t"),
                     scalar1=1.0,
                     scalar2=0.0,
                     op0=ALU.mult,
                     op1=ALU.add,
                 )
 
-            def mix_views(dst, src):
-                return (
-                    dst.rearrange("p (c i t) -> p c t i", i=4, t=4),
-                    src.rearrange("p t (c i) -> p c t i", i=4),
+            def mix(copy, dst, src):
+                copy(
+                    out=dst.rearrange("p (c i t) -> p c t i", i=4, t=4),
+                    in_=src.rearrange("p t (c i) -> p c t i", i=4),
                 )
 
-            def h_mix_v(nm, raw, g):
-                d, sr = mix_views(h_grp[(nm, g)][:], raw[g][:])
-                nc.vector.tensor_copy(out=d, in_=sr)
-
-            def h_quant(nm, codes, sc, g):
-                nc.vector.quantize_mx(out=codes[g][:].bitcast(E4M3X4), scales=sc[g][:], in_=h_grp[(nm, g)][:])
-
-            v_wide = {}
-            v_grp = {}
-
-            def widen(h, g, t):
-                if t == 0:
-                    v_wide[(h, g)] = r4("v_wide%d_%d" % (h, g))
-                nc.scalar.activation(
-                    v_wide[(h, g)][:, t, :],
-                    v_raw[g][:, t, 512 * h : 512 * h + 512].bitcast(E4M3),
-                    ACT.Copy,
-                    scale=vs[:, g, t : t + 1],
-                )
-
-            def v_mix(mp, g, c):
-                if c == 0:
-                    v_grp[(mp, g)] = ring.tile(
-                        [P, 1024], BF16, name="v_grp%d_%d" % (mp, g), tag="v_grp", bufs=5, align_bytes=256
-                    )
-                c0 = P * (2 * (mp % 2) + c)
-                dst = v_grp[(mp, g)][:, 512 * c : 512 * c + 512]
-                src = v_wide[(mp // 2, g)][:, :, c0 : c0 + P]
-                d, sr = mix_views(dst, src)
-                if c == 1 and (mp, g) in S_SHARE:
-                    nc.scalar.copy(out=d, in_=sr)
-                elif (mp, g) in G_SHARE:
-                    nc.gpsimd.tensor_scalar(
-                        out=dst.rearrange("p (c t) -> p c t", t=4),
-                        in0=src.rearrange("p t c -> p c t"),
-                        scalar1=1.0,
-                        scalar2=0.0,
-                        op0=ALU.mult,
-                        op1=ALU.add,
+            def widen(h, g, t, on_vector):
+                if (h, g) not in v_wide:
+                    v_wide[(h, g)] = rows_tile("v_wide1_%d" % g, g)
+                dst = v_wide[(h, g)][:, t, :]
+                src = v_raw[g][:, t, 512 * h : 512 * h + 512].bitcast(E4M3)
+                if on_vector:
+                    nc.vector.tensor_scalar(
+                        out=dst, in0=src, scalar1=vs[:, g, t : t + 1], scalar2=None, op0=ALU.mult
                     )
                 else:
-                    nc.vector.tensor_copy(out=d, in_=sr)
+                    nc.scalar.activation(dst, src, ACT.Copy, scale=vs[:, g, t : t + 1])
+
+            v_grp = {}
+
+            def v_mix(mp, g, copy=nc.vector.tensor_copy, tag="v_grp"):
+                v_grp[(mp, g)] = ring.tile(
+                    [P, 1024], BF16, name="v_grp%d_%d" % (mp, g), tag=tag, bufs=3, align_bytes=256
+                )
+                c0 = 256 * (mp % 2)
+                mix(copy, v_grp[(mp, g)][:], v_wide[(mp // 2, g)][:, :, c0 : c0 + 256])
 
             def v_quant(mp, g):
-                c0 = 256 * mp
-                nc.vector.quantize_mx(
-                    out=v_codes[g][:, c0 : c0 + 256].bitcast(E4M3X4),
-                    scales=v_sc[g][:, c0 : c0 + 256],
-                    in_=v_grp[(mp, g)][:],
-                )
+                quant(v_codes[g], v_sc[g], 256 * mp, 256, v_grp[(mp, g)][:])
 
-            def h_mix_s(nm, raw, g):
-                h_new(nm, g)
-                d, sr = mix_views(h_grp[(nm, g)][:], raw[g][:])
-                nc.scalar.copy(out=d, in_=sr)
-
-            def quant_hn(g):
-                h_quant("n", hn_codes, hn_sc, g)
-
-            def quant_hp(g):
-                h_quant("p", hp_codes, hp_sc, g)
-
-            def mix_gp(nm, raw, g):
-                h_new(nm, g)
-                for c in range(H // GP_COLS):
-                    h_mix_gp(nm, raw, g, GP_COLS * c, GP_COLS)
-
-            if not V_N0:
-                mix_gp("n", hn_raw, 0)
-            mix_gp("n", hn_raw, 1)
-            mix_gp("n", hn_raw, 2)
-            mix_gp("n", hn_raw, 3)
-
-            widen_list = [(h, g, t) for h in range(2) for g in range(G) for t in range(4)]
-            done = [0]
+            todo = [(0, 0, t) for t in range(4)] + [(1, 0, t) for t in range(HEAD_WIDEN - 4)]
+            todo = todo + [(0, g, t) for g in range(1, G) for t in range(4)]
+            todo = todo + [(1, g, t) for g in range(1, G) for t in range(4)]
 
             def widen_some(n):
-                for k in range(n):
-                    if done[0] < len(widen_list):
-                        widen(*widen_list[done[0]])
-                        done[0] = done[0] + 1
+                for k in range(min(n, len(todo))):
+                    widen(*todo[0], False)
+                    todo.remove(todo[0])
 
             hf_turn(0, 0)
             hf_turn(0, 1)
-            hf_out(0, 0)
-            hf_out(0, 1)
+            hf_out(0, 0, True)
             nc.vector.tensor_copy(out=b_rows32[:], in_=b_rows[:])
-            hf_quant(0, 0)
+            quant(hf_codes[0], hf_sc[0], 0, 256, hf_grp[0][:, 0:1024])
+            hf_out(0, 1, True)
             b_bank = bank("t", [P, P])
             nc.tensor.transpose(b_bank[:], b_rows32[:], ident[:])
             nc.vector.tensor_copy(out=bias[:], in_=b_bank[:, 0:MT])
-            hf_quant(0, 1)
-            nc.vector.tensor_scalar(
-                out=s_neg[:], in0=s_bf[:], scalar1=-1.0, scalar2=None, op0=ALU.mult
-            )
-            widen_some(HEAD_WIDEN[0])
-            for u in range(4):
+            quant(hf_codes[0], hf_sc[0], 256, 256, hf_grp[0][:, 1024:2048])
+            hf_turn(1, 0)
+            hf_out(1, 0, True)
+            widen_some(HEAD_WIDEN)
+            for u in range(3):
                 field(u)
-            widen_some(HEAD_WIDEN[1])
-            if V_N0:
-                h_new("n", 0)
-                h_mix_v("n", hn_raw, 0)
+            hf_turn(1, 1)
             tanh(0)
+            field(3)
             tanh(1)
-            mix_gp("p", hp_raw, 0)
-            mix_gp("p", hp_raw, 1)
+            nc.vector.tensor_scalar(out=s_neg[:], in0=s_bf[:], scalar1=-1.0, scalar2=None, op0=ALU.mult)
+            v_mix(0, 0)
+            v_mix(1, 0)
+            v_quant(0, 0)
+            v_quant(1, 0)
+            hf_out(1, 1, True)
 
-            hq = [(quant_hn, 0), (quant_hn, 1), (quant_hn, 2), (quant_hn, 3), (quant_hp, 0), (quant_hp, 1), (quant_hp, 2), (quant_hp, 3)]
-            nq = 0
-            npairs = G * MT // 2
-            for j in range(npairs):
-                hg = TR_AT.get(j, 0)
-                if hg:
-                    hf_turn(hg, 0)
-                    hf_turn(hg, 1)
-                    hf_out(hg, 0)
-                    hf_out(hg, 1)
-                turn(2 * j)
-                turn(2 * j + 1)
-                if j + 2 < npairs:
-                    field(2 * j + 4)
-                    field(2 * j + 5)
-                if j + 1 < npairs:
-                    tanh(2 * j + 2)
-                    tanh(2 * j + 3)
-                weight(2 * j)
-                if hg:
-                    nc.vector.quantize_mx(
-                        out=hf_codes[hg][:].bitcast(E4M3X4), scales=hf_sc[hg][:], in_=hf_grp[hg][:]
-                    )
-                if V1Q == 8 and j % 4 == 0 and j > 0:
-                    v1_quant(j // 4 - 1, 0, 8)
-                if V1Q == 4 and j % 2 == 0 and j > 0:
-                    v1_quant((j - 2) // 4, 4 * ((j - 2) // 2 % 2), 4)
-                weight(2 * j + 1)
-                if j in HQ_AT:
-                    hq[nq][0](hq[nq][1])
-                    nq = nq + 1
-                widen_some(WIDEN_AT.get(j, 1))
-            for g in GP_LATE:
-                mix_gp("p", hp_raw, g)
-            v1_quant(G - 1, 8 - V1Q, V1Q)
-
-            acc = [bank("f", [P, H]) for m in range(HALF)] + [bank("t", [P, H]) for m in range(HALF)]
+            acc = {}
 
             def one_pass(m, codes, sc, rc, rs, g, first, last):
                 c0 = P * m
@@ -381,9 +285,69 @@ def tile_persistentmeanfieldisingrbmgradient_w4_kernel(
                     stop=last,
                 )
 
-            def store(m):
-                res = ring.tile([P, H], F32, name="res%d" % m, tag="th", bufs=8)
-                if m in V_OUT:
+            passes = {}
+
+            def open_acc(kind):
+                m = len(acc)
+                acc[m] = bank(kind, [P, H], True)
+                passes[m] = 0
+
+            def neg_upto(n):
+                for m in acc:
+                    for g in range(passes[m], n):
+                        one_pass(m, v1_codes, v1_sc, hn_codes, hn_sc, g, g == 0, False)
+                    passes[m] = max(passes[m], n)
+
+            rest = 2 * H - GP_COLS
+            for j in range(PAIRS):
+                g = j // 4
+                turn(2 * j)
+                turn(2 * j + 1)
+                if j + 1 < PAIRS:
+                    tanh(2 * j + 2)
+                turns_hf = j % 4 in (1, 2) and g + 2 < G
+                if turns_hf:
+                    hf_turn(g + 2, j % 4 - 1)
+                if j + 1 < PAIRS:
+                    tanh(2 * j + 3)
+                if turns_hf:
+                    hf_out(g + 2, j % 4 - 1, False)
+                if j + 2 < PAIRS:
+                    field(2 * j + 4)
+                    field(2 * j + 5)
+                if j == EARLY:
+                    open_acc("t")
+                if j + 2 == PAIRS:
+                    open_acc("f")
+                if j + 1 == PAIRS:
+                    open_acc("f")
+                    open_acc("f")
+                if j % 4 == 1 or j + 2 >= PAIRS:
+                    neg_upto(g)
+                if not turns_hf and j > 0:
+                    widen_some(1)
+                if j % 4 == 0 and j:
+                    h_grp = gate("h_grp%d" % g)
+                    mix_gpsimd(h_grp[:], h_raw[g][:, :, 0:GP_COLS])
+                weight(2 * j)
+                weight(2 * j + 1)
+                if j == 0:
+                    for t in range(HEAD_WIDEN - 4, 4):
+                        widen(1, 0, t, True)
+                    quant(hf_codes[1], hf_sc[1], 0, 512, hf_grp[1][:, 0:2048])
+                    h_grp = gate("h_grp%d" % g)
+                    mix_gpsimd(h_grp[:], h_raw[g][:, :, 0:GP_COLS])
+                if j % 4 == 3:
+                    v1_quant(g, 0)
+                    quant(hp_codes[g], hp_sc[g], 0, GP_COLS - H, h_grp[:, 4 * H : 4 * GP_COLS])
+                    if g + 2 < G:
+                        quant(hf_codes[g + 2], hf_sc[g + 2], 0, 512, hf_grp[g + 2][:])
+                    v1_quant(g, 1)
+                    quant(hn_codes[g], hn_sc[g], 0, 512, h_grp[:, 0 : 4 * H])
+
+            def store(m, on_vector):
+                res = ring.tile([P, H], F32, name="res%d" % m, tag="th", bufs=8, align_bytes=256)
+                if on_vector:
                     nc.vector.tensor_scalar(
                         out=res[:], in0=acc[m][:], scalar1=float(B) ** -0.5, scalar2=None, op0=ALU.mult
                     )
@@ -391,36 +355,29 @@ def tile_persistentmeanfieldisingrbmgradient_w4_kernel(
                     nc.scalar.activation(res[:], acc[m][:], ACT.Copy, scale=float(B) ** -0.5)
                 nc.sync.dma_start(out=out[P * m : P * m + P, :], in_=res[:])
 
-            while nq < 4:
-                hq[nq][0](hq[nq][1])
-                nq = nq + 1
-            for g in range(G):
-                for h in range(2):
-                    for mm in range(HALF):
-                        one_pass(HALF * h + mm, v1_codes, v1_sc, hn_codes, hn_sc, g, g == 0, False)
-            for g in S_HP:
-                h_mix_s("p", hp_raw, g)
+            while len(acc) < MT:
+                open_acc("t")
+                neg_upto(G - 1)
+            neg_upto(G)
+
             jobs = [(mp, g) for mp in range(4) for g in range(G)]
-
-            def mix_job(i):
-                for c in range(2):
-                    v_mix(jobs[i][0], jobs[i][1], c)
-
-            for g in V_HP:
-                h_new("p", g)
-                h_mix_v("p", hp_raw, g)
-            mix_job(0)
-            for i in range(len(jobs)):
-                widen_some(WIDEN_PER_JOB)
-                if i + 1 < len(jobs):
-                    mix_job(i + 1)
-                v_quant(*jobs[i])
-                if nq < len(hq):
-                    hq[nq][0](hq[nq][1])
-                    nq = nq + 1
-                mp, g = jobs[i]
+            widen_some(len(todo) - 12)
+            for g in range(G):
+                mix(nc.scalar.copy, hp_rest[g][:], h_raw[g][:, :, GP_COLS : 2 * H])
+            widen_some(12)
+            todo_v = [job for job in jobs if job not in v_grp]
+            for job in todo_v[len(todo_v) - S_MIX :]:
+                v_mix(*job, nc.scalar.copy, "v_late")
+            v_mix(*todo_v[0])
+            for i in range(len(todo_v)):
+                if i + 1 < len(todo_v) - S_MIX:
+                    v_mix(*todo_v[i + 1])
+                v_quant(*todo_v[i])
+                if i < G:
+                    quant(hp_codes[i], hp_sc[i], H - rest, rest, hp_rest[i][:])
+            for mp, g in jobs:
                 for c in range(2):
                     one_pass(2 * mp + c, v_codes, v_sc, hp_codes, hp_sc, g, False, g == G - 1)
-                for (m, at) in STORE_AT:
-                    if at == i:
-                        store(m)
+                if g == G - 1:
+                    store(2 * mp, False)
+                    store(2 * mp + 1, mp == 3)

@@ -21,11 +21,17 @@ P = 128
 G = 4
 MT = V // P
 PAIRS = G * MT // 2
-HEAD_WIDEN = 6
 S_MIX = 2
+V_OUT = (5, 7)
+WARM = (4, 1, 1, 1)
+V1_TAG = (1, 3, 1, 4, 1, 5, 2, 0)
 T_BANKS = 5
-EARLY = 99
-GP_COLS = 768
+GP_COLS = (768, 896, 768, 768)
+V_HF = (2,)
+WIDEN_AT = (1, 2, 3)
+S_HEAD = 2
+HEAD_JOB = 1
+RES_EARLY = 2
 
 
 def tile_persistentmeanfieldisingrbmgradient_w4_kernel(
@@ -38,7 +44,7 @@ def tile_persistentmeanfieldisingrbmgradient_w4_kernel(
         psum = ctx.enter_context(tc.psum_pool(name="psum", bufs=1))
 
         def kt(name, shape, dtype):
-            return keep.tile(shape, dtype, name=name, align_bytes=256)
+            return keep.tile(shape, dtype, name=name, align_bytes=64)
 
         rings = {"t": ["bank%d" % i for i in range(T_BANKS)], "f": ["bank%d" % i for i in range(T_BANKS, 8)]}
 
@@ -54,8 +60,9 @@ def tile_persistentmeanfieldisingrbmgradient_w4_kernel(
 
         hf_raw = [rows_tile("hf_raw%d" % g, g) for g in range(G)]
         h_raw = [kt("h_raw%d" % g, [P, 4, 2 * H], BF16) for g in range(G)]
-        hp_rest = [kt("hp_rest%d" % g, [P, 4 * (2 * H - GP_COLS)], BF16) for g in range(G)]
-        v_raw = [kt("v_raw%d" % g, [P, 4, V], U8) for g in range(G)]
+        hp_rest = {g: kt("hp_rest%d" % g, [P, 4 * (2 * H - GP_COLS[g])], BF16) for g in range(G) if GP_COLS[g] < 2 * H}
+        v_raw = {g: kt("v_raw%d" % g, [P, 4, V], U8) for g in range(1, G)}
+        v_first = [kt("v_first%d" % h, [P, 4, 512], U8) for h in range(2)]
         v_wide = {(0, g): kt("v_wide0_%d" % g, [P, 4, 512], BF16) for g in range(G)}
         hf_codes = [kt("hf_codes%d" % g, [P, 512], U32) for g in range(G)]
         hf_sc = [kt("hf_sc%d" % g, [P, 512], U8) for g in range(G)]
@@ -76,12 +83,14 @@ def tile_persistentmeanfieldisingrbmgradient_w4_kernel(
         s_bf = kt("s_bf", [P, G, 4], BF16)
         s_neg = kt("s_neg", [P, G, 4], F32)
         vs = kt("vs", [P, G, 4], F32)
+        zeros = kt("zeros", [P, 512], BF16)
         warm = kt("warm", [P, 1], F32)
 
         with tc.manual_schedule():
-            nc.vector.memset(b_rows[:], 0.0)
-            nc.vector.memset(w_sc[:].bitcast(I32), 0)
             nc.vector.memset(warm[:], 0.0)
+            nc.vector.memset(b_rows[:], 0.0)
+            nc.vector.memset(zeros[:], 0.0)
+            nc.vector.memset(w_sc[:].bitcast(I32), 0)
             make_identity(nc, ident[:])
             nc.scalar.dma_start(out=vs[:], in_=v_scale.rearrange("(g p t) o -> p g (t o)", p=P, t=4))
             nc.scalar.dma_start(out=b_rows[0:MT, :], in_=b.rearrange("(m c) -> m c", c=P))
@@ -96,9 +105,13 @@ def tile_persistentmeanfieldisingrbmgradient_w4_kernel(
             def load_half(g, h):
                 nc.sync.dma_start(out=hf_raw[g][:, 2 * h : 2 * h + 2, :], in_=rows(hf, g)[:, 2 * h : 2 * h + 2, :])
 
+            def load_v0(h):
+                nc.sync.dma_start(out=v_first[h][:], in_=rows(v_bytes, 0)[:, :, 512 * h : 512 * h + 512])
+
+            load_v0(0)
             load_half(0, 0)
             load_half(0, 1)
-            load(v_raw, v_bytes, 0)
+            load_v0(1)
             load_half(1, 0)
             nc.sync.dma_start(out=w_codes[:], in_=w_words[0])
             for q in range(4):
@@ -119,16 +132,16 @@ def tile_persistentmeanfieldisingrbmgradient_w4_kernel(
             hf_grp = {}
             tr_bank = {}
 
-            def grp(nm):
-                return ring.tile([P, 2048], BF16, name=nm, tag="grp", bufs=2, align_bytes=256)
+            def grp(nm, tag):
+                return ring.tile([P, 2048], BF16, name=nm, tag="grp%d" % tag, bufs=1, align_bytes=256)
 
             def gate(nm):
-                return ring.tile([P, 4 * GP_COLS], BF16, name=nm, tag="gate", bufs=1, align_bytes=256)
+                return ring.tile([P, 4 * max(GP_COLS)], BF16, name=nm, tag="gate", bufs=1, align_bytes=256)
 
             def hf_turn(g, h):
                 if h == 0:
-                    hf_grp[g] = gate("hf_grp1") if g == 1 else grp("hf_grp%d" % g)
-                bk = bank("f" if g > 1 else "t", [P, 2, 2, P])
+                    hf_grp[g] = gate("hf_grp1") if g == 1 else grp("hf_grp%d" % g, g % 3)
+                bk = bank("f" if g > 1 and g not in V_HF else "t", [P, 2, 2, P])
                 tr_bank[(g, h)] = bk
                 words = hf_raw[g][:].rearrange("p t k -> p (t k)").bitcast(F32)
                 for i in range(2):
@@ -147,7 +160,16 @@ def tile_persistentmeanfieldisingrbmgradient_w4_kernel(
                     nc.scalar.copy(out=dst, in_=src)
 
             def quant(codes, sc, c0, n, src):
-                nc.vector.quantize_mx(out=codes[:, c0 : c0 + n].bitcast(E4M3X4), scales=sc[:, c0 : c0 + n], in_=src)
+                done = 0
+                for w in (512, 256, 128):
+                    if n - done >= w:
+                        a = c0 + done
+                        nc.vector.quantize_mx(
+                            out=codes[:, a : a + w].bitcast(E4M3X4),
+                            scales=sc[:, a : a + w],
+                            in_=src[:, 4 * done : 4 * (done + w)],
+                        )
+                        done = done + w
 
             f_bank = {}
             th = {}
@@ -182,9 +204,7 @@ def tile_persistentmeanfieldisingrbmgradient_w4_kernel(
             def weight(u):
                 g, m = u // MT, u % MT
                 if m % 4 == 0:
-                    v1_grp[u // 4] = ring.tile(
-                        [P, 2048], BF16, name="v1_grp%d" % (u // 4), tag="v1_grp", bufs=2, align_bytes=256
-                    )
+                    v1_grp[u // 4] = grp("v1_grp%d" % (u // 4), V1_TAG[u // 4])
                 c = m % 4
                 nc.vector.tensor_tensor(
                     out=v1_grp[u // 4][:, 512 * c : 512 * c + 512].rearrange("p (q t) -> p q t", t=4),
@@ -216,7 +236,10 @@ def tile_persistentmeanfieldisingrbmgradient_w4_kernel(
                 if (h, g) not in v_wide:
                     v_wide[(h, g)] = rows_tile("v_wide1_%d" % g, g)
                 dst = v_wide[(h, g)][:, t, :]
-                src = v_raw[g][:, t, 512 * h : 512 * h + 512].bitcast(E4M3)
+                if g:
+                    src = v_raw[g][:, t, 512 * h : 512 * h + 512].bitcast(E4M3)
+                else:
+                    src = v_first[h][:, t, :].bitcast(E4M3)
                 if on_vector:
                     nc.vector.tensor_scalar(
                         out=dst, in0=src, scalar1=vs[:, g, t : t + 1], scalar2=None, op0=ALU.mult
@@ -228,7 +251,7 @@ def tile_persistentmeanfieldisingrbmgradient_w4_kernel(
 
             def v_mix(mp, g, copy=nc.vector.tensor_copy, tag="v_grp"):
                 v_grp[(mp, g)] = ring.tile(
-                    [P, 1024], BF16, name="v_grp%d_%d" % (mp, g), tag=tag, bufs=3, align_bytes=256
+                    [P, 1024], BF16, name="v_grp%d_%d" % (mp, g), tag=tag, bufs=4, align_bytes=256
                 )
                 c0 = 256 * (mp % 2)
                 mix(copy, v_grp[(mp, g)][:], v_wide[(mp // 2, g)][:, :, c0 : c0 + 256])
@@ -236,7 +259,7 @@ def tile_persistentmeanfieldisingrbmgradient_w4_kernel(
             def v_quant(mp, g):
                 quant(v_codes[g], v_sc[g], 256 * mp, 256, v_grp[(mp, g)][:])
 
-            todo = [(0, 0, t) for t in range(4)] + [(1, 0, t) for t in range(HEAD_WIDEN - 4)]
+            todo = [(0, 0, 0)] + [(1, 0, t) for t in range(S_HEAD)]
             todo = todo + [(0, g, t) for g in range(1, G) for t in range(4)]
             todo = todo + [(1, g, t) for g in range(1, G) for t in range(4)]
 
@@ -245,19 +268,35 @@ def tile_persistentmeanfieldisingrbmgradient_w4_kernel(
                     widen(*todo[0], False)
                     todo.remove(todo[0])
 
+            def warm_up(n):
+                for i in range(n):
+                    nc.tensor.matmul(warm_bank[:], lhsT=zeros[:, 0:P], rhs=zeros[:], start=True, stop=True)
+
+            warm_bank = psum.tile([P, 512], F32, name="warm_bank", tag="bank7")
+            warm_up(WARM[0])
+            widen_some(1)
+            for t in range(1, 4):
+                widen(0, 0, t, True)
             hf_turn(0, 0)
+            warm_up(WARM[1])
             hf_turn(0, 1)
-            hf_out(0, 0, True)
+            warm_up(WARM[2])
+            v_mix(0, 0)
+            v_mix(1, 0)
+            hf_out(0, 0, False)
             nc.vector.tensor_copy(out=b_rows32[:], in_=b_rows[:])
             quant(hf_codes[0], hf_sc[0], 0, 256, hf_grp[0][:, 0:1024])
-            hf_out(0, 1, True)
+            hf_out(0, 1, False)
             b_bank = bank("t", [P, P])
             nc.tensor.transpose(b_bank[:], b_rows32[:], ident[:])
-            nc.vector.tensor_copy(out=bias[:], in_=b_bank[:, 0:MT])
+            v_quant(0, 0)
             quant(hf_codes[0], hf_sc[0], 256, 256, hf_grp[0][:, 1024:2048])
+            nc.vector.tensor_copy(out=bias[:], in_=b_bank[:, 0:MT])
+            v_quant(1, 0)
             hf_turn(1, 0)
+            warm_up(WARM[3])
+            widen_some(S_HEAD)
             hf_out(1, 0, True)
-            widen_some(HEAD_WIDEN)
             for u in range(3):
                 field(u)
             hf_turn(1, 1)
@@ -265,11 +304,13 @@ def tile_persistentmeanfieldisingrbmgradient_w4_kernel(
             field(3)
             tanh(1)
             nc.vector.tensor_scalar(out=s_neg[:], in0=s_bf[:], scalar1=-1.0, scalar2=None, op0=ALU.mult)
-            v_mix(0, 0)
-            v_mix(1, 0)
-            v_quant(0, 0)
-            v_quant(1, 0)
+            for t in range(S_HEAD, 4):
+                widen(1, 0, t, True)
+            if HEAD_JOB:
+                v_mix(2, 0)
             hf_out(1, 1, True)
+            if HEAD_JOB:
+                v_quant(2, 0)
 
             acc = {}
 
@@ -298,7 +339,6 @@ def tile_persistentmeanfieldisingrbmgradient_w4_kernel(
                         one_pass(m, v1_codes, v1_sc, hn_codes, hn_sc, g, g == 0, False)
                     passes[m] = max(passes[m], n)
 
-            rest = 2 * H - GP_COLS
             for j in range(PAIRS):
                 g = j // 4
                 turn(2 * j)
@@ -310,39 +350,38 @@ def tile_persistentmeanfieldisingrbmgradient_w4_kernel(
                     hf_turn(g + 2, j % 4 - 1)
                 if j + 1 < PAIRS:
                     tanh(2 * j + 3)
-                if turns_hf:
+                if turns_hf and g + 2 not in V_HF:
                     hf_out(g + 2, j % 4 - 1, False)
                 if j + 2 < PAIRS:
                     field(2 * j + 4)
                     field(2 * j + 5)
-                if j == EARLY:
-                    open_acc("t")
                 if j + 2 == PAIRS:
                     open_acc("f")
                 if j + 1 == PAIRS:
                     open_acc("f")
                     open_acc("f")
-                if j % 4 == 1 or j + 2 >= PAIRS:
-                    neg_upto(g)
-                if not turns_hf and j > 0:
+                if j + 2 >= PAIRS:
+                    neg_upto(G - 1)
+                if (turns_hf and g + 2 in V_HF) or (not turns_hf and j % 4 in WIDEN_AT):
                     widen_some(1)
                 if j % 4 == 0 and j:
                     h_grp = gate("h_grp%d" % g)
-                    mix_gpsimd(h_grp[:], h_raw[g][:, :, 0:GP_COLS])
+                    mix_gpsimd(h_grp[:, 0 : 4 * GP_COLS[g]], h_raw[g][:, :, 0 : GP_COLS[g]])
                 weight(2 * j)
                 weight(2 * j + 1)
+                if turns_hf and g + 2 in V_HF:
+                    hf_out(g + 2, j % 4 - 1, True)
                 if j == 0:
-                    for t in range(HEAD_WIDEN - 4, 4):
-                        widen(1, 0, t, True)
                     quant(hf_codes[1], hf_sc[1], 0, 512, hf_grp[1][:, 0:2048])
                     h_grp = gate("h_grp%d" % g)
-                    mix_gpsimd(h_grp[:], h_raw[g][:, :, 0:GP_COLS])
+                    mix_gpsimd(h_grp[:, 0 : 4 * GP_COLS[g]], h_raw[g][:, :, 0 : GP_COLS[g]])
                 if j % 4 == 3:
-                    v1_quant(g, 0)
-                    quant(hp_codes[g], hp_sc[g], 0, GP_COLS - H, h_grp[:, 4 * H : 4 * GP_COLS])
                     if g + 2 < G:
                         quant(hf_codes[g + 2], hf_sc[g + 2], 0, 512, hf_grp[g + 2][:])
-                    v1_quant(g, 1)
+                    if g == G - 1:
+                        v1_quant(0, 1)
+                    v1_quant(g, 0)
+                    quant(hp_codes[g], hp_sc[g], 0, GP_COLS[g] - H, h_grp[:, 4 * H : 4 * GP_COLS[g]])
                     quant(hn_codes[g], hn_sc[g], 0, 512, h_grp[:, 0 : 4 * H])
 
             def store(m, on_vector):
@@ -355,29 +394,51 @@ def tile_persistentmeanfieldisingrbmgradient_w4_kernel(
                     nc.scalar.activation(res[:], acc[m][:], ACT.Copy, scale=float(B) ** -0.5)
                 nc.sync.dma_start(out=out[P * m : P * m + P, :], in_=res[:])
 
+            for g in range(1, G):
+                v1_quant(g, 1)
+            open_acc("t")
+            neg_upto(G - 1)
             while len(acc) < MT:
                 open_acc("t")
-                neg_upto(G - 1)
-            neg_upto(G)
+                passes[len(acc) - 1] = 1
+                one_pass(len(acc) - 1, v1_codes, v1_sc, hn_codes, hn_sc, 0, True, False)
+            for m in range(4):
+                one_pass(m, v1_codes, v1_sc, hn_codes, hn_sc, G - 1, False, False)
+            for g in range(1, G):
+                for m in range(4, MT):
+                    one_pass(m, v1_codes, v1_sc, hn_codes, hn_sc, g, False, False)
 
             jobs = [(mp, g) for mp in range(4) for g in range(G)]
-            widen_some(len(todo) - 12)
-            for g in range(G):
-                mix(nc.scalar.copy, hp_rest[g][:], h_raw[g][:, :, GP_COLS : 2 * H])
-            widen_some(12)
             todo_v = [job for job in jobs if job not in v_grp]
-            for job in todo_v[len(todo_v) - S_MIX :]:
-                v_mix(*job, nc.scalar.copy, "v_late")
+            by_scalar = todo_v[len(todo_v) - S_MIX :]
+
+            def job_passes(mp, g):
+                for m in (2 * mp, 2 * mp + 1):
+                    one_pass(m, v_codes, v_sc, hp_codes, hp_sc, g, False, g == G - 1)
+
+            widen_some(len(todo) - 12)
+            for g in hp_rest:
+                mix(nc.scalar.copy, hp_rest[g][:], h_raw[g][:, :, GP_COLS[g] : 2 * H])
+            widen_some(12)
             v_mix(*todo_v[0])
-            for i in range(len(todo_v)):
-                if i + 1 < len(todo_v) - S_MIX:
-                    v_mix(*todo_v[i + 1])
-                v_quant(*todo_v[i])
-                if i < G:
-                    quant(hp_codes[i], hp_sc[i], H - rest, rest, hp_rest[i][:])
             for mp, g in jobs:
-                for c in range(2):
-                    one_pass(2 * mp + c, v_codes, v_sc, hp_codes, hp_sc, g, False, g == G - 1)
-                if g == G - 1:
-                    store(2 * mp, False)
-                    store(2 * mp + 1, mp == 3)
+                if (mp, g) == (1, 0):
+                    for m in range(RES_EARLY):
+                        store(m, False)
+                    for job in by_scalar:
+                        v_mix(*job, nc.scalar.copy, "v_late")
+                    for m in range(RES_EARLY, 2):
+                        store(m, False)
+                if (mp, g) in todo_v:
+                    i = todo_v.index((mp, g))
+                    if i + 1 < len(todo_v) - S_MIX:
+                        v_mix(*todo_v[i + 1])
+                    v_quant(mp, g)
+                if mp == 0 and g in hp_rest:
+                    quant(hp_codes[g], hp_sc[g], GP_COLS[g] - H, 2 * H - GP_COLS[g], hp_rest[g][:])
+                job_passes(mp, g)
+                if (mp, g) == (1, G - 1):
+                    store(2, False)
+                    store(3, False)
+            for m in range(4, MT):
+                store(m, m in V_OUT)

@@ -25,13 +25,18 @@ S_MIX = 2
 V_OUT = (5, 7)
 WARM = (4, 1, 1, 1)
 V1_TAG = (1, 3, 1, 4, 1, 5, 2, 0)
+TAIL_PARTS = 1
+V0_FIRST = False
+S_FIRST = 1
+HF1A_V = True
+HF_FIRST = 1
+SPLIT_F = 0
 T_BANKS = 5
 GP_COLS = (768, 896, 768, 768)
 V_HF = (2,)
 WIDEN_AT = (1, 2, 3)
-S_HEAD = 2
+S_HEAD = 3
 HEAD_JOB = 1
-RES_EARLY = 2
 
 
 def tile_persistentmeanfieldisingrbmgradient_w4_kernel(
@@ -59,7 +64,8 @@ def tile_persistentmeanfieldisingrbmgradient_w4_kernel(
             return ring.tile([P, 4, H], BF16, name=name, tag="rows%d" % g, bufs=1, align_bytes=256)
 
         hf_raw = [rows_tile("hf_raw%d" % g, g) for g in range(G)]
-        h_raw = [kt("h_raw%d" % g, [P, 4, 2 * H], BF16) for g in range(G)]
+        hn_raw = [kt("hn_raw%d" % g, [P, 4, H], BF16) for g in range(G)]
+        hp_raw = [kt("hp_raw%d" % g, [P, 4, H], BF16) for g in range(G)]
         hp_rest = {g: kt("hp_rest%d" % g, [P, 4 * (2 * H - GP_COLS[g])], BF16) for g in range(G) if GP_COLS[g] < 2 * H}
         v_raw = {g: kt("v_raw%d" % g, [P, 4, V], U8) for g in range(1, G)}
         v_first = [kt("v_first%d" % h, [P, 4, 512], U8) for h in range(2)]
@@ -109,9 +115,12 @@ def tile_persistentmeanfieldisingrbmgradient_w4_kernel(
                 nc.sync.dma_start(out=v_first[h][:], in_=rows(v_bytes, 0)[:, :, 512 * h : 512 * h + 512])
 
             load_v0(0)
+            if V0_FIRST:
+                load_v0(1)
             load_half(0, 0)
             load_half(0, 1)
-            load_v0(1)
+            if not V0_FIRST:
+                load_v0(1)
             load_half(1, 0)
             nc.sync.dma_start(out=w_codes[:], in_=w_words[0])
             for q in range(4):
@@ -122,9 +131,11 @@ def tile_persistentmeanfieldisingrbmgradient_w4_kernel(
             load_half(1, 1)
             nc.sync.dma_start(out=s_bf[:], in_=s.rearrange("(g p t) -> p g t", p=P, t=4))
             for g in range(G):
-                nc.sync.dma_start(out=h_raw[g][:, :, 0:H], in_=rows(hn, g))
-                nc.sync.dma_start(out=h_raw[g][:, :, H : 2 * H], in_=rows(hp, g))
-                if g + 2 < G:
+                load(hn_raw, hn, g)
+                if g + 2 < G and HF_FIRST:
+                    load(hf_raw, hf, g + 2)
+                load(hp_raw, hp, g)
+                if g + 2 < G and not HF_FIRST:
                     load(hf_raw, hf, g + 2)
                 if g + 1 < G:
                     load(v_raw, v_bytes, g + 1)
@@ -161,7 +172,7 @@ def tile_persistentmeanfieldisingrbmgradient_w4_kernel(
 
             def quant(codes, sc, c0, n, src):
                 done = 0
-                for w in (512, 256, 128):
+                for w in (512, 256, 128, 64):
                     if n - done >= w:
                         a = c0 + done
                         nc.vector.quantize_mx(
@@ -249,17 +260,19 @@ def tile_persistentmeanfieldisingrbmgradient_w4_kernel(
 
             v_grp = {}
 
-            def v_mix(mp, g, copy=nc.vector.tensor_copy, tag="v_grp"):
-                v_grp[(mp, g)] = ring.tile(
-                    [P, 1024], BF16, name="v_grp%d_%d" % (mp, g), tag=tag, bufs=4, align_bytes=256
+            def v_mix(job, copy=nc.vector.tensor_copy, tag="v_grp"):
+                m0, n, g = job
+                v_grp[job] = ring.tile(
+                    [P, 512 * n], BF16, name="v_grp%d_%d" % (m0, g), tag=tag, bufs=4, align_bytes=256
                 )
-                c0 = 256 * (mp % 2)
-                mix(copy, v_grp[(mp, g)][:], v_wide[(mp // 2, g)][:, :, c0 : c0 + 256])
+                c0 = P * (m0 % 4)
+                mix(copy, v_grp[job][:], v_wide[(m0 // 4, g)][:, :, c0 : c0 + P * n])
 
-            def v_quant(mp, g):
-                quant(v_codes[g], v_sc[g], 256 * mp, 256, v_grp[(mp, g)][:])
+            def v_quant(job):
+                m0, n, g = job
+                quant(v_codes[g], v_sc[g], P * m0, P * n, v_grp[job][:])
 
-            todo = [(0, 0, 0)] + [(1, 0, t) for t in range(S_HEAD)]
+            todo = ([] if V0_FIRST else [(0, 0, 0)]) + [(1, 0, t) for t in range(S_HEAD)]
             todo = todo + [(0, g, t) for g in range(1, G) for t in range(4)]
             todo = todo + [(1, g, t) for g in range(1, G) for t in range(4)]
 
@@ -274,29 +287,29 @@ def tile_persistentmeanfieldisingrbmgradient_w4_kernel(
 
             warm_bank = psum.tile([P, 512], F32, name="warm_bank", tag="bank7")
             warm_up(WARM[0])
-            widen_some(1)
-            for t in range(1, 4):
+            widen_some(S_FIRST)
+            for t in range(0 if V0_FIRST else 1, 4):
                 widen(0, 0, t, True)
             hf_turn(0, 0)
             warm_up(WARM[1])
             hf_turn(0, 1)
             warm_up(WARM[2])
-            v_mix(0, 0)
-            v_mix(1, 0)
+            v_mix((0, 2, 0))
+            v_mix((2, 2, 0))
             hf_out(0, 0, False)
             nc.vector.tensor_copy(out=b_rows32[:], in_=b_rows[:])
             quant(hf_codes[0], hf_sc[0], 0, 256, hf_grp[0][:, 0:1024])
             hf_out(0, 1, False)
             b_bank = bank("t", [P, P])
             nc.tensor.transpose(b_bank[:], b_rows32[:], ident[:])
-            v_quant(0, 0)
+            v_quant((0, 2, 0))
             quant(hf_codes[0], hf_sc[0], 256, 256, hf_grp[0][:, 1024:2048])
             nc.vector.tensor_copy(out=bias[:], in_=b_bank[:, 0:MT])
-            v_quant(1, 0)
+            v_quant((2, 2, 0))
             hf_turn(1, 0)
             warm_up(WARM[3])
-            widen_some(S_HEAD)
-            hf_out(1, 0, True)
+            widen_some(S_HEAD - (S_FIRST if V0_FIRST else 0))
+            hf_out(1, 0, HF1A_V)
             for u in range(3):
                 field(u)
             hf_turn(1, 1)
@@ -306,11 +319,11 @@ def tile_persistentmeanfieldisingrbmgradient_w4_kernel(
             nc.vector.tensor_scalar(out=s_neg[:], in0=s_bf[:], scalar1=-1.0, scalar2=None, op0=ALU.mult)
             for t in range(S_HEAD, 4):
                 widen(1, 0, t, True)
-            if HEAD_JOB:
-                v_mix(2, 0)
+            for i in range(HEAD_JOB):
+                v_mix((4 + 2 * i, 2, 0))
             hf_out(1, 1, True)
-            if HEAD_JOB:
-                v_quant(2, 0)
+            for i in range(HEAD_JOB):
+                v_quant((4 + 2 * i, 2, 0))
 
             acc = {}
 
@@ -346,6 +359,9 @@ def tile_persistentmeanfieldisingrbmgradient_w4_kernel(
                 if j + 1 < PAIRS:
                     tanh(2 * j + 2)
                 turns_hf = j % 4 in (1, 2) and g + 2 < G
+                early_field = SPLIT_F and turns_hf and g + 2 in V_HF
+                if early_field:
+                    field(2 * j + 4)
                 if turns_hf:
                     hf_turn(g + 2, j % 4 - 1)
                 if j + 1 < PAIRS:
@@ -353,7 +369,8 @@ def tile_persistentmeanfieldisingrbmgradient_w4_kernel(
                 if turns_hf and g + 2 not in V_HF:
                     hf_out(g + 2, j % 4 - 1, False)
                 if j + 2 < PAIRS:
-                    field(2 * j + 4)
+                    if not early_field:
+                        field(2 * j + 4)
                     field(2 * j + 5)
                 if j + 2 == PAIRS:
                     open_acc("f")
@@ -366,7 +383,8 @@ def tile_persistentmeanfieldisingrbmgradient_w4_kernel(
                     widen_some(1)
                 if j % 4 == 0 and j:
                     h_grp = gate("h_grp%d" % g)
-                    mix_gpsimd(h_grp[:, 0 : 4 * GP_COLS[g]], h_raw[g][:, :, 0 : GP_COLS[g]])
+                    mix_gpsimd(h_grp[:, 0 : 4 * H], hn_raw[g][:])
+                    mix_gpsimd(h_grp[:, 4 * H : 4 * GP_COLS[g]], hp_raw[g][:, :, 0 : GP_COLS[g] - H])
                 weight(2 * j)
                 weight(2 * j + 1)
                 if turns_hf and g + 2 in V_HF:
@@ -374,7 +392,8 @@ def tile_persistentmeanfieldisingrbmgradient_w4_kernel(
                 if j == 0:
                     quant(hf_codes[1], hf_sc[1], 0, 512, hf_grp[1][:, 0:2048])
                     h_grp = gate("h_grp%d" % g)
-                    mix_gpsimd(h_grp[:, 0 : 4 * GP_COLS[g]], h_raw[g][:, :, 0 : GP_COLS[g]])
+                    mix_gpsimd(h_grp[:, 0 : 4 * H], hn_raw[g][:])
+                    mix_gpsimd(h_grp[:, 4 * H : 4 * GP_COLS[g]], hp_raw[g][:, :, 0 : GP_COLS[g] - H])
                 if j % 4 == 3:
                     if g + 2 < G:
                         quant(hf_codes[g + 2], hf_sc[g + 2], 0, 512, hf_grp[g + 2][:])
@@ -384,15 +403,17 @@ def tile_persistentmeanfieldisingrbmgradient_w4_kernel(
                     quant(hp_codes[g], hp_sc[g], 0, GP_COLS[g] - H, h_grp[:, 4 * H : 4 * GP_COLS[g]])
                     quant(hn_codes[g], hn_sc[g], 0, 512, h_grp[:, 0 : 4 * H])
 
-            def store(m, on_vector):
+            def store(m, on_vector, parts=1):
                 res = ring.tile([P, H], F32, name="res%d" % m, tag="th", bufs=8, align_bytes=256)
-                if on_vector:
-                    nc.vector.tensor_scalar(
-                        out=res[:], in0=acc[m][:], scalar1=float(B) ** -0.5, scalar2=None, op0=ALU.mult
-                    )
-                else:
-                    nc.scalar.activation(res[:], acc[m][:], ACT.Copy, scale=float(B) ** -0.5)
-                nc.sync.dma_start(out=out[P * m : P * m + P, :], in_=res[:])
+                for i in range(parts):
+                    cols = slice(H // parts * i, H // parts * (i + 1))
+                    if on_vector:
+                        nc.vector.tensor_scalar(
+                            out=res[:, cols], in0=acc[m][:, cols], scalar1=float(B) ** -0.5, scalar2=None, op0=ALU.mult
+                        )
+                    else:
+                        nc.scalar.activation(res[:, cols], acc[m][:, cols], ACT.Copy, scale=float(B) ** -0.5)
+                    nc.sync.dma_start(out=out[P * m : P * m + P, cols], in_=res[:, cols])
 
             for g in range(1, G):
                 v1_quant(g, 1)
@@ -408,37 +429,36 @@ def tile_persistentmeanfieldisingrbmgradient_w4_kernel(
                 for m in range(4, MT):
                     one_pass(m, v1_codes, v1_sc, hn_codes, hn_sc, g, False, False)
 
-            jobs = [(mp, g) for mp in range(4) for g in range(G)]
-            todo_v = [job for job in jobs if job not in v_grp]
-            by_scalar = todo_v[len(todo_v) - S_MIX :]
-
-            def job_passes(mp, g):
-                for m in (2 * mp, 2 * mp + 1):
-                    one_pass(m, v_codes, v_sc, hp_codes, hp_sc, g, False, g == G - 1)
+            jobs = [(m0, 2, g) for m0 in range(0, MT, 2) for g in range(G)]
+            jobs = jobs[:-1] + [(MT - 2, 1, G - 1), (MT - 1, 1, G - 1)]
+            waiting = [job for job in jobs if job not in v_grp]
+            by_scalar = waiting[len(waiting) - 2 - S_MIX : len(waiting) - 2]
+            by_vector = [job for job in waiting if job not in by_scalar]
 
             widen_some(len(todo) - 12)
             for g in hp_rest:
-                mix(nc.scalar.copy, hp_rest[g][:], h_raw[g][:, :, GP_COLS[g] : 2 * H])
+                mix(nc.scalar.copy, hp_rest[g][:], hp_raw[g][:, :, GP_COLS[g] - H : H])
             widen_some(12)
-            v_mix(*todo_v[0])
-            for mp, g in jobs:
-                if (mp, g) == (1, 0):
-                    for m in range(RES_EARLY):
-                        store(m, False)
-                    for job in by_scalar:
-                        v_mix(*job, nc.scalar.copy, "v_late")
-                    for m in range(RES_EARLY, 2):
-                        store(m, False)
-                if (mp, g) in todo_v:
-                    i = todo_v.index((mp, g))
-                    if i + 1 < len(todo_v) - S_MIX:
-                        v_mix(*todo_v[i + 1])
-                    v_quant(mp, g)
-                if mp == 0 and g in hp_rest:
+            v_mix(by_vector[0])
+            mixed = 1
+            for job in jobs:
+                m0, n, g = job
+                if job == (2, 2, 0):
+                    store(0, False)
+                    store(1, False)
+                    for late in by_scalar:
+                        v_mix(late, nc.scalar.copy, "v_late")
+                if job in waiting:
+                    if mixed < len(by_vector) and (job in by_vector or job == by_scalar[-1]):
+                        v_mix(by_vector[mixed])
+                        mixed = mixed + 1
+                    v_quant(job)
+                if m0 == 0 and g in hp_rest:
                     quant(hp_codes[g], hp_sc[g], GP_COLS[g] - H, 2 * H - GP_COLS[g], hp_rest[g][:])
-                job_passes(mp, g)
-                if (mp, g) == (1, G - 1):
+                for m in range(m0, m0 + n):
+                    one_pass(m, v_codes, v_sc, hp_codes, hp_sc, g, False, g == G - 1)
+                if job == (2, 2, G - 1):
                     store(2, False)
                     store(3, False)
             for m in range(4, MT):
-                store(m, m in V_OUT)
+                store(m, m in V_OUT, TAIL_PARTS if m >= 6 else 1)

@@ -32,7 +32,7 @@ HF1A_V = True
 HF_FIRST = 1
 SPLIT_F = 0
 T_BANKS = 5
-GP_COLS = (768, 896, 768, 768)
+GP_COLS = (768, 768, 768, 768)
 V_HF = (2,)
 WIDEN_AT = (1, 2, 3)
 S_HEAD = 3
@@ -134,11 +134,9 @@ def tile_persistentmeanfieldisingrbmgradient_w4_kernel(
                 load(hn_raw, hn, g)
                 if g + 2 < G and HF_FIRST:
                     load(hf_raw, hf, g + 2)
-                load(hp_raw, hp, g)
-                if g + 2 < G and not HF_FIRST:
-                    load(hf_raw, hf, g + 2)
                 if g + 1 < G:
                     load(v_raw, v_bytes, g + 1)
+                load(hp_raw, hp, g)
 
             hf_grp = {}
             tr_bank = {}
@@ -152,19 +150,17 @@ def tile_persistentmeanfieldisingrbmgradient_w4_kernel(
             def hf_turn(g, h):
                 if h == 0:
                     hf_grp[g] = gate("hf_grp1") if g == 1 else grp("hf_grp%d" % g, g % 3)
-                bk = bank("f" if g > 1 and g not in V_HF else "t", [P, 2, 2, P])
+                bk = bank("f" if g > 1 and g not in V_HF else "t", [P, 2, P, 2])
                 tr_bank[(g, h)] = bk
                 words = hf_raw[g][:].rearrange("p t k -> p (t k)").bitcast(F32)
                 for i in range(2):
                     for u in range(2):
                         base = 256 * (2 * h + i)
-                        nc.tensor.transpose(bk[:, i, u, :], words[:, base + u : base + 256 : 2], ident[:])
+                        nc.tensor.transpose(bk[:, i, :, u], words[:, base + u : base + 256 : 2], ident[:])
 
             def hf_out(g, h, on_vector):
-                dst = hf_grp[g][:, 1024 * h : 1024 * h + 1024].bitcast(F32).rearrange(
-                    "p (i m u) -> p i m u", i=2, u=2
-                )
-                src = tr_bank[(g, h)][:].rearrange("p i u m -> p i m u")
+                dst = hf_grp[g][:, 1024 * h : 1024 * h + 1024].bitcast(F32)
+                src = tr_bank[(g, h)][:].rearrange("p i m u -> p (i m u)")
                 if on_vector:
                     nc.vector.tensor_copy(out=dst, in_=src)
                 else:

@@ -49,7 +49,8 @@ def tile_persistentmeanfieldisingrbmgradient_w4_kernel(
         psum = ctx.enter_context(tc.psum_pool(name="psum", bufs=1))
 
         def kt(name, shape, dtype):
-            return keep.tile(shape, dtype, name=name, align_bytes=64)
+            mx = name.split("_")[1].startswith("codes") or name.split("_")[1].startswith("sc") if "_" in name else False
+            return keep.tile(shape, dtype, name=name, align_bytes=256 if mx else 64)
 
         rings = {"t": ["bank%d" % i for i in range(T_BANKS)], "f": ["bank%d" % i for i in range(T_BANKS, 8)]}
 
@@ -89,6 +90,7 @@ def tile_persistentmeanfieldisingrbmgradient_w4_kernel(
         s_bf = kt("s_bf", [P, G, 4], BF16)
         s_neg = kt("s_neg", [P, G, 4], F32)
         vs = kt("vs", [P, G, 4], F32)
+        vs_first = kt("vs_first", [P, 4], F32)
         zeros = kt("zeros", [P, 512], BF16)
         warm = kt("warm", [P, 1], F32)
 
@@ -98,7 +100,8 @@ def tile_persistentmeanfieldisingrbmgradient_w4_kernel(
             nc.vector.memset(zeros[:], 0.0)
             nc.vector.memset(w_sc[:].bitcast(I32), 0)
             make_identity(nc, ident[:])
-            nc.scalar.dma_start(out=vs[:], in_=v_scale.rearrange("(g p t) o -> p g (t o)", p=P, t=4))
+            scale_rows = v_scale.rearrange("(g p t) o -> p g (t o)", p=P, t=4)
+            nc.scalar.dma_start(out=vs_first[:], in_=scale_rows[:, 0, :])
             nc.scalar.dma_start(out=b_rows[0:MT, :], in_=b.rearrange("(m c) -> m c", c=P))
             nc.scalar.activation(warm[:], warm[:], ACT.Tanh)
 
@@ -130,6 +133,7 @@ def tile_persistentmeanfieldisingrbmgradient_w4_kernel(
                 )
             load_half(1, 1)
             nc.sync.dma_start(out=s_bf[:], in_=s.rearrange("(g p t) -> p g t", p=P, t=4))
+            nc.sync.dma_start(out=vs[:, 1:G, :], in_=scale_rows[:, 1:G, :])
             for g in range(G):
                 load(hn_raw, hn, g)
                 if g + 2 < G and HF_FIRST:
@@ -247,19 +251,18 @@ def tile_persistentmeanfieldisingrbmgradient_w4_kernel(
                     src = v_raw[g][:, t, 512 * h : 512 * h + 512].bitcast(E4M3)
                 else:
                     src = v_first[h][:, t, :].bitcast(E4M3)
+                scale = vs[:, g, t : t + 1] if g else vs_first[:, t : t + 1]
                 if on_vector:
-                    nc.vector.tensor_scalar(
-                        out=dst, in0=src, scalar1=vs[:, g, t : t + 1], scalar2=None, op0=ALU.mult
-                    )
+                    nc.vector.tensor_scalar(out=dst, in0=src, scalar1=scale, scalar2=None, op0=ALU.mult)
                 else:
-                    nc.scalar.activation(dst, src, ACT.Copy, scale=vs[:, g, t : t + 1])
+                    nc.scalar.activation(dst, src, ACT.Copy, scale=scale)
 
             v_grp = {}
 
             def v_mix(job, copy=nc.vector.tensor_copy, tag="v_grp"):
                 m0, n, g = job
                 v_grp[job] = ring.tile(
-                    [P, 512 * n], BF16, name="v_grp%d_%d" % (m0, g), tag=tag, bufs=4, align_bytes=256
+                    [P, 512 * n], BF16, name="v_grp%d_%d" % (m0, g), tag=tag, bufs=4 if tag == "v_grp" else S_MIX, align_bytes=256
                 )
                 c0 = P * (m0 % 4)
                 mix(copy, v_grp[job][:], v_wide[(m0 // 4, g)][:, :, c0 : c0 + P * n])

@@ -18,25 +18,17 @@ ACT = mybir.ActivationFunctionType
 ALU = mybir.AluOpType
 
 P = 128
-G = 4
+SLOTS = 4
+G = B // (P * SLOTS)
 MT = V // P
+HALF = V // 2
 PAIRS = G * MT // 2
-S_MIX = 2
-V_OUT = (5, 7)
-WARM = (4, 1, 1, 1)
-V1_TAG = (1, 3, 1, 4, 1, 5, 2, 0)
-TAIL_PARTS = 1
-V0_FIRST = False
-S_FIRST = 1
-HF1A_V = True
-HF_FIRST = 1
-SPLIT_F = 0
-T_BANKS = 5
-GP_COLS = (768, 768, 768, 768)
-V_HF = (2,)
-WIDEN_AT = (1, 2, 3)
-S_HEAD = 3
-HEAD_JOB = 1
+PAIRS_PER_GROUP = MT // 2
+
+TURN_BANKS = 5
+HP_GPSIMD = 256
+HEAD_SLOTS_SCALAR = 3
+SCALAR_JOBS = 2
 
 
 def tile_persistentmeanfieldisingrbmgradient_w4_kernel(
@@ -48,416 +40,420 @@ def tile_persistentmeanfieldisingrbmgradient_w4_kernel(
         ring = ctx.enter_context(tc.tile_pool(name="ring", bufs=1))
         psum = ctx.enter_context(tc.psum_pool(name="psum", bufs=1))
 
-        def kt(name, shape, dtype):
-            mx = name.split("_")[1].startswith("codes") or name.split("_")[1].startswith("sc") if "_" in name else False
-            return keep.tile(shape, dtype, name=name, align_bytes=256 if mx else 64)
+        def kept(name, shape, dtype, align=64):
+            return keep.tile(shape, dtype, name=name, align_bytes=align)
 
-        rings = {"t": ["bank%d" % i for i in range(T_BANKS)], "f": ["bank%d" % i for i in range(T_BANKS, 8)]}
+        def reused(name, shape, dtype, tag, bufs=1):
+            return ring.tile(shape, dtype, name=name, tag=tag, bufs=bufs, align_bytes=256)
 
-        def bank(kind, shape, keep_it=False):
-            nm = rings[kind][0]
-            rings[kind].remove(nm)
-            if not keep_it:
-                rings[kind].append(nm)
-            return psum.tile(shape, F32, name=nm, tag=nm)
+        def mx_operand(name, width):
+            codes = [kept("%s_codes%d" % (name, g), [P, width], U32, 256) for g in range(G)]
+            scales = [kept("%s_scales%d" % (name, g), [P, width], U8, 256) for g in range(G)]
+            return codes, scales
 
-        def rows_tile(name, g):
-            return ring.tile([P, 4, H], BF16, name=name, tag="rows%d" % g, bufs=1, align_bytes=256)
+        turns = {
+            "turn": ["bank%d" % i for i in range(TURN_BANKS)],
+            "field": ["bank%d" % i for i in range(TURN_BANKS, 8)],
+        }
 
-        hf_raw = [rows_tile("hf_raw%d" % g, g) for g in range(G)]
-        hn_raw = [kt("hn_raw%d" % g, [P, 4, H], BF16) for g in range(G)]
-        hp_raw = [kt("hp_raw%d" % g, [P, 4, H], BF16) for g in range(G)]
-        hp_rest = {g: kt("hp_rest%d" % g, [P, 4 * (2 * H - GP_COLS[g])], BF16) for g in range(G) if GP_COLS[g] < 2 * H}
-        v_raw = {g: kt("v_raw%d" % g, [P, 4, V], U8) for g in range(1, G)}
-        v_first = [kt("v_first%d" % h, [P, 4, 512], U8) for h in range(2)]
-        v_wide = {(0, g): kt("v_wide0_%d" % g, [P, 4, 512], BF16) for g in range(G)}
-        hf_codes = [kt("hf_codes%d" % g, [P, 512], U32) for g in range(G)]
-        hf_sc = [kt("hf_sc%d" % g, [P, 512], U8) for g in range(G)]
-        hn_codes = [kt("hn_codes%d" % g, [P, H], U32) for g in range(G)]
-        hn_sc = [kt("hn_sc%d" % g, [P, H], U8) for g in range(G)]
-        hp_codes = [kt("hp_codes%d" % g, [P, H], U32) for g in range(G)]
-        hp_sc = [kt("hp_sc%d" % g, [P, H], U8) for g in range(G)]
-        v1_codes = [kt("v1_codes%d" % g, [P, V], U32) for g in range(G)]
-        v1_sc = [kt("v1_sc%d" % g, [P, V], U8) for g in range(G)]
-        v_codes = [kt("v_codes%d" % g, [P, V], U32) for g in range(G)]
-        v_sc = [kt("v_sc%d" % g, [P, V], U8) for g in range(G)]
-        w_codes = kt("w_codes", [P, 2 * V], U8)
-        w_sc = kt("w_sc", [P, V], U8)
-        ident = kt("ident", [P, P], F32)
-        b_rows = kt("b_rows", [P, P], BF16)
-        b_rows32 = kt("b_rows32", [P, P], F32)
-        bias = kt("bias", [P, MT], F32)
-        s_bf = kt("s_bf", [P, G, 4], BF16)
-        s_neg = kt("s_neg", [P, G, 4], F32)
-        vs = kt("vs", [P, G, 4], F32)
-        vs_first = kt("vs_first", [P, 4], F32)
-        zeros = kt("zeros", [P, 512], BF16)
-        warm = kt("warm", [P, 1], F32)
+        def next_bank(kind, shape, for_good=False):
+            name = turns[kind][0]
+            turns[kind].remove(name)
+            if not for_good:
+                turns[kind].append(name)
+            return psum.tile(shape, F32, name=name, tag=name)
+
+        hf_rows = [reused("hf_rows%d" % g, [P, SLOTS, H], BF16, "rows%d" % g) for g in range(G)]
+        hn_rows = [kept("hn_rows%d" % g, [P, SLOTS, H], BF16) for g in range(G)]
+        hp_rows = [kept("hp_rows%d" % g, [P, SLOTS, H], BF16) for g in range(G)]
+        hp_rest = [kept("hp_rest%d" % g, [P, SLOTS * (H - HP_GPSIMD)], BF16) for g in range(G)]
+        v_rows = {g: kept("v_rows%d" % g, [P, SLOTS, V], U8) for g in range(1, G)}
+        v_rows_first = [kept("v_rows_first%d" % half, [P, SLOTS, HALF], U8) for half in range(2)]
+        v_wide = {(0, g): kept("v_wide0_%d" % g, [P, SLOTS, HALF], BF16) for g in range(G)}
+        hf_mx = mx_operand("hf", P * SLOTS)
+        hn_mx = mx_operand("hn", H)
+        hp_mx = mx_operand("hp", H)
+        v1_mx = mx_operand("v1", V)
+        v_mx = mx_operand("v", V)
+        w_codes = kept("w_codes", [P, 2 * V], U8, 256)
+        w_plane = kept("w_plane", [P, V], U8, 256)
+        ident = kept("ident", [P, P], F32)
+        b_rows = kept("b_rows", [P, P], BF16)
+        b_rows32 = kept("b_rows32", [P, P], F32)
+        bias = kept("bias", [P, MT], F32)
+        s_rows = kept("s_rows", [P, G, SLOTS], BF16)
+        s_neg = kept("s_neg", [P, G, SLOTS], F32)
+        scale_later = kept("scale_later", [P, G - 1, SLOTS], F32)
+        scale_first = kept("scale_first", [P, SLOTS], F32)
+        zeros = kept("zeros", [P, 512], BF16)
+        table_warm = kept("table_warm", [P, 1], F32)
 
         with tc.manual_schedule():
-            nc.vector.memset(warm[:], 0.0)
+            nc.vector.memset(table_warm[:], 0.0)
             nc.vector.memset(b_rows[:], 0.0)
             nc.vector.memset(zeros[:], 0.0)
-            nc.vector.memset(w_sc[:].bitcast(I32), 0)
+            nc.vector.memset(w_plane[:].bitcast(I32), 0)
             make_identity(nc, ident[:])
-            scale_rows = v_scale.rearrange("(g p t) o -> p g (t o)", p=P, t=4)
-            nc.scalar.dma_start(out=vs_first[:], in_=scale_rows[:, 0, :])
-            nc.scalar.dma_start(out=b_rows[0:MT, :], in_=b.rearrange("(m c) -> m c", c=P))
-            nc.scalar.activation(warm[:], warm[:], ACT.Tanh)
+            scale_view = v_scale.rearrange("(g p t) o -> p g (t o)", p=P, t=SLOTS)
+            nc.scalar.dma_start(out=scale_first[:], in_=scale_view[:, 0, :])
+            nc.scalar.activation(table_warm[:], table_warm[:], ACT.Tanh)
 
-            def rows(x, g):
-                return x.rearrange("(g p t) k -> g p t k", p=P, t=4)[g]
+            def group_rows(x, g):
+                return x.rearrange("(g p t) c -> g p t c", p=P, t=SLOTS)[g]
 
-            def load(dst, x, g):
-                nc.sync.dma_start(out=dst[g][:], in_=rows(x, g))
+            def load(tiles, x, g):
+                nc.sync.dma_start(out=tiles[g][:], in_=group_rows(x, g))
 
-            def load_half(g, h):
-                nc.sync.dma_start(out=hf_raw[g][:, 2 * h : 2 * h + 2, :], in_=rows(hf, g)[:, 2 * h : 2 * h + 2, :])
+            def load_hf_slots(g, pair):
+                slots = slice(2 * pair, 2 * pair + 2)
+                nc.sync.dma_start(out=hf_rows[g][:, slots, :], in_=group_rows(hf, g)[:, slots, :])
 
-            def load_v0(h):
-                nc.sync.dma_start(out=v_first[h][:], in_=rows(v_bytes, 0)[:, :, 512 * h : 512 * h + 512])
+            def load_v_first(half):
+                cols = slice(HALF * half, HALF * half + HALF)
+                nc.sync.dma_start(out=v_rows_first[half][:], in_=group_rows(v_bytes, 0)[:, :, cols])
 
-            load_v0(0)
-            if V0_FIRST:
-                load_v0(1)
-            load_half(0, 0)
-            load_half(0, 1)
-            if not V0_FIRST:
-                load_v0(1)
-            load_half(1, 0)
+            load_v_first(0)
+            load_hf_slots(0, 0)
+            load_hf_slots(0, 1)
+            nc.sync.dma_start(out=b_rows[0:MT, :], in_=b.rearrange("(m c) -> m c", c=P))
+            load_v_first(1)
+            load_hf_slots(1, 0)
             nc.sync.dma_start(out=w_codes[:], in_=w_words[0])
             for q in range(4):
                 nc.sync.dma_start(
-                    out=w_sc[32 * q : 32 * q + 4, :].bitcast(I32),
+                    out=w_plane[32 * q : 32 * q + 4, :].bitcast(I32),
                     in_=w_scales[0][4 * q : 4 * q + 4, :].bitcast(I32),
                 )
-            load_half(1, 1)
-            nc.sync.dma_start(out=s_bf[:], in_=s.rearrange("(g p t) -> p g t", p=P, t=4))
-            nc.sync.dma_start(out=vs[:, 1:G, :], in_=scale_rows[:, 1:G, :])
+            load_hf_slots(1, 1)
+            nc.sync.dma_start(out=s_rows[:], in_=s.rearrange("(g p t) -> p g t", p=P, t=SLOTS))
+            nc.sync.dma_start(out=scale_later[:], in_=scale_view[:, 1:G, :])
             for g in range(G):
-                load(hn_raw, hn, g)
-                if g + 2 < G and HF_FIRST:
-                    load(hf_raw, hf, g + 2)
+                load(hn_rows, hn, g)
+                if g + 2 < G:
+                    load(hf_rows, hf, g + 2)
                 if g + 1 < G:
-                    load(v_raw, v_bytes, g + 1)
-                load(hp_raw, hp, g)
+                    load(v_rows, v_bytes, g + 1)
+                load(hp_rows, hp, g)
 
-            hf_grp = {}
-            tr_bank = {}
+            def quantise(operand, g, col, width, src):
+                codes, scales = operand
+                nc.vector.quantize_mx(
+                    out=codes[g][:, col : col + width].bitcast(E4M3X4),
+                    scales=scales[g][:, col : col + width],
+                    in_=src,
+                )
 
-            def grp(nm, tag):
-                return ring.tile([P, 2048], BF16, name=nm, tag="grp%d" % tag, bufs=1, align_bytes=256)
+            def staging(name, number):
+                return reused(name, [P, SLOTS * 512], BF16, "staging%d" % number)
 
-            def gate(nm):
-                return ring.tile([P, 4 * max(GP_COLS)], BF16, name=nm, tag="gate", bufs=1, align_bytes=256)
+            def gpsimd_buffer(name):
+                return reused(name, [P, SLOTS * (H + HP_GPSIMD)], BF16, "gpsimd_buffer")
 
-            def hf_turn(g, h):
-                if h == 0:
-                    hf_grp[g] = gate("hf_grp1") if g == 1 else grp("hf_grp%d" % g, g % 3)
-                bk = bank("f" if g > 1 and g not in V_HF else "t", [P, 2, P, 2])
-                tr_bank[(g, h)] = bk
-                words = hf_raw[g][:].rearrange("p t k -> p (t k)").bitcast(F32)
+            hf_staged = {}
+            hf_bank = {}
+
+            def on_field_bank(g):
+                return g == G - 1
+
+            def hf_turn(g, pair):
+                if pair == 0:
+                    if g == 1:
+                        hf_staged[g] = gpsimd_buffer("hf_staged1")
+                    else:
+                        hf_staged[g] = staging("hf_staged%d" % g, g % 3)
+                bank = next_bank("field" if on_field_bank(g) else "turn", [P, 2, P, 2])
+                hf_bank[(g, pair)] = bank
+                words = hf_rows[g][:].rearrange("p t k -> p (t k)").bitcast(F32)
                 for i in range(2):
+                    first = H // 2 * (2 * pair + i)
                     for u in range(2):
-                        base = 256 * (2 * h + i)
-                        nc.tensor.transpose(bk[:, i, :, u], words[:, base + u : base + 256 : 2], ident[:])
+                        nc.tensor.transpose(bank[:, i, :, u], words[:, first + u : first + H // 2 : 2], ident[:])
 
-            def hf_out(g, h, on_vector):
-                dst = hf_grp[g][:, 1024 * h : 1024 * h + 1024].bitcast(F32)
-                src = tr_bank[(g, h)][:].rearrange("p i m u -> p (i m u)")
-                if on_vector:
-                    nc.vector.tensor_copy(out=dst, in_=src)
-                else:
-                    nc.scalar.copy(out=dst, in_=src)
+            def hf_copy_out(g, pair, copy):
+                copy(
+                    out=hf_staged[g][:, 1024 * pair : 1024 * pair + 1024].bitcast(F32),
+                    in_=hf_bank[(g, pair)][:].rearrange("p i r u -> p (i r u)"),
+                )
 
-            def quant(codes, sc, c0, n, src):
-                done = 0
-                for w in (512, 256, 128, 64):
-                    if n - done >= w:
-                        a = c0 + done
-                        nc.vector.quantize_mx(
-                            out=codes[:, a : a + w].bitcast(E4M3X4),
-                            scales=sc[:, a : a + w],
-                            in_=src[:, 4 * done : 4 * (done + w)],
-                        )
-                        done = done + w
+            field_bank = {}
+            tanh_tile = {}
+            turned_bank = {}
+            v1_staged = {}
 
-            f_bank = {}
-            th = {}
-            t_bank = {}
-            v1_grp = {}
-
-            def field(u):
-                g, m = u // MT, u % MT
-                f_bank[u] = bank("f", [P, 512])
+            def field(unit):
+                g, m = divmod(unit, MT)
+                field_bank[unit] = next_bank("field", [P, P * SLOTS])
                 nc.tensor.matmul_mx(
-                    out=f_bank[u][:],
-                    lhsT=w_codes[:, 256 * m : 256 * m + 256].bitcast(E2M1X4),
-                    lhsT_scale=w_sc[:, P * m : P * m + P],
-                    rhs=hf_codes[g][:].bitcast(E4M3X4),
-                    rhs_scale=hf_sc[g][:],
+                    out=field_bank[unit][:],
+                    lhsT=w_codes[:, 2 * P * m : 2 * P * (m + 1)].bitcast(E2M1X4),
+                    lhsT_scale=w_plane[:, P * m : P * (m + 1)],
+                    rhs=hf_mx[0][g][:].bitcast(E4M3X4),
+                    rhs_scale=hf_mx[1][g][:],
                     start=True,
                     stop=True,
                 )
 
-            def tanh(u):
-                m = u % MT
-                th[u] = ring.tile([P, 4, P], F32, name="th%d" % u, tag="th", bufs=8, align_bytes=256)
+            def float_tile(name, shape):
+                return reused(name, shape, F32, "float_tile", 8)
+
+            def tanh(unit):
+                m = unit % MT
+                tanh_tile[unit] = float_tile("tanh%d" % unit, [P, SLOTS, P])
                 nc.scalar.activation(
-                    th[u][:].rearrange("p t q -> p (t q)"), f_bank[u][:], ACT.Tanh, bias=bias[:, m : m + 1]
+                    tanh_tile[unit][:].rearrange("p t r -> p (t r)"),
+                    field_bank[unit][:],
+                    ACT.Tanh,
+                    bias=bias[:, m : m + 1],
                 )
 
-            def turn(u):
-                t_bank[u] = bank("t", [P, 4, P])
-                for t in range(4):
-                    nc.tensor.transpose(t_bank[u][:, t, :], th[u][:, t, :], ident[:])
+            def turn(unit):
+                turned_bank[unit] = next_bank("turn", [P, SLOTS, P])
+                for t in range(SLOTS):
+                    nc.tensor.transpose(turned_bank[unit][:, t, :], tanh_tile[unit][:, t, :], ident[:])
 
-            def weight(u):
-                g, m = u // MT, u % MT
-                if m % 4 == 0:
-                    v1_grp[u // 4] = grp("v1_grp%d" % (u // 4), V1_TAG[u // 4])
-                c = m % 4
+            def v1_buffer(g, half):
+                if g == G - 1:
+                    return (2 + half) % 3
+                return 3 + g if half else 1
+
+            def weight(unit):
+                g, m = divmod(unit, MT)
+                half, c = divmod(m, MT // 2)
+                if c == 0:
+                    v1_staged[(g, half)] = staging("v1_staged%d_%d" % (g, half), v1_buffer(g, half))
                 nc.vector.tensor_tensor(
-                    out=v1_grp[u // 4][:, 512 * c : 512 * c + 512].rearrange("p (q t) -> p q t", t=4),
-                    in0=t_bank[u][:].rearrange("p t q -> p q t"),
-                    in1=s_neg[:, g, :].unsqueeze(1).to_broadcast([P, P, 4]),
+                    out=v1_staged[(g, half)][:, 512 * c : 512 * c + 512].rearrange("p (c t) -> p c t", t=SLOTS),
+                    in0=turned_bank[unit][:].rearrange("p t c -> p c t"),
+                    in1=s_neg[:, g, :].unsqueeze(1).to_broadcast([P, P, SLOTS]),
                     op=ALU.mult,
                 )
 
-            def v1_quant(g, h):
-                quant(v1_codes[g], v1_sc[g], 512 * h, 512, v1_grp[2 * g + h][:])
+            def v1_quantise(g, half):
+                quantise(v1_mx, g, HALF * half, HALF, v1_staged[(g, half)][:])
 
-            def mix_gpsimd(dst, src):
-                nc.gpsimd.tensor_scalar(
-                    out=dst.rearrange("p (c t) -> p c t", t=4),
-                    in0=src.rearrange("p t c -> p c t"),
-                    scalar1=1.0,
-                    scalar2=0.0,
-                    op0=ALU.mult,
-                    op1=ALU.add,
-                )
-
-            def mix(copy, dst, src):
+            def interleave(copy, dst, src):
                 copy(
-                    out=dst.rearrange("p (c i t) -> p c t i", i=4, t=4),
+                    out=dst.rearrange("p (c i t) -> p c t i", i=4, t=SLOTS),
                     in_=src.rearrange("p t (c i) -> p c t i", i=4),
                 )
 
-            def widen(h, g, t, on_vector):
-                if (h, g) not in v_wide:
-                    v_wide[(h, g)] = rows_tile("v_wide1_%d" % g, g)
-                dst = v_wide[(h, g)][:, t, :]
-                if g:
-                    src = v_raw[g][:, t, 512 * h : 512 * h + 512].bitcast(E4M3)
+            def gpsimd_share(g):
+                staged = gpsimd_buffer("h_staged%d" % g)
+                parts = (
+                    (staged[:, 0 : SLOTS * H], hn_rows[g][:]),
+                    (staged[:, SLOTS * H :], hp_rows[g][:, :, 0:HP_GPSIMD]),
+                )
+                for dst, src in parts:
+                    nc.gpsimd.tensor_scalar(
+                        out=dst.rearrange("p (c t) -> p c t", t=SLOTS),
+                        in0=src.rearrange("p t c -> p c t"),
+                        scalar1=1.0,
+                        scalar2=0.0,
+                        op0=ALU.mult,
+                        op1=ALU.add,
+                    )
+                return staged
+
+            def widen(half, g, t, on_vector):
+                if (half, g) not in v_wide:
+                    v_wide[(half, g)] = reused("v_wide1_%d" % g, [P, SLOTS, HALF], BF16, "rows%d" % g)
+                dst = v_wide[(half, g)][:, t, :]
+                if g == 0:
+                    src = v_rows_first[half][:, t, :].bitcast(E4M3)
+                    scale = scale_first[:, t : t + 1]
                 else:
-                    src = v_first[h][:, t, :].bitcast(E4M3)
-                scale = vs[:, g, t : t + 1] if g else vs_first[:, t : t + 1]
+                    src = v_rows[g][:, t, HALF * half : HALF * half + HALF].bitcast(E4M3)
+                    scale = scale_later[:, g - 1, t : t + 1]
                 if on_vector:
                     nc.vector.tensor_scalar(out=dst, in0=src, scalar1=scale, scalar2=None, op0=ALU.mult)
                 else:
                     nc.scalar.activation(dst, src, ACT.Copy, scale=scale)
 
-            v_grp = {}
+            v_staged = {}
 
-            def v_mix(job, copy=nc.vector.tensor_copy, tag="v_grp"):
-                m0, n, g = job
-                v_grp[job] = ring.tile(
-                    [P, 512 * n], BF16, name="v_grp%d_%d" % (m0, g), tag=tag, bufs=4 if tag == "v_grp" else S_MIX, align_bytes=256
+            def v_interleave(job, on_vector=True):
+                m0, tiles, g = job
+                name = "v_staged%d_%d" % (m0, g)
+                if on_vector:
+                    v_staged[job] = reused(name, [P, 512 * tiles], BF16, "v_staged", 4)
+                else:
+                    v_staged[job] = reused(name, [P, 512 * tiles], BF16, "v_staged_scalar", SCALAR_JOBS)
+                half, first = divmod(P * m0, HALF)
+                interleave(
+                    nc.vector.tensor_copy if on_vector else nc.scalar.copy,
+                    v_staged[job][:],
+                    v_wide[(half, g)][:, :, first : first + P * tiles],
                 )
-                c0 = P * (m0 % 4)
-                mix(copy, v_grp[job][:], v_wide[(m0 // 4, g)][:, :, c0 : c0 + P * n])
 
-            def v_quant(job):
-                m0, n, g = job
-                quant(v_codes[g], v_sc[g], P * m0, P * n, v_grp[job][:])
+            def v_quantise(job):
+                m0, tiles, g = job
+                quantise(v_mx, g, P * m0, P * tiles, v_staged[job][:])
 
-            todo = ([] if V0_FIRST else [(0, 0, 0)]) + [(1, 0, t) for t in range(S_HEAD)]
-            todo = todo + [(0, g, t) for g in range(1, G) for t in range(4)]
-            todo = todo + [(1, g, t) for g in range(1, G) for t in range(4)]
+            acc = []
 
-            def widen_some(n):
-                for k in range(min(n, len(todo))):
-                    widen(*todo[0], False)
-                    todo.remove(todo[0])
+            def open_acc(kind):
+                acc.append(next_bank(kind, [P, H], True))
 
-            def warm_up(n):
-                for i in range(n):
-                    nc.tensor.matmul(warm_bank[:], lhsT=zeros[:, 0:P], rhs=zeros[:], start=True, stop=True)
-
-            warm_bank = psum.tile([P, 512], F32, name="warm_bank", tag="bank7")
-            warm_up(WARM[0])
-            widen_some(S_FIRST)
-            for t in range(0 if V0_FIRST else 1, 4):
-                widen(0, 0, t, True)
-            hf_turn(0, 0)
-            warm_up(WARM[1])
-            hf_turn(0, 1)
-            warm_up(WARM[2])
-            v_mix((0, 2, 0))
-            v_mix((2, 2, 0))
-            hf_out(0, 0, False)
-            nc.vector.tensor_copy(out=b_rows32[:], in_=b_rows[:])
-            quant(hf_codes[0], hf_sc[0], 0, 256, hf_grp[0][:, 0:1024])
-            hf_out(0, 1, False)
-            b_bank = bank("t", [P, P])
-            nc.tensor.transpose(b_bank[:], b_rows32[:], ident[:])
-            v_quant((0, 2, 0))
-            quant(hf_codes[0], hf_sc[0], 256, 256, hf_grp[0][:, 1024:2048])
-            nc.vector.tensor_copy(out=bias[:], in_=b_bank[:, 0:MT])
-            v_quant((2, 2, 0))
-            hf_turn(1, 0)
-            warm_up(WARM[3])
-            widen_some(S_HEAD - (S_FIRST if V0_FIRST else 0))
-            hf_out(1, 0, HF1A_V)
-            for u in range(3):
-                field(u)
-            hf_turn(1, 1)
-            tanh(0)
-            field(3)
-            tanh(1)
-            nc.vector.tensor_scalar(out=s_neg[:], in0=s_bf[:], scalar1=-1.0, scalar2=None, op0=ALU.mult)
-            for t in range(S_HEAD, 4):
-                widen(1, 0, t, True)
-            for i in range(HEAD_JOB):
-                v_mix((4 + 2 * i, 2, 0))
-            hf_out(1, 1, True)
-            for i in range(HEAD_JOB):
-                v_quant((4 + 2 * i, 2, 0))
-
-            acc = {}
-
-            def one_pass(m, codes, sc, rc, rs, g, first, last):
-                c0 = P * m
+            def correlate(m, vis_mx, hid_mx, g, first=False, last=False):
                 nc.tensor.matmul_mx(
                     out=acc[m][:],
-                    lhsT=codes[g][:, c0 : c0 + P].bitcast(E4M3X4),
-                    lhsT_scale=sc[g][:, c0 : c0 + P],
-                    rhs=rc[g][:].bitcast(E4M3X4),
-                    rhs_scale=rs[g][:],
+                    lhsT=vis_mx[0][g][:, P * m : P * (m + 1)].bitcast(E4M3X4),
+                    lhsT_scale=vis_mx[1][g][:, P * m : P * (m + 1)],
+                    rhs=hid_mx[0][g][:].bitcast(E4M3X4),
+                    rhs_scale=hid_mx[1][g][:],
                     start=first,
                     stop=last,
                 )
 
-            passes = {}
+            def open_with_early_groups(kind):
+                open_acc(kind)
+                for g in range(G - 1):
+                    correlate(len(acc) - 1, v1_mx, hn_mx, g, first=g == 0)
 
-            def open_acc(kind):
-                m = len(acc)
-                acc[m] = bank(kind, [P, H], True)
-                passes[m] = 0
+            def store(m, on_vector):
+                result = float_tile("result%d" % m, [P, H])
+                if on_vector:
+                    nc.vector.tensor_scalar(
+                        out=result[:], in0=acc[m][:], scalar1=float(B) ** -0.5, scalar2=None, op0=ALU.mult
+                    )
+                else:
+                    nc.scalar.activation(result[:], acc[m][:], ACT.Copy, scale=float(B) ** -0.5)
+                nc.sync.dma_start(out=out[P * m : P * (m + 1), :], in_=result[:])
 
-            def neg_upto(n):
-                for m in acc:
-                    for g in range(passes[m], n):
-                        one_pass(m, v1_codes, v1_sc, hn_codes, hn_sc, g, g == 0, False)
-                    passes[m] = max(passes[m], n)
+            warm_bank = psum.tile([P, 512], F32, name="warm_bank", tag="bank7")
 
+            def warm_up():
+                nc.tensor.matmul(warm_bank[:], lhsT=zeros[:, 0:P], rhs=zeros[:], start=True, stop=True)
+
+            for i in range(4):
+                warm_up()
+            widen(0, 0, 0, False)
+            for t in range(1, SLOTS):
+                widen(0, 0, t, True)
+            for pair in range(2):
+                hf_turn(0, pair)
+                warm_up()
+            v_interleave((0, 2, 0))
+            v_interleave((2, 2, 0))
+            hf_copy_out(0, 0, nc.scalar.copy)
+            nc.vector.tensor_copy(out=b_rows32[:], in_=b_rows[:])
+            quantise(hf_mx, 0, 0, 256, hf_staged[0][:, 0:1024])
+            hf_copy_out(0, 1, nc.scalar.copy)
+            bias_bank = next_bank("turn", [P, P])
+            nc.tensor.transpose(bias_bank[:], b_rows32[:], ident[:])
+            v_quantise((0, 2, 0))
+            quantise(hf_mx, 0, 256, 256, hf_staged[0][:, 1024:2048])
+            nc.vector.tensor_copy(out=bias[:], in_=bias_bank[:, 0:MT])
+            v_quantise((2, 2, 0))
+            hf_turn(1, 0)
+            warm_up()
+            for t in range(HEAD_SLOTS_SCALAR):
+                widen(1, 0, t, False)
+            hf_copy_out(1, 0, nc.vector.tensor_copy)
+            for unit in range(3):
+                field(unit)
+            hf_turn(1, 1)
+            tanh(0)
+            field(3)
+            tanh(1)
+            nc.vector.tensor_scalar(out=s_neg[:], in0=s_rows[:], scalar1=-1.0, scalar2=None, op0=ALU.mult)
+            for t in range(HEAD_SLOTS_SCALAR, SLOTS):
+                widen(1, 0, t, True)
+            v_interleave((4, 2, 0))
+            hf_copy_out(1, 1, nc.vector.tensor_copy)
+            v_quantise((4, 2, 0))
+
+            first_halves = [(0, g, t) for g in range(1, G) for t in range(SLOTS)]
+            widened = 0
             for j in range(PAIRS):
-                g = j // 4
+                g, step = divmod(j, PAIRS_PER_GROUP)
+                hf_next = g + 2 if step in (1, 2) and g + 2 < G else None
+                by_scalar = hf_next is not None and on_field_bank(hf_next)
                 turn(2 * j)
                 turn(2 * j + 1)
                 if j + 1 < PAIRS:
                     tanh(2 * j + 2)
-                turns_hf = j % 4 in (1, 2) and g + 2 < G
-                early_field = SPLIT_F and turns_hf and g + 2 in V_HF
-                if early_field:
-                    field(2 * j + 4)
-                if turns_hf:
-                    hf_turn(g + 2, j % 4 - 1)
+                if hf_next:
+                    hf_turn(hf_next, step - 1)
                 if j + 1 < PAIRS:
                     tanh(2 * j + 3)
-                if turns_hf and g + 2 not in V_HF:
-                    hf_out(g + 2, j % 4 - 1, False)
+                if by_scalar:
+                    hf_copy_out(hf_next, step - 1, nc.scalar.copy)
                 if j + 2 < PAIRS:
-                    if not early_field:
-                        field(2 * j + 4)
+                    field(2 * j + 4)
                     field(2 * j + 5)
                 if j + 2 == PAIRS:
-                    open_acc("f")
+                    open_with_early_groups("field")
                 if j + 1 == PAIRS:
-                    open_acc("f")
-                    open_acc("f")
-                if j + 2 >= PAIRS:
-                    neg_upto(G - 1)
-                if (turns_hf and g + 2 in V_HF) or (not turns_hf and j % 4 in WIDEN_AT):
-                    widen_some(1)
-                if j % 4 == 0 and j:
-                    h_grp = gate("h_grp%d" % g)
-                    mix_gpsimd(h_grp[:, 0 : 4 * H], hn_raw[g][:])
-                    mix_gpsimd(h_grp[:, 4 * H : 4 * GP_COLS[g]], hp_raw[g][:, :, 0 : GP_COLS[g] - H])
+                    open_with_early_groups("field")
+                    open_with_early_groups("field")
+                if step > 0 and not by_scalar:
+                    widen(*first_halves[widened], False)
+                    widened = widened + 1
+                if step == 0 and g > 0:
+                    h_staged = gpsimd_share(g)
                 weight(2 * j)
                 weight(2 * j + 1)
-                if turns_hf and g + 2 in V_HF:
-                    hf_out(g + 2, j % 4 - 1, True)
+                if hf_next and not by_scalar:
+                    hf_copy_out(hf_next, step - 1, nc.vector.tensor_copy)
                 if j == 0:
-                    quant(hf_codes[1], hf_sc[1], 0, 512, hf_grp[1][:, 0:2048])
-                    h_grp = gate("h_grp%d" % g)
-                    mix_gpsimd(h_grp[:, 0 : 4 * H], hn_raw[g][:])
-                    mix_gpsimd(h_grp[:, 4 * H : 4 * GP_COLS[g]], hp_raw[g][:, :, 0 : GP_COLS[g] - H])
-                if j % 4 == 3:
+                    quantise(hf_mx, 1, 0, 512, hf_staged[1][:, 0:2048])
+                    h_staged = gpsimd_share(0)
+                if step == PAIRS_PER_GROUP - 1:
                     if g + 2 < G:
-                        quant(hf_codes[g + 2], hf_sc[g + 2], 0, 512, hf_grp[g + 2][:])
+                        quantise(hf_mx, g + 2, 0, 512, hf_staged[g + 2][:])
                     if g == G - 1:
-                        v1_quant(0, 1)
-                    v1_quant(g, 0)
-                    quant(hp_codes[g], hp_sc[g], 0, GP_COLS[g] - H, h_grp[:, 4 * H : 4 * GP_COLS[g]])
-                    quant(hn_codes[g], hn_sc[g], 0, 512, h_grp[:, 0 : 4 * H])
-
-            def store(m, on_vector, parts=1):
-                res = ring.tile([P, H], F32, name="res%d" % m, tag="th", bufs=8, align_bytes=256)
-                for i in range(parts):
-                    cols = slice(H // parts * i, H // parts * (i + 1))
-                    if on_vector:
-                        nc.vector.tensor_scalar(
-                            out=res[:, cols], in0=acc[m][:, cols], scalar1=float(B) ** -0.5, scalar2=None, op0=ALU.mult
-                        )
-                    else:
-                        nc.scalar.activation(res[:, cols], acc[m][:, cols], ACT.Copy, scale=float(B) ** -0.5)
-                    nc.sync.dma_start(out=out[P * m : P * m + P, cols], in_=res[:, cols])
+                        v1_quantise(0, 1)
+                    v1_quantise(g, 0)
+                    quantise(hp_mx, g, 0, HP_GPSIMD, h_staged[:, SLOTS * H :])
+                    quantise(hn_mx, g, 0, H, h_staged[:, 0 : SLOTS * H])
 
             for g in range(1, G):
-                v1_quant(g, 1)
-            open_acc("t")
-            neg_upto(G - 1)
-            while len(acc) < MT:
-                open_acc("t")
-                passes[len(acc) - 1] = 1
-                one_pass(len(acc) - 1, v1_codes, v1_sc, hn_codes, hn_sc, 0, True, False)
-            for m in range(4):
-                one_pass(m, v1_codes, v1_sc, hn_codes, hn_sc, G - 1, False, False)
+                v1_quantise(g, 1)
+            open_with_early_groups("turn")
+            for m in range(MT // 2, MT):
+                open_acc("turn")
+                correlate(m, v1_mx, hn_mx, 0, first=True)
+            for m in range(MT // 2):
+                correlate(m, v1_mx, hn_mx, G - 1)
             for g in range(1, G):
-                for m in range(4, MT):
-                    one_pass(m, v1_codes, v1_sc, hn_codes, hn_sc, g, False, False)
+                for m in range(MT // 2, MT):
+                    correlate(m, v1_mx, hn_mx, g)
 
             jobs = [(m0, 2, g) for m0 in range(0, MT, 2) for g in range(G)]
             jobs = jobs[:-1] + [(MT - 2, 1, G - 1), (MT - 1, 1, G - 1)]
-            waiting = [job for job in jobs if job not in v_grp]
-            by_scalar = waiting[len(waiting) - 2 - S_MIX : len(waiting) - 2]
-            by_vector = [job for job in waiting if job not in by_scalar]
+            to_make = [job for job in jobs if job not in v_staged]
+            scalar_jobs = to_make[-2 - SCALAR_JOBS : -2]
+            vector_jobs = [job for job in to_make if job not in scalar_jobs]
 
-            widen_some(len(todo) - 12)
-            for g in hp_rest:
-                mix(nc.scalar.copy, hp_rest[g][:], hp_raw[g][:, :, GP_COLS[g] - H : H])
-            widen_some(12)
-            v_mix(by_vector[0])
-            mixed = 1
+            for item in first_halves[widened:]:
+                widen(*item, False)
+            for g in range(G):
+                interleave(nc.scalar.copy, hp_rest[g][:], hp_rows[g][:, :, HP_GPSIMD:H])
+            for g in range(1, G):
+                for t in range(SLOTS):
+                    widen(1, g, t, False)
+
+            v_interleave(vector_jobs[0])
+            started = 1
             for job in jobs:
-                m0, n, g = job
+                m0, tiles, g = job
                 if job == (2, 2, 0):
                     store(0, False)
                     store(1, False)
-                    for late in by_scalar:
-                        v_mix(late, nc.scalar.copy, "v_late")
-                if job in waiting:
-                    if mixed < len(by_vector) and (job in by_vector or job == by_scalar[-1]):
-                        v_mix(by_vector[mixed])
-                        mixed = mixed + 1
-                    v_quant(job)
-                if m0 == 0 and g in hp_rest:
-                    quant(hp_codes[g], hp_sc[g], GP_COLS[g] - H, 2 * H - GP_COLS[g], hp_rest[g][:])
-                for m in range(m0, m0 + n):
-                    one_pass(m, v_codes, v_sc, hp_codes, hp_sc, g, False, g == G - 1)
+                    for late in scalar_jobs:
+                        v_interleave(late, False)
+                if job in to_make:
+                    if started < len(vector_jobs) and job not in scalar_jobs[:-1]:
+                        v_interleave(vector_jobs[started])
+                        started = started + 1
+                    v_quantise(job)
+                if m0 == 0:
+                    quantise(hp_mx, g, HP_GPSIMD, H - HP_GPSIMD, hp_rest[g][:])
+                for m in range(m0, m0 + tiles):
+                    correlate(m, v_mx, hp_mx, g, last=g == G - 1)
                 if job == (2, 2, G - 1):
                     store(2, False)
                     store(3, False)
-            for m in range(4, MT):
-                store(m, m in V_OUT, TAIL_PARTS if m >= 6 else 1)
+            for m in range(MT // 2, MT):
+                store(m, m % 2 == 1)

@@ -22,13 +22,17 @@ SLOTS = 4
 G = B // (P * SLOTS)
 MT = V // P
 HALF = V // 2
-PAIRS = G * MT // 2
-PAIRS_PER_GROUP = MT // 2
+QUAD = 4
+QUADS = G * MT // QUAD
 
-TURN_BANKS = 5
-HP_GPSIMD = 256
-HEAD_SLOTS_SCALAR = 3
-SCALAR_JOBS = 2
+
+H_REST = 96
+WARM = 6
+AHEAD = 2
+SCALAR_LIST = [(4, 2, 2), (6, 2, 1), (6, 2, 2)]
+V1_AFTER = (0, 2, 4)
+SCALAR_JOBS = 3
+WIDEN_PER_QUAD = [0, 0, 0, 0, 1, 0, 1, 0]
 
 
 def tile_persistentmeanfieldisingrbmgradient_w4_kernel(
@@ -47,29 +51,33 @@ def tile_persistentmeanfieldisingrbmgradient_w4_kernel(
             return ring.tile(shape, dtype, name=name, tag=tag, bufs=bufs, align_bytes=256)
 
         def mx_operand(name, width):
-            codes = [kept("%s_codes%d" % (name, g), [P, width], U32, 256) for g in range(G)]
-            scales = [kept("%s_scales%d" % (name, g), [P, width], U8, 256) for g in range(G)]
-            return codes, scales
+            codes = kept("%s_codes" % name, [P, G * width], U32, 256)
+            scales = kept("%s_scales" % name, [P, G * width], U8, 256)
+            groups = [slice(width * g, width * g + width) for g in range(G)]
+            return [codes[:, cols] for cols in groups], [scales[:, cols] for cols in groups]
 
         turns = {
-            "turn": ["bank%d" % i for i in range(TURN_BANKS)],
-            "field": ["bank%d" % i for i in range(TURN_BANKS, 8)],
+            "turn": ["bank%d" % i for i in range(QUAD)],
+            "field": ["bank%d" % i for i in range(QUAD, 2 * QUAD)],
         }
 
-        def next_bank(kind, shape, for_good=False):
+        def next_bank(kind, shape, for_good=False, dtype=F32):
             name = turns[kind][0]
             turns[kind].remove(name)
             if not for_good:
                 turns[kind].append(name)
-            return psum.tile(shape, F32, name=name, tag=name)
+            return psum.tile(shape, dtype, name=name, tag=name)
 
         hf_rows = [reused("hf_rows%d" % g, [P, SLOTS, H], BF16, "rows%d" % g) for g in range(G)]
-        hn_rows = [kept("hn_rows%d" % g, [P, SLOTS, H], BF16) for g in range(G)]
-        hp_rows = [kept("hp_rows%d" % g, [P, SLOTS, H], BF16) for g in range(G)]
-        hp_rest = [kept("hp_rest%d" % g, [P, SLOTS * (H - HP_GPSIMD)], BF16) for g in range(G)]
-        v_rows = {g: kept("v_rows%d" % g, [P, SLOTS, V], U8) for g in range(1, G)}
-        v_rows_first = [kept("v_rows_first%d" % half, [P, SLOTS, HALF], U8) for half in range(2)]
-        v_wide = {(0, g): kept("v_wide0_%d" % g, [P, SLOTS, HALF], BF16) for g in range(G)}
+        h_rows = [kept("h_rows%d" % g, [P, 2, SLOTS, H], BF16) for g in range(G)]
+        h_staged = kept("h_staged", [P, SLOTS * (2 * H + (G - 1) * (H + H_REST))], BF16, 256)
+        v_rows = {g: kept("v_rows%d" % g, [P, SLOTS, V], U8) for g in range(2, G)}
+        v_rows_second = [kept("v_rows_second%d" % half, [P, SLOTS, HALF], U8) for half in range(2)]
+        v_rows_first = [kept("v_rows_first%d" % pair, [P, 2, V], U8) for pair in range(2)]
+        v_wide_first = kept("v_wide_first", [P, SLOTS, V], BF16)
+        v_wide = {(0, g): kept("v_wide0_%d" % g, [P, SLOTS, HALF], BF16) for g in range(1, G)}
+        for half in range(2):
+            v_wide[(half, 0)] = v_wide_first[:, :, HALF * half : HALF * half + HALF]
         hf_mx = mx_operand("hf", P * SLOTS)
         hn_mx = mx_operand("hn", H)
         hp_mx = mx_operand("hp", H)
@@ -80,9 +88,8 @@ def tile_persistentmeanfieldisingrbmgradient_w4_kernel(
         ident = kept("ident", [P, P], F32)
         b_rows = kept("b_rows", [P, P], BF16)
         b_rows32 = kept("b_rows32", [P, P], F32)
-        bias = kept("bias", [P, MT], F32)
+        bias_neg = kept("bias_neg", [P, MT], F32)
         s_rows = kept("s_rows", [P, G, SLOTS], BF16)
-        s_neg = kept("s_neg", [P, G, SLOTS], F32)
         scale_later = kept("scale_later", [P, G - 1, SLOTS], F32)
         scale_first = kept("scale_first", [P, SLOTS], F32)
         zeros = kept("zeros", [P, 512], BF16)
@@ -104,36 +111,47 @@ def tile_persistentmeanfieldisingrbmgradient_w4_kernel(
             def load(tiles, x, g):
                 nc.sync.dma_start(out=tiles[g][:], in_=group_rows(x, g))
 
+            def load_h(g):
+                nc.sync.dma_start(out=h_rows[g][:, 0], in_=group_rows(hn, g))
+                nc.sync.dma_start(out=h_rows[g][:, 1], in_=group_rows(hp, g))
+
             def load_hf_slots(g, pair):
                 slots = slice(2 * pair, 2 * pair + 2)
                 nc.sync.dma_start(out=hf_rows[g][:, slots, :], in_=group_rows(hf, g)[:, slots, :])
 
-            def load_v_first(half):
+            def load_v_first(pair):
+                nc.sync.dma_start(out=v_rows_first[pair][:], in_=group_rows(v_bytes, 0)[:, 2 * pair : 2 * pair + 2, :])
+
+            def load_v_second(half):
                 cols = slice(HALF * half, HALF * half + HALF)
-                nc.sync.dma_start(out=v_rows_first[half][:], in_=group_rows(v_bytes, 0)[:, :, cols])
+                nc.sync.dma_start(out=v_rows_second[half][:], in_=group_rows(v_bytes, 1)[:, :, cols])
 
             load_v_first(0)
+            load_v_first(1)
             load_hf_slots(0, 0)
             load_hf_slots(0, 1)
             nc.sync.dma_start(out=b_rows[0:MT, :], in_=b.rearrange("(m c) -> m c", c=P))
-            load_v_first(1)
-            load_hf_slots(1, 0)
             nc.sync.dma_start(out=w_codes[:], in_=w_words[0])
             for q in range(4):
                 nc.sync.dma_start(
                     out=w_plane[32 * q : 32 * q + 4, :].bitcast(I32),
                     in_=w_scales[0][4 * q : 4 * q + 4, :].bitcast(I32),
                 )
+            load_hf_slots(1, 0)
             load_hf_slots(1, 1)
-            nc.sync.dma_start(out=s_rows[:], in_=s.rearrange("(g p t) -> p g t", p=P, t=SLOTS))
             nc.sync.dma_start(out=scale_later[:], in_=scale_view[:, 1:G, :])
-            for g in range(G):
-                load(hn_rows, hn, g)
-                if g + 2 < G:
-                    load(hf_rows, hf, g + 2)
+            load_v_second(0)
+            nc.sync.dma_start(out=s_rows[:], in_=s.rearrange("(g p t) -> p g t", p=P, t=SLOTS))
+            nc.sync.dma_start(out=h_rows[0][:, 0], in_=group_rows(hn, 0))
+            load_hf_slots(2, 0)
+            nc.sync.dma_start(out=h_rows[0][:, 1], in_=group_rows(hp, 0))
+            load_hf_slots(2, 1)
+            load(hf_rows, hf, 3)
+            load_v_second(1)
+            for g in range(1, G):
+                load_h(g)
                 if g + 1 < G:
                     load(v_rows, v_bytes, g + 1)
-                load(hp_rows, hp, g)
 
             def quantise(operand, g, col, width, src):
                 codes, scales = operand
@@ -146,22 +164,17 @@ def tile_persistentmeanfieldisingrbmgradient_w4_kernel(
             def staging(name, number):
                 return reused(name, [P, SLOTS * 512], BF16, "staging%d" % number)
 
-            def gpsimd_buffer(name):
-                return reused(name, [P, SLOTS * (H + HP_GPSIMD)], BF16, "gpsimd_buffer")
+            def h_place(g, first, last):
+                base = SLOTS * (H + H_REST) * (G - 1 - g)
+                return h_staged[:, base + SLOTS * first : base + SLOTS * last]
 
             hf_staged = {}
             hf_bank = {}
 
-            def on_field_bank(g):
-                return g == G - 1
-
-            def hf_turn(g, pair):
+            def hf_turn(g, pair, kind):
                 if pair == 0:
-                    if g == 1:
-                        hf_staged[g] = gpsimd_buffer("hf_staged1")
-                    else:
-                        hf_staged[g] = staging("hf_staged%d" % g, g % 3)
-                bank = next_bank("field" if on_field_bank(g) else "turn", [P, 2, P, 2])
+                    hf_staged[g] = staging("hf_staged%d" % g, (0, 3, 2, 0)[g])
+                bank = next_bank(kind, [P, 2, P, 2])
                 hf_bank[(g, pair)] = bank
                 words = hf_rows[g][:].rearrange("p t k -> p (t k)").bitcast(F32)
                 for i in range(2):
@@ -203,7 +216,8 @@ def tile_persistentmeanfieldisingrbmgradient_w4_kernel(
                     tanh_tile[unit][:].rearrange("p t r -> p (t r)"),
                     field_bank[unit][:],
                     ACT.Tanh,
-                    bias=bias[:, m : m + 1],
+                    bias=bias_neg[:, m : m + 1],
+                    scale=-1.0,
                 )
 
             def turn(unit):
@@ -212,9 +226,9 @@ def tile_persistentmeanfieldisingrbmgradient_w4_kernel(
                     nc.tensor.transpose(turned_bank[unit][:, t, :], tanh_tile[unit][:, t, :], ident[:])
 
             def v1_buffer(g, half):
-                if g == G - 1:
-                    return (2 + half) % 3
-                return 3 + g if half else 1
+                if half:
+                    return (3 + g) % 6
+                return 1 + g % 2
 
             def weight(unit):
                 g, m = divmod(unit, MT)
@@ -224,7 +238,7 @@ def tile_persistentmeanfieldisingrbmgradient_w4_kernel(
                 nc.vector.tensor_tensor(
                     out=v1_staged[(g, half)][:, 512 * c : 512 * c + 512].rearrange("p (c t) -> p c t", t=SLOTS),
                     in0=turned_bank[unit][:].rearrange("p t c -> p c t"),
-                    in1=s_neg[:, g, :].unsqueeze(1).to_broadcast([P, P, SLOTS]),
+                    in1=s_rows[:, g, :].unsqueeze(1).to_broadcast([P, P, SLOTS]),
                     op=ALU.mult,
                 )
 
@@ -238,46 +252,55 @@ def tile_persistentmeanfieldisingrbmgradient_w4_kernel(
                 )
 
             def gpsimd_share(g):
-                staged = gpsimd_buffer("h_staged%d" % g)
-                parts = (
-                    (staged[:, 0 : SLOTS * H], hn_rows[g][:]),
-                    (staged[:, SLOTS * H :], hp_rows[g][:, :, 0:HP_GPSIMD]),
+                nc.gpsimd.tensor_scalar(
+                    out=h_place(g, 0, 2 * H).rearrange("p (a c t) -> p a c t", a=2, t=SLOTS)[:, :, H_REST:, :],
+                    in0=h_rows[g][:, :, :, H_REST:].rearrange("p a t c -> p a c t"),
+                    scalar1=1.0,
+                    scalar2=0.0,
+                    op0=ALU.mult,
+                    op1=ALU.add,
                 )
-                for dst, src in parts:
-                    nc.gpsimd.tensor_scalar(
-                        out=dst.rearrange("p (c t) -> p c t", t=SLOTS),
-                        in0=src.rearrange("p t c -> p c t"),
-                        scalar1=1.0,
-                        scalar2=0.0,
-                        op0=ALU.mult,
-                        op1=ALU.add,
-                    )
-                return staged
+
+            def h_rest(g, copy):
+                dst = h_place(g, 0, 2 * H).rearrange("p (a c i t) -> p a c t i", a=2, i=4, t=SLOTS)
+                copy(
+                    out=dst[:, :, : H_REST // 4],
+                    in_=h_rows[g][:, :, :, :H_REST].rearrange("p a t (c i) -> p a c t i", i=4),
+                )
+
+            def hp_quantise(g):
+                quantise(hp_mx, g, 0, H, h_place(g, H, 2 * H))
+
+            def widen_columns(dst, src, scale, on_vector):
+                if on_vector:
+                    nc.vector.tensor_scalar(out=dst, in0=src.bitcast(E4M3), scalar1=scale, scalar2=None, op0=ALU.mult)
+                else:
+                    nc.scalar.activation(dst, src.bitcast(E4M3), ACT.Copy, scale=scale)
+
+            def widen_first(t, cols, on_vector):
+                src = v_rows_first[t // 2][:, t % 2, cols]
+                widen_columns(v_wide_first[:, t, cols], src, scale_first[:, t : t + 1], on_vector)
 
             def widen(half, g, t, on_vector):
                 if (half, g) not in v_wide:
                     v_wide[(half, g)] = reused("v_wide1_%d" % g, [P, SLOTS, HALF], BF16, "rows%d" % g)
-                dst = v_wide[(half, g)][:, t, :]
-                if g == 0:
-                    src = v_rows_first[half][:, t, :].bitcast(E4M3)
-                    scale = scale_first[:, t : t + 1]
+                if g == 1:
+                    src = v_rows_second[half][:, t, :]
                 else:
-                    src = v_rows[g][:, t, HALF * half : HALF * half + HALF].bitcast(E4M3)
-                    scale = scale_later[:, g - 1, t : t + 1]
-                if on_vector:
-                    nc.vector.tensor_scalar(out=dst, in0=src, scalar1=scale, scalar2=None, op0=ALU.mult)
-                else:
-                    nc.scalar.activation(dst, src, ACT.Copy, scale=scale)
+                    src = v_rows[g][:, t, HALF * half : HALF * half + HALF]
+                widen_columns(v_wide[(half, g)][:, t, :], src, scale_later[:, g - 1, t : t + 1], on_vector)
 
             v_staged = {}
 
             def v_interleave(job, on_vector=True):
                 m0, tiles, g = job
                 name = "v_staged%d_%d" % (m0, g)
-                if on_vector:
-                    v_staged[job] = reused(name, [P, 512 * tiles], BF16, "v_staged", 4)
+                if job == (2, 2, 0):
+                    v_staged[job] = h_place(0, 2 * P, 4 * P)
+                elif on_vector:
+                    v_staged[job] = reused(name, [P, 512 * tiles], BF16, "v_staged", 5)
                 else:
-                    v_staged[job] = reused(name, [P, 512 * tiles], BF16, "v_staged_scalar", SCALAR_JOBS)
+                    v_staged[job] = staging(name, 1 + SCALAR_LIST.index(job))[:, 0 : 512 * tiles]
                 half, first = divmod(P * m0, HALF)
                 interleave(
                     nc.vector.tensor_copy if on_vector else nc.scalar.copy,
@@ -325,135 +348,135 @@ def tile_persistentmeanfieldisingrbmgradient_w4_kernel(
             def warm_up():
                 nc.tensor.matmul(warm_bank[:], lhsT=zeros[:, 0:P], rhs=zeros[:], start=True, stop=True)
 
-            for i in range(4):
+            for i in range(WARM):
                 warm_up()
-            widen(0, 0, 0, False)
-            for t in range(1, SLOTS):
-                widen(0, 0, t, True)
+            widen_first(0, slice(0, V), False)
+            widen_first(1, slice(0, V), True)
+            widen_first(2, slice(HALF, V), True)
+            widen_first(3, slice(HALF, V), True)
+            widen_first(2, slice(0, HALF), True)
+            widen_first(3, slice(0, HALF), False)
             for pair in range(2):
-                hf_turn(0, pair)
-                warm_up()
-            v_interleave((0, 2, 0))
-            v_interleave((2, 2, 0))
-            hf_copy_out(0, 0, nc.scalar.copy)
+                hf_turn(0, pair, "turn")
+            v_interleave((4, 2, 0))
             nc.vector.tensor_copy(out=b_rows32[:], in_=b_rows[:])
-            quantise(hf_mx, 0, 0, 256, hf_staged[0][:, 0:1024])
-            hf_copy_out(0, 1, nc.scalar.copy)
             bias_bank = next_bank("turn", [P, P])
             nc.tensor.transpose(bias_bank[:], b_rows32[:], ident[:])
-            v_quantise((0, 2, 0))
-            quantise(hf_mx, 0, 256, 256, hf_staged[0][:, 1024:2048])
-            nc.vector.tensor_copy(out=bias[:], in_=bias_bank[:, 0:MT])
-            v_quantise((2, 2, 0))
-            hf_turn(1, 0)
             warm_up()
-            for t in range(HEAD_SLOTS_SCALAR):
-                widen(1, 0, t, False)
-            hf_copy_out(1, 0, nc.vector.tensor_copy)
-            for unit in range(3):
-                field(unit)
-            hf_turn(1, 1)
-            tanh(0)
-            field(3)
-            tanh(1)
-            nc.vector.tensor_scalar(out=s_neg[:], in0=s_rows[:], scalar1=-1.0, scalar2=None, op0=ALU.mult)
-            for t in range(HEAD_SLOTS_SCALAR, SLOTS):
-                widen(1, 0, t, True)
-            v_interleave((4, 2, 0))
-            hf_copy_out(1, 1, nc.vector.tensor_copy)
+            warm_up()
+            v_interleave((6, 2, 0))
+            hf_copy_out(0, 0, nc.scalar.copy)
+            hf_copy_out(0, 1, nc.scalar.copy)
+            quantise(hf_mx, 0, 0, 256, hf_staged[0][:, 0:1024])
             v_quantise((4, 2, 0))
+            nc.vector.tensor_scalar(out=bias_neg[:], in0=bias_bank[:, 0:MT], scalar1=-1.0, scalar2=None, op0=ALU.mult)
+            quantise(hf_mx, 0, 256, 256, hf_staged[0][:, 1024:2048])
+            v_interleave((0, 2, 0))
+            v_interleave((2, 2, 0))
+            hf_turn(1, 0, "turn")
+            hf_copy_out(1, 0, nc.scalar.copy)
+            for unit in range(QUAD):
+                field(unit)
+            hf_turn(1, 1, "turn")
+            for m0 in (6, 0):
+                v_quantise((m0, 2, 0))
+            for unit in range(2):
+                tanh(unit)
+                field(unit + QUAD)
+            hf_copy_out(1, 1, nc.scalar.copy)
+            for t in range(SLOTS):
+                widen(0, 1, t, True)
+            quantise(hf_mx, 1, 0, 512, hf_staged[1][:])
+            v_interleave((0, 2, 1))
+            v_quantise((2, 2, 0))
+            h_rest(0, nc.vector.tensor_copy)
 
-            first_halves = [(0, g, t) for g in range(1, G) for t in range(SLOTS)]
-            widened = 0
-            for j in range(PAIRS):
-                g, step = divmod(j, PAIRS_PER_GROUP)
-                hf_next = g + 2 if step in (1, 2) and g + 2 < G else None
-                by_scalar = hf_next is not None and on_field_bank(hf_next)
-                turn(2 * j)
-                turn(2 * j + 1)
-                if j + 1 < PAIRS:
-                    tanh(2 * j + 2)
-                if hf_next:
-                    hf_turn(hf_next, step - 1)
-                if j + 1 < PAIRS:
-                    tanh(2 * j + 3)
-                if by_scalar:
-                    hf_copy_out(hf_next, step - 1, nc.scalar.copy)
-                if j + 2 < PAIRS:
-                    field(2 * j + 4)
-                    field(2 * j + 5)
-                if j + 2 == PAIRS:
-                    open_with_early_groups("field")
-                if j + 1 == PAIRS:
-                    open_with_early_groups("field")
-                    open_with_early_groups("field")
-                if step > 0 and not by_scalar:
-                    widen(*first_halves[widened], False)
-                    widened = widened + 1
-                if step == 0 and g > 0:
-                    h_staged = gpsimd_share(g)
-                weight(2 * j)
-                weight(2 * j + 1)
-                if hf_next and not by_scalar:
-                    hf_copy_out(hf_next, step - 1, nc.vector.tensor_copy)
-                if j == 0:
-                    quantise(hf_mx, 1, 0, 512, hf_staged[1][:, 0:2048])
-                    h_staged = gpsimd_share(0)
-                if step == PAIRS_PER_GROUP - 1:
-                    if g + 2 < G:
-                        quantise(hf_mx, g + 2, 0, 512, hf_staged[g + 2][:])
-                    if g == G - 1:
-                        v1_quantise(0, 1)
-                    v1_quantise(g, 0)
-                    quantise(hp_mx, g, 0, HP_GPSIMD, h_staged[:, SLOTS * H :])
-                    quantise(hn_mx, g, 0, H, h_staged[:, 0 : SLOTS * H])
+            to_widen = [(half, g, t) for half in range(2) for g in range(1, G) for t in range(SLOTS)]
+            widened = [SLOTS]
 
-            for g in range(1, G):
-                v1_quantise(g, 1)
-            open_with_early_groups("turn")
+            def widen_some(count):
+                for item in to_widen[widened[0] : widened[0] + count]:
+                    widen(*item, False)
+                widened.append(widened.pop() + count)
+
+            def stretch(g):
+                if g + 2 < G:
+                    quantise(hf_mx, g + 2, 0, 512, hf_staged[g + 2][:])
+                    if g == 0:
+                        h_rest(1, nc.vector.tensor_copy)
+                elif g == G - 1:
+                    v1_quantise(0, 1)
+                quantise(hn_mx, g, 0, H, h_place(g, 0, H))
+                v1_quantise(g, 0)
+
+            units = G * MT
+            for q in range(QUADS):
+                g, second = divmod(q, 2)
+                first = QUAD * q
+                if not second:
+                    gpsimd_share(g)
+                for unit in range(first + 2, min(first + 6, units)):
+                    tanh(unit)
+                for unit in range(first, first + QUAD):
+                    turn(unit)
+                    if g + 2 < G and unit == first + 1:
+                        hf_turn(g + 2, second, "field")
+                if g + 2 < G:
+                    hf_copy_out(g + 2, second, nc.scalar.copy)
+                if second and g + 2 >= G:
+                    h_rest(g, nc.scalar.copy)
+                widen_some(WIDEN_PER_QUAD[q])
+                for unit in range(first + 6, first + 10):
+                    if unit < units:
+                        field(unit)
+                    elif unit == units:
+                        open_with_early_groups("field")
+                if q == QUADS - 1:
+                    for m in range(1, MT // 2):
+                        open_with_early_groups("field")
+                for unit in range(first, first + QUAD):
+                    weight(unit)
+                if second:
+                    stretch(g)
+
+            hp_quantise(0)
             for m in range(MT // 2, MT):
                 open_acc("turn")
                 correlate(m, v1_mx, hn_mx, 0, first=True)
             for m in range(MT // 2):
                 correlate(m, v1_mx, hn_mx, G - 1)
-            for g in range(1, G):
-                for m in range(MT // 2, MT):
-                    correlate(m, v1_mx, hn_mx, g)
+            for m in range(MT):
+                correlate(m, v_mx, hp_mx, 0)
 
-            jobs = [(m0, 2, g) for m0 in range(0, MT, 2) for g in range(G)]
-            jobs = jobs[:-1] + [(MT - 2, 1, G - 1), (MT - 1, 1, G - 1)]
-            to_make = [job for job in jobs if job not in v_staged]
-            scalar_jobs = to_make[-2 - SCALAR_JOBS : -2]
-            vector_jobs = [job for job in to_make if job not in scalar_jobs]
+            jobs = [(m0, 2, g) for m0 in range(0, MT, 2) for g in range(1, G)]
+            scalar_jobs = SCALAR_LIST
+            widen_some(len(to_widen))
 
-            for item in first_halves[widened:]:
-                widen(*item, False)
-            for g in range(G):
-                interleave(nc.scalar.copy, hp_rest[g][:], hp_rows[g][:, :, HP_GPSIMD:H])
-            for g in range(1, G):
-                for t in range(SLOTS):
-                    widen(1, g, t, False)
-
-            v_interleave(vector_jobs[0])
-            started = 1
-            for job in jobs:
+            for index, job in enumerate(jobs):
                 m0, tiles, g = job
-                if job == (2, 2, 0):
-                    store(0, False)
-                    store(1, False)
-                    for late in scalar_jobs:
-                        v_interleave(late, False)
-                if job in to_make:
-                    if started < len(vector_jobs) and job not in scalar_jobs[:-1]:
-                        v_interleave(vector_jobs[started])
-                        started = started + 1
-                    v_quantise(job)
                 if m0 == 0:
-                    quantise(hp_mx, g, HP_GPSIMD, H - HP_GPSIMD, hp_rest[g][:])
-                for m in range(m0, m0 + tiles):
+                    hp_quantise(g)
+                later = [
+                    other for other in jobs[index + 1 : index + 1 + AHEAD] if other not in v_staged and other not in scalar_jobs
+                ]
+                if later:
+                    v_interleave(later[0])
+                v_quantise(job)
+                for m in range(m0, min(m0 + tiles, MT - 1)):
                     correlate(m, v_mx, hp_mx, g, last=g == G - 1)
-                if job == (2, 2, G - 1):
-                    store(2, False)
-                    store(3, False)
-            for m in range(MT // 2, MT):
-                store(m, m % 2 == 1)
+                if index in V1_AFTER:
+                    late = V1_AFTER.index(index) + 1
+                    v1_quantise(late, 1)
+                    for m in range(MT // 2, MT):
+                        correlate(m, v1_mx, hn_mx, late)
+                if g == G - 1:
+                    store(m0, False)
+                    if m0 < MT - 4:
+                        store(m0 + 1, False)
+                    if m0 == 0:
+                        for late in scalar_jobs:
+                            v_interleave(late, False)
+            store(MT - 3, True)
+            for g in range(1, G):
+                correlate(MT - 1, v_mx, hp_mx, g, last=g == G - 1)
+            store(MT - 1, True)

@@ -88,7 +88,8 @@ def tile_persistentmeanfieldisingrbmgradient_w4_kernel(
         ident = kept("ident", [P, P], F32)
         b_rows = kept("b_rows", [P, P], BF16)
         b_rows32 = kept("b_rows32", [P, P], F32)
-        bias_neg = kept("bias_neg", [P, MT], F32)
+        bias = kept("bias", [P, MT], F32)
+        s_neg = kept("s_neg", [P, G, SLOTS], F32)
         s_rows = kept("s_rows", [P, G, SLOTS], BF16)
         scale_later = kept("scale_later", [P, G - 1, SLOTS], F32)
         scale_first = kept("scale_first", [P, SLOTS], F32)
@@ -146,12 +147,12 @@ def tile_persistentmeanfieldisingrbmgradient_w4_kernel(
             load_hf_slots(2, 0)
             nc.sync.dma_start(out=h_rows[0][:, 1], in_=group_rows(hp, 0))
             load_hf_slots(2, 1)
+            load_h(1)
             load(hf_rows, hf, 3)
             load_v_second(1)
-            for g in range(1, G):
+            for g in range(2, G):
+                load(v_rows, v_bytes, g)
                 load_h(g)
-                if g + 1 < G:
-                    load(v_rows, v_bytes, g + 1)
 
             def quantise(operand, g, col, width, src):
                 codes, scales = operand
@@ -216,8 +217,7 @@ def tile_persistentmeanfieldisingrbmgradient_w4_kernel(
                     tanh_tile[unit][:].rearrange("p t r -> p (t r)"),
                     field_bank[unit][:],
                     ACT.Tanh,
-                    bias=bias_neg[:, m : m + 1],
-                    scale=-1.0,
+                    bias=bias[:, m : m + 1],
                 )
 
             def turn(unit):
@@ -238,7 +238,7 @@ def tile_persistentmeanfieldisingrbmgradient_w4_kernel(
                 nc.vector.tensor_tensor(
                     out=v1_staged[(g, half)][:, 512 * c : 512 * c + 512].rearrange("p (c t) -> p c t", t=SLOTS),
                     in0=turned_bank[unit][:].rearrange("p t c -> p c t"),
-                    in1=s_rows[:, g, :].unsqueeze(1).to_broadcast([P, P, SLOTS]),
+                    in1=s_neg[:, g, :].unsqueeze(1).to_broadcast([P, P, SLOTS]),
                     op=ALU.mult,
                 )
 
@@ -369,7 +369,7 @@ def tile_persistentmeanfieldisingrbmgradient_w4_kernel(
             hf_copy_out(0, 1, nc.scalar.copy)
             quantise(hf_mx, 0, 0, 256, hf_staged[0][:, 0:1024])
             v_quantise((4, 2, 0))
-            nc.vector.tensor_scalar(out=bias_neg[:], in0=bias_bank[:, 0:MT], scalar1=-1.0, scalar2=None, op0=ALU.mult)
+            nc.vector.tensor_copy(out=bias[:], in_=bias_bank[:, 0:MT])
             quantise(hf_mx, 0, 256, 256, hf_staged[0][:, 1024:2048])
             v_interleave((0, 2, 0))
             v_interleave((2, 2, 0))
@@ -387,9 +387,9 @@ def tile_persistentmeanfieldisingrbmgradient_w4_kernel(
             for t in range(SLOTS):
                 widen(0, 1, t, True)
             quantise(hf_mx, 1, 0, 512, hf_staged[1][:])
-            v_interleave((0, 2, 1))
+            nc.vector.tensor_scalar(out=s_neg[:], in0=s_rows[:], scalar1=-1.0, scalar2=None, op0=ALU.mult)
             v_quantise((2, 2, 0))
-            h_rest(0, nc.vector.tensor_copy)
+            v_interleave((0, 2, 1))
 
             to_widen = [(half, g, t) for half in range(2) for g in range(1, G) for t in range(SLOTS)]
             widened = [SLOTS]
@@ -401,6 +401,8 @@ def tile_persistentmeanfieldisingrbmgradient_w4_kernel(
 
             def stretch(g):
                 if g + 2 < G:
+                    if g == 0:
+                        h_rest(0, nc.vector.tensor_copy)
                     quantise(hf_mx, g + 2, 0, 512, hf_staged[g + 2][:])
                     if g == 0:
                         h_rest(1, nc.vector.tensor_copy)
@@ -469,6 +471,8 @@ def tile_persistentmeanfieldisingrbmgradient_w4_kernel(
                     v1_quantise(late, 1)
                     for m in range(MT // 2, MT):
                         correlate(m, v1_mx, hn_mx, late)
+                if job == jobs[-1]:
+                    store(MT - 3, True)
                 if g == G - 1:
                     store(m0, False)
                     if m0 < MT - 4:
@@ -476,7 +480,6 @@ def tile_persistentmeanfieldisingrbmgradient_w4_kernel(
                     if m0 == 0:
                         for late in scalar_jobs:
                             v_interleave(late, False)
-            store(MT - 3, True)
             for g in range(1, G):
                 correlate(MT - 1, v_mx, hp_mx, g, last=g == G - 1)
             store(MT - 1, True)

@@ -68,16 +68,14 @@ def tile_persistentmeanfieldisingrbmgradient_w4_kernel(
                 turns[kind].append(name)
             return psum.tile(shape, dtype, name=name, tag=name)
 
-        hf_rows = [reused("hf_rows%d" % g, [P, SLOTS, H], BF16, "rows%d" % g) for g in range(G)]
-        h_rows = [kept("h_rows%d" % g, [P, 2, SLOTS, H], BF16) for g in range(G)]
-        h_staged = kept("h_staged", [P, SLOTS * (2 * H + (G - 1) * (H + H_REST))], BF16, 256)
+        hf_rows = [reused("hf_rows%d" % g, [P, SLOTS * H], BF16, "rows%d" % g) for g in range(G)]
+        h_rows = [kept("h_rows%d" % g, [P, 2 * SLOTS * H + H_REST], BF16) for g in range(G)]
+        h_staged = kept("h_staged", [P, SLOTS * (G + 1) * H], BF16, 256)
         v_rows = {g: kept("v_rows%d" % g, [P, SLOTS, V], U8) for g in range(2, G)}
         v_rows_second = [kept("v_rows_second%d" % half, [P, SLOTS, HALF], U8) for half in range(2)]
         v_rows_first = [kept("v_rows_first%d" % pair, [P, 2, V], U8) for pair in range(2)]
-        v_wide_first = kept("v_wide_first", [P, SLOTS, V], BF16)
-        v_wide = {(0, g): kept("v_wide0_%d" % g, [P, SLOTS, HALF], BF16) for g in range(1, G)}
-        for half in range(2):
-            v_wide[(half, 0)] = v_wide_first[:, :, HALF * half : HALF * half + HALF]
+        v_wide = {(0, g): kept("v_wide0_%d" % g, [P, SLOTS, HALF], BF16) for g in range(G)}
+        v_wide[(1, 0)] = kept("v_wide1_0", [P, SLOTS, HALF], BF16)
         hf_mx = mx_operand("hf", P * SLOTS)
         hn_mx = mx_operand("hn", H)
         hp_mx = mx_operand("hp", H)
@@ -112,13 +110,22 @@ def tile_persistentmeanfieldisingrbmgradient_w4_kernel(
             def load(tiles, x, g):
                 nc.sync.dma_start(out=tiles[g][:], in_=group_rows(x, g))
 
-            def load_h(g):
-                nc.sync.dma_start(out=h_rows[g][:, 0], in_=group_rows(hn, g))
-                nc.sync.dma_start(out=h_rows[g][:, 1], in_=group_rows(hp, g))
+            def h_source(g, a):
+                first = (SLOTS * H + H_REST) * a
+                return h_rows[g][:, first : first + SLOTS * H]
 
-            def load_hf_slots(g, pair):
-                slots = slice(2 * pair, 2 * pair + 2)
-                nc.sync.dma_start(out=hf_rows[g][:, slots, :], in_=group_rows(hf, g)[:, slots, :])
+            def load_h_part(g, a):
+                nc.sync.dma_start(out=h_source(g, a), in_=group_rows((hn, hp)[a], g).rearrange("p t c -> p (t c)"))
+
+            def load_h(g):
+                load_h_part(g, 0)
+                load_h_part(g, 1)
+
+            def load_hf_slots(g, first, count):
+                nc.sync.dma_start(
+                    out=hf_rows[g][:, H * first : H * (first + count)],
+                    in_=group_rows(hf, g)[:, first : first + count, :].rearrange("p t c -> p (t c)"),
+                )
 
             def load_v_first(pair):
                 nc.sync.dma_start(out=v_rows_first[pair][:], in_=group_rows(v_bytes, 0)[:, 2 * pair : 2 * pair + 2, :])
@@ -129,8 +136,8 @@ def tile_persistentmeanfieldisingrbmgradient_w4_kernel(
 
             load_v_first(0)
             load_v_first(1)
-            load_hf_slots(0, 0)
-            load_hf_slots(0, 1)
+            load_hf_slots(0, 0, 2)
+            load_hf_slots(0, 2, 2)
             nc.sync.dma_start(out=b_rows[0:MT, :], in_=b.rearrange("(m c) -> m c", c=P))
             nc.sync.dma_start(out=w_codes[:], in_=w_words[0])
             for q in range(4):
@@ -138,17 +145,17 @@ def tile_persistentmeanfieldisingrbmgradient_w4_kernel(
                     out=w_plane[32 * q : 32 * q + 4, :].bitcast(I32),
                     in_=w_scales[0][4 * q : 4 * q + 4, :].bitcast(I32),
                 )
-            load_hf_slots(1, 0)
-            load_hf_slots(1, 1)
+            load_hf_slots(1, 0, 2)
+            load_hf_slots(1, 2, 2)
             nc.sync.dma_start(out=scale_later[:], in_=scale_view[:, 1:G, :])
             load_v_second(0)
             nc.sync.dma_start(out=s_rows[:], in_=s.rearrange("(g p t) -> p g t", p=P, t=SLOTS))
-            nc.sync.dma_start(out=h_rows[0][:, 0], in_=group_rows(hn, 0))
-            load_hf_slots(2, 0)
-            nc.sync.dma_start(out=h_rows[0][:, 1], in_=group_rows(hp, 0))
-            load_hf_slots(2, 1)
+            load_h_part(0, 0)
+            load_hf_slots(2, 0, 2)
+            load_h_part(0, 1)
+            load_hf_slots(2, 2, 2)
             load_h(1)
-            load(hf_rows, hf, 3)
+            load_hf_slots(3, 0, SLOTS)
             load_v_second(1)
             for g in range(2, G):
                 load(v_rows, v_bytes, g)
@@ -166,7 +173,7 @@ def tile_persistentmeanfieldisingrbmgradient_w4_kernel(
                 return reused(name, [P, SLOTS * 512], BF16, "staging%d" % number)
 
             def h_place(g, first, last):
-                base = SLOTS * (H + H_REST) * (G - 1 - g)
+                base = SLOTS * H * (G - 1 - g)
                 return h_staged[:, base + SLOTS * first : base + SLOTS * last]
 
             hf_staged = {}
@@ -177,7 +184,7 @@ def tile_persistentmeanfieldisingrbmgradient_w4_kernel(
                     hf_staged[g] = staging("hf_staged%d" % g, (0, 3, 2, 0)[g])
                 bank = next_bank(kind, [P, 2, P, 2])
                 hf_bank[(g, pair)] = bank
-                words = hf_rows[g][:].rearrange("p t k -> p (t k)").bitcast(F32)
+                words = hf_rows[g][:].bitcast(F32)
                 for i in range(2):
                     first = H // 2 * (2 * pair + i)
                     for u in range(2):
@@ -252,21 +259,20 @@ def tile_persistentmeanfieldisingrbmgradient_w4_kernel(
                 )
 
             def gpsimd_share(g):
+                rows = h_rows[g][:, 0 : 2 * SLOTS * H].rearrange("p (a t c) -> p a c t", a=2, t=SLOTS)
                 nc.gpsimd.tensor_scalar(
-                    out=h_place(g, 0, 2 * H).rearrange("p (a c t) -> p a c t", a=2, t=SLOTS)[:, :, H_REST:, :],
-                    in0=h_rows[g][:, :, :, H_REST:].rearrange("p a t c -> p a c t"),
+                    out=h_place(g, H_REST, 2 * H - H_REST).rearrange("p (a c t) -> p a c t", a=2, t=SLOTS),
+                    in0=rows[:, :, H_REST:, :],
                     scalar1=1.0,
                     scalar2=0.0,
                     op0=ALU.mult,
                     op1=ALU.add,
                 )
 
-            def h_rest(g, copy):
-                dst = h_place(g, 0, 2 * H).rearrange("p (a c i t) -> p a c t i", a=2, i=4, t=SLOTS)
-                copy(
-                    out=dst[:, :, : H_REST // 4],
-                    in_=h_rows[g][:, :, :, :H_REST].rearrange("p a t (c i) -> p a c t i", i=4),
-                )
+            def h_rest(g, a, copy):
+                first = (H - H_REST) * a
+                rows = h_source(g, a).rearrange("p (t c) -> p t c", t=SLOTS)
+                interleave(copy, h_place(g, H * a + first, H * a + first + H_REST), rows[:, :, first : first + H_REST])
 
             def hp_quantise(g):
                 quantise(hp_mx, g, 0, H, h_place(g, H, 2 * H))
@@ -277,9 +283,9 @@ def tile_persistentmeanfieldisingrbmgradient_w4_kernel(
                 else:
                     nc.scalar.activation(dst, src.bitcast(E4M3), ACT.Copy, scale=scale)
 
-            def widen_first(t, cols, on_vector):
-                src = v_rows_first[t // 2][:, t % 2, cols]
-                widen_columns(v_wide_first[:, t, cols], src, scale_first[:, t : t + 1], on_vector)
+            def widen_first(t, half, on_vector):
+                src = v_rows_first[t // 2][:, t % 2, HALF * half : HALF * half + HALF]
+                widen_columns(v_wide[(half, 0)][:, t, :], src, scale_first[:, t : t + 1], on_vector)
 
             def widen(half, g, t, on_vector):
                 if (half, g) not in v_wide:
@@ -350,12 +356,14 @@ def tile_persistentmeanfieldisingrbmgradient_w4_kernel(
 
             for i in range(WARM):
                 warm_up()
-            widen_first(0, slice(0, V), False)
-            widen_first(1, slice(0, V), True)
-            widen_first(2, slice(HALF, V), True)
-            widen_first(3, slice(HALF, V), True)
-            widen_first(2, slice(0, HALF), True)
-            widen_first(3, slice(0, HALF), False)
+            widen_first(0, 1, False)
+            widen_first(0, 0, False)
+            widen_first(3, 0, False)
+            widen_first(1, 1, True)
+            widen_first(1, 0, True)
+            widen_first(2, 1, True)
+            widen_first(3, 1, True)
+            widen_first(2, 0, True)
             for pair in range(2):
                 hf_turn(0, pair, "turn")
             v_interleave((4, 2, 0))
@@ -401,11 +409,9 @@ def tile_persistentmeanfieldisingrbmgradient_w4_kernel(
 
             def stretch(g):
                 if g + 2 < G:
-                    if g == 0:
-                        h_rest(0, nc.vector.tensor_copy)
+                    h_rest(g, 0, nc.vector.tensor_copy)
+                    h_rest(g, 1, nc.vector.tensor_copy)
                     quantise(hf_mx, g + 2, 0, 512, hf_staged[g + 2][:])
-                    if g == 0:
-                        h_rest(1, nc.vector.tensor_copy)
                 elif g == G - 1:
                     v1_quantise(0, 1)
                 quantise(hn_mx, g, 0, H, h_place(g, 0, H))
@@ -426,7 +432,8 @@ def tile_persistentmeanfieldisingrbmgradient_w4_kernel(
                 if g + 2 < G:
                     hf_copy_out(g + 2, second, nc.scalar.copy)
                 if second and g + 2 >= G:
-                    h_rest(g, nc.scalar.copy)
+                    h_rest(g, 0, nc.scalar.copy)
+                    h_rest(g, 1, nc.scalar.copy)
                 widen_some(WIDEN_PER_QUAD[q])
                 for unit in range(first + 6, first + 10):
                     if unit < units:

@@ -28,11 +28,13 @@ QUADS = G * MT // QUAD
 
 H_REST = 96
 WARM = 6
+SPLIT = (4, 5, 6)
+SPLIT_N = 2
 AHEAD = 2
 SCALAR_LIST = [(4, 2, 2), (6, 2, 1), (6, 2, 2)]
 V1_AFTER = (0, 2, 4)
 SCALAR_JOBS = 3
-WIDEN_PER_QUAD = [0, 0, 0, 0, 1, 0, 1, 0]
+WIDEN_PER_QUAD = [0, 1, 1, 1, 1, 0, 1, 0]
 
 
 def tile_persistentmeanfieldisingrbmgradient_w4_kernel(
@@ -147,13 +149,13 @@ def tile_persistentmeanfieldisingrbmgradient_w4_kernel(
                 )
             load_hf_slots(1, 0, 2)
             load_hf_slots(1, 2, 2)
-            nc.sync.dma_start(out=scale_later[:], in_=scale_view[:, 1:G, :])
-            load_v_second(0)
             nc.sync.dma_start(out=s_rows[:], in_=s.rearrange("(g p t) -> p g t", p=P, t=SLOTS))
             load_h_part(0, 0)
             load_hf_slots(2, 0, 2)
             load_h_part(0, 1)
             load_hf_slots(2, 2, 2)
+            nc.sync.dma_start(out=scale_later[:], in_=scale_view[:, 1:G, :])
+            load_v_second(0)
             load_h(1)
             load_hf_slots(3, 0, SLOTS)
             load_v_second(1)
@@ -306,7 +308,7 @@ def tile_persistentmeanfieldisingrbmgradient_w4_kernel(
                 elif on_vector:
                     v_staged[job] = reused(name, [P, 512 * tiles], BF16, "v_staged", 5)
                 else:
-                    v_staged[job] = staging(name, 1 + SCALAR_LIST.index(job))[:, 0 : 512 * tiles]
+                    v_staged[job] = staging(name, 1 + (SCALAR_LIST + [job]).index(job))[:, 0 : 512 * tiles]
                 half, first = divmod(P * m0, HALF)
                 interleave(
                     nc.vector.tensor_copy if on_vector else nc.scalar.copy,
@@ -339,15 +341,17 @@ def tile_persistentmeanfieldisingrbmgradient_w4_kernel(
                 for g in range(G - 1):
                     correlate(len(acc) - 1, v1_mx, hn_mx, g, first=g == 0)
 
-            def store(m, on_vector):
+            def store(m, on_vector, parts=1):
                 result = float_tile("result%d" % m, [P, H])
-                if on_vector:
-                    nc.vector.tensor_scalar(
-                        out=result[:], in0=acc[m][:], scalar1=float(B) ** -0.5, scalar2=None, op0=ALU.mult
-                    )
-                else:
-                    nc.scalar.activation(result[:], acc[m][:], ACT.Copy, scale=float(B) ** -0.5)
-                nc.sync.dma_start(out=out[P * m : P * (m + 1), :], in_=result[:])
+                for part in range(parts):
+                    cols = slice(H // parts * part, H // parts * (part + 1))
+                    if on_vector:
+                        nc.vector.tensor_scalar(
+                            out=result[:, cols], in0=acc[m][:, cols], scalar1=float(B) ** -0.5, scalar2=None, op0=ALU.mult
+                        )
+                    else:
+                        nc.scalar.activation(result[:, cols], acc[m][:, cols], ACT.Copy, scale=float(B) ** -0.5)
+                    nc.sync.dma_start(out=out[P * m : P * (m + 1), cols], in_=result[:, cols])
 
             warm_bank = psum.tile([P, 512], F32, name="warm_bank", tag="bank7")
 
@@ -379,10 +383,10 @@ def tile_persistentmeanfieldisingrbmgradient_w4_kernel(
             v_quantise((4, 2, 0))
             nc.vector.tensor_copy(out=bias[:], in_=bias_bank[:, 0:MT])
             quantise(hf_mx, 0, 256, 256, hf_staged[0][:, 1024:2048])
-            v_interleave((0, 2, 0))
+            v_interleave((0, 2, 0), False)
             v_interleave((2, 2, 0))
             hf_turn(1, 0, "turn")
-            hf_copy_out(1, 0, nc.scalar.copy)
+            hf_copy_out(1, 0, nc.vector.tensor_copy)
             for unit in range(QUAD):
                 field(unit)
             hf_turn(1, 1, "turn")
@@ -391,16 +395,13 @@ def tile_persistentmeanfieldisingrbmgradient_w4_kernel(
             for unit in range(2):
                 tanh(unit)
                 field(unit + QUAD)
-            hf_copy_out(1, 1, nc.scalar.copy)
-            for t in range(SLOTS):
-                widen(0, 1, t, True)
-            quantise(hf_mx, 1, 0, 512, hf_staged[1][:])
             nc.vector.tensor_scalar(out=s_neg[:], in0=s_rows[:], scalar1=-1.0, scalar2=None, op0=ALU.mult)
+            hf_copy_out(1, 1, nc.vector.tensor_copy)
             v_quantise((2, 2, 0))
-            v_interleave((0, 2, 1))
+            quantise(hf_mx, 1, 0, 512, hf_staged[1][:])
 
             to_widen = [(half, g, t) for half in range(2) for g in range(1, G) for t in range(SLOTS)]
-            widened = [SLOTS]
+            widened = [0]
 
             def widen_some(count):
                 for item in to_widen[widened[0] : widened[0] + count]:
@@ -410,7 +411,8 @@ def tile_persistentmeanfieldisingrbmgradient_w4_kernel(
             def stretch(g):
                 if g + 2 < G:
                     h_rest(g, 0, nc.vector.tensor_copy)
-                    h_rest(g, 1, nc.vector.tensor_copy)
+                    if g == 0:
+                        h_rest(g, 1, nc.vector.tensor_copy)
                     quantise(hf_mx, g + 2, 0, 512, hf_staged[g + 2][:])
                 elif g == G - 1:
                     v1_quantise(0, 1)
@@ -429,6 +431,9 @@ def tile_persistentmeanfieldisingrbmgradient_w4_kernel(
                     turn(unit)
                     if g + 2 < G and unit == first + 1:
                         hf_turn(g + 2, second, "field")
+                    if q in SPLIT and unit == first + 1:
+                        for ahead in range(first + 6, first + 6 + SPLIT_N):
+                            field(ahead)
                 if g + 2 < G:
                     hf_copy_out(g + 2, second, nc.scalar.copy)
                 if second and g + 2 >= G:
@@ -436,6 +441,8 @@ def tile_persistentmeanfieldisingrbmgradient_w4_kernel(
                     h_rest(g, 1, nc.scalar.copy)
                 widen_some(WIDEN_PER_QUAD[q])
                 for unit in range(first + 6, first + 10):
+                    if unit in field_bank:
+                        continue
                     if unit < units:
                         field(unit)
                     elif unit == units:
@@ -448,6 +455,7 @@ def tile_persistentmeanfieldisingrbmgradient_w4_kernel(
                 if second:
                     stretch(g)
 
+            h_rest(1, 1, nc.vector.tensor_copy)
             hp_quantise(0)
             for m in range(MT // 2, MT):
                 open_acc("turn")
@@ -461,6 +469,7 @@ def tile_persistentmeanfieldisingrbmgradient_w4_kernel(
             scalar_jobs = SCALAR_LIST
             widen_some(len(to_widen))
 
+            v_interleave(jobs[0])
             for index, job in enumerate(jobs):
                 m0, tiles, g = job
                 if m0 == 0:
@@ -489,4 +498,4 @@ def tile_persistentmeanfieldisingrbmgradient_w4_kernel(
                             v_interleave(late, False)
             for g in range(1, G):
                 correlate(MT - 1, v_mx, hp_mx, g, last=g == G - 1)
-            store(MT - 1, True)
+            store(MT - 1, True, 2)

@@ -27,7 +27,8 @@ QUADS = G * MT // QUAD
 
 
 H_REST = 96
-WARM = 6
+WARM = 7
+HF_QUAD = 1
 SPLIT = (4, 5, 6)
 SPLIT_N = 2
 AHEAD = 2
@@ -141,17 +142,17 @@ def tile_persistentmeanfieldisingrbmgradient_w4_kernel(
             load_hf_slots(0, 0, 2)
             load_hf_slots(0, 2, 2)
             nc.sync.dma_start(out=b_rows[0:MT, :], in_=b.rearrange("(m c) -> m c", c=P))
+            load_hf_slots(1, 0, 2)
+            load_hf_slots(1, 2, 2)
             nc.sync.dma_start(out=w_codes[:], in_=w_words[0])
             for q in range(4):
                 nc.sync.dma_start(
                     out=w_plane[32 * q : 32 * q + 4, :].bitcast(I32),
                     in_=w_scales[0][4 * q : 4 * q + 4, :].bitcast(I32),
                 )
-            load_hf_slots(1, 0, 2)
-            load_hf_slots(1, 2, 2)
             nc.sync.dma_start(out=s_rows[:], in_=s.rearrange("(g p t) -> p g t", p=P, t=SLOTS))
-            load_h_part(0, 0)
             load_hf_slots(2, 0, 2)
+            load_h_part(0, 0)
             load_h_part(0, 1)
             load_hf_slots(2, 2, 2)
             nc.sync.dma_start(out=scale_later[:], in_=scale_view[:, 1:G, :])
@@ -191,6 +192,13 @@ def tile_persistentmeanfieldisingrbmgradient_w4_kernel(
                     first = H // 2 * (2 * pair + i)
                     for u in range(2):
                         nc.tensor.transpose(bank[:, i, :, u], words[:, first + u : first + H // 2 : 2], ident[:])
+
+            def hf_turn_slot(g, t):
+                bank = next_bank("field", [P, P, 2])
+                words = hf_rows[g][:].bitcast(F32)
+                for u in range(2):
+                    nc.tensor.transpose(bank[:, :, u], words[:, H // 2 * t + u : H // 2 * (t + 1) : 2], ident[:])
+                return bank
 
             def hf_copy_out(g, pair, copy):
                 copy(
@@ -368,35 +376,39 @@ def tile_persistentmeanfieldisingrbmgradient_w4_kernel(
             widen_first(2, 1, True)
             widen_first(3, 1, True)
             widen_first(2, 0, True)
-            for pair in range(2):
-                hf_turn(0, pair, "turn")
-            v_interleave((4, 2, 0))
+            hf_turn(0, 0, "turn")
+            last_banks = [hf_turn_slot(0, t) for t in (2, 3)]
             nc.vector.tensor_copy(out=b_rows32[:], in_=b_rows[:])
+            v_interleave((4, 2, 0))
             bias_bank = next_bank("turn", [P, P])
             nc.tensor.transpose(bias_bank[:], b_rows32[:], ident[:])
             warm_up()
             warm_up()
+            hf_turn(1, 0, "turn")
+            hf_turn(1, 1, "turn")
             v_interleave((6, 2, 0))
             hf_copy_out(0, 0, nc.scalar.copy)
-            hf_copy_out(0, 1, nc.scalar.copy)
+            for t in (2, 3):
+                nc.scalar.copy(out=hf_staged[0][:, 512 * t : 512 * t + 512].bitcast(F32), in_=last_banks[t - 2][:].rearrange("p r u -> p (r u)"))
             quantise(hf_mx, 0, 0, 256, hf_staged[0][:, 0:1024])
-            v_quantise((4, 2, 0))
+            quantise(hf_mx, 0, 256, 128, hf_staged[0][:, 1024:1536])
             nc.vector.tensor_copy(out=bias[:], in_=bias_bank[:, 0:MT])
-            quantise(hf_mx, 0, 256, 256, hf_staged[0][:, 1024:2048])
+            quantise(hf_mx, 0, 384, 128, hf_staged[0][:, 1536:2048])
+            v_quantise((4, 2, 0))
             v_interleave((0, 2, 0), False)
             v_interleave((2, 2, 0))
-            hf_turn(1, 0, "turn")
             hf_copy_out(1, 0, nc.vector.tensor_copy)
             for unit in range(QUAD):
                 field(unit)
-            hf_turn(1, 1, "turn")
+            hf_turn(2, 0, "turn")
+            hf_copy_out(1, 1, nc.vector.tensor_copy)
             for m0 in (6, 0):
                 v_quantise((m0, 2, 0))
             for unit in range(2):
                 tanh(unit)
                 field(unit + QUAD)
             nc.vector.tensor_scalar(out=s_neg[:], in0=s_rows[:], scalar1=-1.0, scalar2=None, op0=ALU.mult)
-            hf_copy_out(1, 1, nc.vector.tensor_copy)
+            hf_copy_out(2, 0, nc.vector.tensor_copy)
             v_quantise((2, 2, 0))
             quantise(hf_mx, 1, 0, 512, hf_staged[1][:])
 
@@ -420,6 +432,7 @@ def tile_persistentmeanfieldisingrbmgradient_w4_kernel(
                 v1_quantise(g, 0)
 
             units = G * MT
+            hf_in_quad = {HF_QUAD: (2, 1), 2: (3, 0), 3: (3, 1)}
             for q in range(QUADS):
                 g, second = divmod(q, 2)
                 first = QUAD * q
@@ -429,13 +442,13 @@ def tile_persistentmeanfieldisingrbmgradient_w4_kernel(
                     tanh(unit)
                 for unit in range(first, first + QUAD):
                     turn(unit)
-                    if g + 2 < G and unit == first + 1:
-                        hf_turn(g + 2, second, "field")
+                    if q in hf_in_quad and unit == first + 1:
+                        hf_turn(*hf_in_quad[q], "field")
                     if q in SPLIT and unit == first + 1:
                         for ahead in range(first + 6, first + 6 + SPLIT_N):
                             field(ahead)
-                if g + 2 < G:
-                    hf_copy_out(g + 2, second, nc.scalar.copy)
+                if q in hf_in_quad:
+                    hf_copy_out(*hf_in_quad[q], nc.scalar.copy)
                 if second and g + 2 >= G:
                     h_rest(g, 0, nc.scalar.copy)
                     h_rest(g, 1, nc.scalar.copy)

@@ -28,11 +28,13 @@ QUADS = G * MT // QUAD
 
 H_REST = 96
 WARM = 7
+EARLY = 2
+EARLY_AT = 0
 HF_QUAD = 1
 SPLIT = (4, 5, 6)
 SPLIT_N = 2
 AHEAD = 2
-SCALAR_LIST = [(4, 2, 2), (6, 2, 1), (6, 2, 2)]
+SCALAR_LIST = [(2, 2, 1), (2, 2, 2), (6, 1, 2), (7, 1, 2)]
 V1_AFTER = (0, 2, 4)
 SCALAR_JOBS = 3
 WIDEN_PER_QUAD = [0, 1, 1, 1, 1, 0, 1, 0]
@@ -313,10 +315,12 @@ def tile_persistentmeanfieldisingrbmgradient_w4_kernel(
                 name = "v_staged%d_%d" % (m0, g)
                 if job == (2, 2, 0):
                     v_staged[job] = h_place(0, 2 * P, 4 * P)
+                elif tiles == 4:
+                    v_staged[job] = staging(name, 5)
                 elif on_vector:
                     v_staged[job] = reused(name, [P, 512 * tiles], BF16, "v_staged", 5)
                 else:
-                    v_staged[job] = staging(name, 1 + (SCALAR_LIST + [job]).index(job))[:, 0 : 512 * tiles]
+                    v_staged[job] = staging(name, (1, 2, 3, 4, 5)[(SCALAR_LIST + [job]).index(job) if job[2] else 0])[:, 0 : 512 * tiles]
                 half, first = divmod(P * m0, HALF)
                 interleave(
                     nc.vector.tensor_copy if on_vector else nc.scalar.copy,
@@ -379,35 +383,33 @@ def tile_persistentmeanfieldisingrbmgradient_w4_kernel(
             hf_turn(0, 0, "turn")
             last_banks = [hf_turn_slot(0, t) for t in (2, 3)]
             nc.vector.tensor_copy(out=b_rows32[:], in_=b_rows[:])
-            v_interleave((4, 2, 0))
+            v_interleave((4, 4, 0))
             bias_bank = next_bank("turn", [P, P])
             nc.tensor.transpose(bias_bank[:], b_rows32[:], ident[:])
             warm_up()
             warm_up()
             hf_turn(1, 0, "turn")
             hf_turn(1, 1, "turn")
-            v_interleave((6, 2, 0))
             hf_copy_out(0, 0, nc.scalar.copy)
             for t in (2, 3):
                 nc.scalar.copy(out=hf_staged[0][:, 512 * t : 512 * t + 512].bitcast(F32), in_=last_banks[t - 2][:].rearrange("p r u -> p (r u)"))
             quantise(hf_mx, 0, 0, 256, hf_staged[0][:, 0:1024])
             quantise(hf_mx, 0, 256, 128, hf_staged[0][:, 1024:1536])
-            nc.vector.tensor_copy(out=bias[:], in_=bias_bank[:, 0:MT])
             quantise(hf_mx, 0, 384, 128, hf_staged[0][:, 1536:2048])
-            v_quantise((4, 2, 0))
+            v_quantise((4, 4, 0))
             v_interleave((0, 2, 0), False)
+            nc.scalar.copy(out=bias[:], in_=bias_bank[:, 0:MT])
             v_interleave((2, 2, 0))
             hf_copy_out(1, 0, nc.vector.tensor_copy)
             for unit in range(QUAD):
                 field(unit)
             hf_turn(2, 0, "turn")
             hf_copy_out(1, 1, nc.vector.tensor_copy)
-            for m0 in (6, 0):
-                v_quantise((m0, 2, 0))
+            v_quantise((0, 2, 0))
             for unit in range(2):
                 tanh(unit)
                 field(unit + QUAD)
-            nc.vector.tensor_scalar(out=s_neg[:], in0=s_rows[:], scalar1=-1.0, scalar2=None, op0=ALU.mult)
+            nc.scalar.activation(s_neg[:], s_rows[:], ACT.Copy, scale=-1.0)
             hf_copy_out(2, 0, nc.vector.tensor_copy)
             v_quantise((2, 2, 0))
             quantise(hf_mx, 1, 0, 512, hf_staged[1][:])
@@ -423,8 +425,6 @@ def tile_persistentmeanfieldisingrbmgradient_w4_kernel(
             def stretch(g):
                 if g + 2 < G:
                     h_rest(g, 0, nc.vector.tensor_copy)
-                    if g == 0:
-                        h_rest(g, 1, nc.vector.tensor_copy)
                     quantise(hf_mx, g + 2, 0, 512, hf_staged[g + 2][:])
                 elif g == G - 1:
                     v1_quantise(0, 1)
@@ -468,6 +468,7 @@ def tile_persistentmeanfieldisingrbmgradient_w4_kernel(
                 if second:
                     stretch(g)
 
+            h_rest(0, 1, nc.vector.tensor_copy)
             h_rest(1, 1, nc.vector.tensor_copy)
             hp_quantise(0)
             for m in range(MT // 2, MT):
@@ -478,8 +479,12 @@ def tile_persistentmeanfieldisingrbmgradient_w4_kernel(
             for m in range(MT):
                 correlate(m, v_mx, hp_mx, 0)
 
-            jobs = [(m0, 2, g) for m0 in range(0, MT, 2) for g in range(1, G)]
+            jobs = [(m0, 2, g) for m0 in range(0, MT - 2, 2) for g in range(1, G)]
+            jobs = jobs + [(m, 1, g) for m in range(MT - 2, MT) for g in range(1, G)]
             scalar_jobs = SCALAR_LIST
+            widen_some(len(to_widen) // 2 + EARLY_AT - widened[0])
+            for late in scalar_jobs[:EARLY]:
+                v_interleave(late, False)
             widen_some(len(to_widen))
 
             v_interleave(jobs[0])
@@ -493,22 +498,17 @@ def tile_persistentmeanfieldisingrbmgradient_w4_kernel(
                 if later:
                     v_interleave(later[0])
                 v_quantise(job)
-                for m in range(m0, min(m0 + tiles, MT - 1)):
+                for m in range(m0, m0 + tiles):
                     correlate(m, v_mx, hp_mx, g, last=g == G - 1)
                 if index in V1_AFTER:
                     late = V1_AFTER.index(index) + 1
                     v1_quantise(late, 1)
                     for m in range(MT // 2, MT):
                         correlate(m, v1_mx, hn_mx, late)
-                if job == jobs[-1]:
-                    store(MT - 3, True)
-                if g == G - 1:
-                    store(m0, False)
-                    if m0 < MT - 4:
-                        store(m0 + 1, False)
+                if g == G - 1 and m0 < MT - 1:
+                    for m in range(m0, m0 + tiles):
+                        store(m, False)
                     if m0 == 0:
-                        for late in scalar_jobs:
+                        for late in scalar_jobs[EARLY:]:
                             v_interleave(late, False)
-            for g in range(1, G):
-                correlate(MT - 1, v_mx, hp_mx, g, last=g == G - 1)
             store(MT - 1, True, 2)

@@ -26,7 +26,7 @@ QUAD = 4
 QUADS = G * MT // QUAD
 
 
-H_REST = 96
+H_REST = 80
 WARM = 7
 EARLY = 2
 EARLY_AT = 0
@@ -90,8 +90,8 @@ def tile_persistentmeanfieldisingrbmgradient_w4_kernel(
         w_plane = kept("w_plane", [P, V], U8, 256)
         ident = kept("ident", [P, P], F32)
         b_rows = kept("b_rows", [P, P], BF16)
-        b_rows32 = kept("b_rows32", [P, P], F32)
-        bias = kept("bias", [P, MT], F32)
+        ident16 = kept("ident16", [P, P], BF16)
+        bias = kept("bias", [P, MT], BF16)
         s_neg = kept("s_neg", [P, G, SLOTS], F32)
         s_rows = kept("s_rows", [P, G, SLOTS], BF16)
         scale_later = kept("scale_later", [P, G - 1, SLOTS], F32)
@@ -105,6 +105,7 @@ def tile_persistentmeanfieldisingrbmgradient_w4_kernel(
             nc.vector.memset(zeros[:], 0.0)
             nc.vector.memset(w_plane[:].bitcast(I32), 0)
             make_identity(nc, ident[:])
+            make_identity(nc, ident16[:])
             scale_view = v_scale.rearrange("(g p t) o -> p g (t o)", p=P, t=SLOTS)
             nc.scalar.dma_start(out=scale_first[:], in_=scale_view[:, 0, :])
             nc.scalar.activation(table_warm[:], table_warm[:], ACT.Tanh)
@@ -382,10 +383,9 @@ def tile_persistentmeanfieldisingrbmgradient_w4_kernel(
             widen_first(2, 0, True)
             hf_turn(0, 0, "turn")
             last_banks = [hf_turn_slot(0, t) for t in (2, 3)]
-            nc.vector.tensor_copy(out=b_rows32[:], in_=b_rows[:])
             v_interleave((4, 4, 0))
-            bias_bank = next_bank("turn", [P, P])
-            nc.tensor.transpose(bias_bank[:], b_rows32[:], ident[:])
+            bias_bank = next_bank("turn", [P, P], dtype=BF16)
+            nc.tensor.transpose(bias_bank[:], b_rows[:], ident16[:])
             warm_up()
             warm_up()
             hf_turn(1, 0, "turn")
@@ -508,7 +508,6 @@ def tile_persistentmeanfieldisingrbmgradient_w4_kernel(
                 if g == G - 1 and m0 < MT - 1:
                     for m in range(m0, m0 + tiles):
                         store(m, False)
-                    if m0 == 0:
-                        for late in scalar_jobs[EARLY:]:
-                            v_interleave(late, False)
+                    if m0 < 4:
+                        v_interleave(scalar_jobs[EARLY + m0 // 2], False)
             store(MT - 1, True, 2)

@@ -209,6 +209,7 @@ def tile_persistentmeanfieldisingrbmgradient_w4_kernel(
                     in_=hf_bank[(g, pair)][:].rearrange("p i r u -> p (i r u)"),
                 )
 
+            ident_pairs = ident[:].rearrange("p (a b) -> p a b", b=2)
             field_bank = {}
             tanh_tile = {}
             turned_bank = {}
@@ -241,9 +242,9 @@ def tile_persistentmeanfieldisingrbmgradient_w4_kernel(
                 )
 
             def turn(unit):
-                turned_bank[unit] = next_bank("turn", [P, SLOTS, P])
+                turned_bank[unit] = next_bank("turn", [P, P // 2, SLOTS, 2])
                 for t in range(SLOTS):
-                    nc.tensor.transpose(turned_bank[unit][:, t, :], tanh_tile[unit][:, t, :], ident[:])
+                    nc.tensor.transpose(turned_bank[unit][:, :, t, :], tanh_tile[unit][:, t, :], ident_pairs)
 
             def v1_buffer(g, half):
                 if half:
@@ -256,9 +257,9 @@ def tile_persistentmeanfieldisingrbmgradient_w4_kernel(
                 if c == 0:
                     v1_staged[(g, half)] = staging("v1_staged%d_%d" % (g, half), v1_buffer(g, half))
                 nc.vector.tensor_tensor(
-                    out=v1_staged[(g, half)][:, 512 * c : 512 * c + 512].rearrange("p (c t) -> p c t", t=SLOTS),
-                    in0=turned_bank[unit][:].rearrange("p t c -> p c t"),
-                    in1=s_neg[:, g, :].unsqueeze(1).to_broadcast([P, P, SLOTS]),
+                    out=v1_staged[(g, half)][:, 512 * c : 512 * c + 512].rearrange("p (a b t) -> p a t b", b=2, t=SLOTS),
+                    in0=turned_bank[unit][:],
+                    in1=s_neg[:, g, :].unsqueeze(1).unsqueeze(3).to_broadcast([P, P // 2, SLOTS, 2]),
                     op=ALU.mult,
                 )
 

@@ -26,7 +26,7 @@ QUAD = 4
 QUADS = G * MT // QUAD
 
 
-H_REST = 80
+H_REST = 40
 WARM = 7
 EARLY = 2
 EARLY_AT = 0
@@ -74,7 +74,7 @@ def tile_persistentmeanfieldisingrbmgradient_w4_kernel(
             return psum.tile(shape, dtype, name=name, tag=name)
 
         hf_rows = [reused("hf_rows%d" % g, [P, SLOTS * H], BF16, "rows%d" % g) for g in range(G)]
-        h_rows = [kept("h_rows%d" % g, [P, 2 * SLOTS * H + H_REST], BF16) for g in range(G)]
+        h_rows = [kept("h_rows%d" % g, [P, SLOTS, 2 * H], BF16) for g in range(G)]
         h_staged = kept("h_staged", [P, SLOTS * (G + 1) * H], BF16, 256)
         v_rows = {g: kept("v_rows%d" % g, [P, SLOTS, V], U8) for g in range(2, G)}
         v_rows_second = [kept("v_rows_second%d" % half, [P, SLOTS, HALF], U8) for half in range(2)]
@@ -117,11 +117,10 @@ def tile_persistentmeanfieldisingrbmgradient_w4_kernel(
                 nc.sync.dma_start(out=tiles[g][:], in_=group_rows(x, g))
 
             def h_source(g, a):
-                first = (SLOTS * H + H_REST) * a
-                return h_rows[g][:, first : first + SLOTS * H]
+                return h_rows[g][:, :, H * a : H * (a + 1)]
 
             def load_h_part(g, a):
-                nc.sync.dma_start(out=h_source(g, a), in_=group_rows((hn, hp)[a], g).rearrange("p t c -> p (t c)"))
+                nc.sync.dma_start(out=h_source(g, a), in_=group_rows((hn, hp)[a], g))
 
             def load_h(g):
                 load_h_part(g, 0)
@@ -273,10 +272,9 @@ def tile_persistentmeanfieldisingrbmgradient_w4_kernel(
                 )
 
             def gpsimd_share(g):
-                rows = h_rows[g][:, 0 : 2 * SLOTS * H].rearrange("p (a t c) -> p a c t", a=2, t=SLOTS)
                 nc.gpsimd.tensor_scalar(
-                    out=h_place(g, H_REST, 2 * H - H_REST).rearrange("p (a c t) -> p a c t", a=2, t=SLOTS),
-                    in0=rows[:, :, H_REST:, :],
+                    out=h_place(g, H_REST, 2 * H - H_REST).rearrange("p (c i t) -> p c t i", i=4, t=SLOTS),
+                    in0=h_rows[g][:, :, H_REST : 2 * H - H_REST].rearrange("p t (c i) -> p c t i", i=4),
                     scalar1=1.0,
                     scalar2=0.0,
                     op0=ALU.mult,
@@ -285,7 +283,7 @@ def tile_persistentmeanfieldisingrbmgradient_w4_kernel(
 
             def h_rest(g, a, copy):
                 first = (H - H_REST) * a
-                rows = h_source(g, a).rearrange("p (t c) -> p t c", t=SLOTS)
+                rows = h_source(g, a)
                 interleave(copy, h_place(g, H * a + first, H * a + first + H_REST), rows[:, :, first : first + H_REST])
 
             def hp_quantise(g):

@@ -19,25 +19,20 @@ ALU = mybir.AluOpType
 
 P = 128
 SLOTS = 4
-G = B // (P * SLOTS)
+PASS = P * SLOTS
+G = B // PASS
 MT = V // P
 HALF = V // 2
 QUAD = 4
 QUADS = G * MT // QUAD
-
+LEAD = 6
+RUN = 4
 
 H_REST = 40
-WARM = 7
-EARLY = 2
-EARLY_AT = 0
-HF_QUAD = 1
-SPLIT = (4, 5, 6)
-SPLIT_N = 2
-AHEAD = 2
-SCALAR_LIST = [(2, 2, 1), (2, 2, 2), (6, 1, 2), (7, 1, 2)]
-V1_AFTER = (0, 2, 4)
-SCALAR_JOBS = 3
-WIDEN_PER_QUAD = [0, 1, 1, 1, 1, 0, 1, 0]
+WARM_FRONT = 7
+WARM_MID = 2
+EARLY_JOBS = 2
+LATE_GROUP = 2
 
 
 def tile_persistentmeanfieldisingrbmgradient_w4_kernel(
@@ -81,7 +76,7 @@ def tile_persistentmeanfieldisingrbmgradient_w4_kernel(
         v_rows_first = [kept("v_rows_first%d" % pair, [P, 2, V], U8) for pair in range(2)]
         v_wide = {(0, g): kept("v_wide0_%d" % g, [P, SLOTS, HALF], BF16) for g in range(G)}
         v_wide[(1, 0)] = kept("v_wide1_0", [P, SLOTS, HALF], BF16)
-        hf_mx = mx_operand("hf", P * SLOTS)
+        hf_mx = mx_operand("hf", PASS)
         hn_mx = mx_operand("hn", H)
         hp_mx = mx_operand("hp", H)
         v1_mx = mx_operand("v1", V)
@@ -96,7 +91,7 @@ def tile_persistentmeanfieldisingrbmgradient_w4_kernel(
         s_rows = kept("s_rows", [P, G, SLOTS], BF16)
         scale_later = kept("scale_later", [P, G - 1, SLOTS], F32)
         scale_first = kept("scale_first", [P, SLOTS], F32)
-        zeros = kept("zeros", [P, 512], BF16)
+        zeros = kept("zeros", [P, PASS], BF16)
         table_warm = kept("table_warm", [P, 1], F32)
 
         with tc.manual_schedule():
@@ -113,39 +108,29 @@ def tile_persistentmeanfieldisingrbmgradient_w4_kernel(
             def group_rows(x, g):
                 return x.rearrange("(g p t) c -> g p t c", p=P, t=SLOTS)[g]
 
-            def load(tiles, x, g):
-                nc.sync.dma_start(out=tiles[g][:], in_=group_rows(x, g))
+            def h_source(g, which):
+                return h_rows[g][:, :, H * which : H * (which + 1)]
 
-            def h_source(g, a):
-                return h_rows[g][:, :, H * a : H * (a + 1)]
+            def load_h(g, which):
+                nc.sync.dma_start(out=h_source(g, which), in_=group_rows((hn, hp)[which], g))
 
-            def load_h_part(g, a):
-                nc.sync.dma_start(out=h_source(g, a), in_=group_rows((hn, hp)[a], g))
-
-            def load_h(g):
-                load_h_part(g, 0)
-                load_h_part(g, 1)
-
-            def load_hf_slots(g, first, count):
+            def load_hf(g, pair):
                 nc.sync.dma_start(
-                    out=hf_rows[g][:, H * first : H * (first + count)],
-                    in_=group_rows(hf, g)[:, first : first + count, :].rearrange("p t c -> p (t c)"),
+                    out=hf_rows[g][:, 2 * H * pair : 2 * H * (pair + 1)],
+                    in_=group_rows(hf, g)[:, 2 * pair : 2 * pair + 2, :].rearrange("p t c -> p (t c)"),
                 )
-
-            def load_v_first(pair):
-                nc.sync.dma_start(out=v_rows_first[pair][:], in_=group_rows(v_bytes, 0)[:, 2 * pair : 2 * pair + 2, :])
 
             def load_v_second(half):
                 cols = slice(HALF * half, HALF * half + HALF)
                 nc.sync.dma_start(out=v_rows_second[half][:], in_=group_rows(v_bytes, 1)[:, :, cols])
 
-            load_v_first(0)
-            load_v_first(1)
-            load_hf_slots(0, 0, 2)
-            load_hf_slots(0, 2, 2)
+            for pair in range(2):
+                nc.sync.dma_start(out=v_rows_first[pair][:], in_=group_rows(v_bytes, 0)[:, 2 * pair : 2 * pair + 2, :])
+            load_hf(0, 0)
+            load_hf(0, 1)
             nc.sync.dma_start(out=b_rows[0:MT, :], in_=b.rearrange("(m c) -> m c", c=P))
-            load_hf_slots(1, 0, 2)
-            load_hf_slots(1, 2, 2)
+            load_hf(1, 0)
+            load_hf(1, 1)
             nc.sync.dma_start(out=w_codes[:], in_=w_words[0])
             for q in range(4):
                 nc.sync.dma_start(
@@ -153,18 +138,20 @@ def tile_persistentmeanfieldisingrbmgradient_w4_kernel(
                     in_=w_scales[0][4 * q : 4 * q + 4, :].bitcast(I32),
                 )
             nc.sync.dma_start(out=s_rows[:], in_=s.rearrange("(g p t) -> p g t", p=P, t=SLOTS))
-            load_hf_slots(2, 0, 2)
-            load_h_part(0, 0)
-            load_h_part(0, 1)
-            load_hf_slots(2, 2, 2)
+            load_hf(2, 0)
+            load_h(0, 0)
+            load_h(0, 1)
+            load_hf(2, 1)
             nc.sync.dma_start(out=scale_later[:], in_=scale_view[:, 1:G, :])
             load_v_second(0)
-            load_h(1)
-            load_hf_slots(3, 0, SLOTS)
+            for part in range(2):
+                load_h(1, part)
+                load_hf(3, part)
             load_v_second(1)
             for g in range(2, G):
-                load(v_rows, v_bytes, g)
-                load_h(g)
+                nc.sync.dma_start(out=v_rows[g][:], in_=group_rows(v_bytes, g))
+                load_h(g, 0)
+                load_h(g, 1)
 
             def quantise(operand, g, col, width, src):
                 codes, scales = operand
@@ -175,7 +162,7 @@ def tile_persistentmeanfieldisingrbmgradient_w4_kernel(
                 )
 
             def staging(name, number):
-                return reused(name, [P, SLOTS * 512], BF16, "staging%d" % number)
+                return reused(name, [P, SLOTS * PASS], BF16, "staging%d" % number)
 
             def h_place(g, first, last):
                 base = SLOTS * H * (G - 1 - g)
@@ -184,31 +171,25 @@ def tile_persistentmeanfieldisingrbmgradient_w4_kernel(
             hf_staged = {}
             hf_bank = {}
 
+            def turn_slot(place, g, t):
+                words = hf_rows[g][:].bitcast(F32)
+                for u in range(2):
+                    nc.tensor.transpose(place[:, :, u], words[:, H // 2 * t + u : H // 2 * (t + 1) : 2], ident[:])
+
             def hf_turn(g, pair, kind):
                 if pair == 0:
                     hf_staged[g] = staging("hf_staged%d" % g, (0, 3, 2, 0)[g])
-                bank = next_bank(kind, [P, 2, P, 2])
-                hf_bank[(g, pair)] = bank
-                words = hf_rows[g][:].bitcast(F32)
+                hf_bank[(g, pair)] = next_bank(kind, [P, 2, P, 2])
                 for i in range(2):
-                    first = H // 2 * (2 * pair + i)
-                    for u in range(2):
-                        nc.tensor.transpose(bank[:, i, :, u], words[:, first + u : first + H // 2 : 2], ident[:])
-
-            def hf_turn_slot(g, t):
-                bank = next_bank("field", [P, P, 2])
-                words = hf_rows[g][:].bitcast(F32)
-                for u in range(2):
-                    nc.tensor.transpose(bank[:, :, u], words[:, H // 2 * t + u : H // 2 * (t + 1) : 2], ident[:])
-                return bank
+                    turn_slot(hf_bank[(g, pair)][:, i, :, :], g, 2 * pair + i)
 
             def hf_copy_out(g, pair, copy):
                 copy(
-                    out=hf_staged[g][:, 1024 * pair : 1024 * pair + 1024].bitcast(F32),
+                    out=hf_staged[g][:, 2 * PASS * pair : 2 * PASS * (pair + 1)].bitcast(F32),
                     in_=hf_bank[(g, pair)][:].rearrange("p i r u -> p (i r u)"),
                 )
 
-            ident_pairs = ident[:].rearrange("p (a b) -> p a b", b=2)
+            ident_pairs = ident[:].rearrange("p (a e) -> p a e", e=2)
             field_bank = {}
             tanh_tile = {}
             turned_bank = {}
@@ -216,7 +197,7 @@ def tile_persistentmeanfieldisingrbmgradient_w4_kernel(
 
             def field(unit):
                 g, m = divmod(unit, MT)
-                field_bank[unit] = next_bank("field", [P, P * SLOTS])
+                field_bank[unit] = next_bank("field", [P, PASS])
                 nc.tensor.matmul_mx(
                     out=field_bank[unit][:],
                     lhsT=w_codes[:, 2 * P * m : 2 * P * (m + 1)].bitcast(E2M1X4),
@@ -228,7 +209,7 @@ def tile_persistentmeanfieldisingrbmgradient_w4_kernel(
                 )
 
             def float_tile(name, shape):
-                return reused(name, shape, F32, "float_tile", 8)
+                return reused(name, shape, F32, "float_tile", 2 * QUAD)
 
             def tanh(unit):
                 m = unit % MT
@@ -245,18 +226,13 @@ def tile_persistentmeanfieldisingrbmgradient_w4_kernel(
                 for t in range(SLOTS):
                     nc.tensor.transpose(turned_bank[unit][:, :, t, :], tanh_tile[unit][:, t, :], ident_pairs)
 
-            def v1_buffer(g, half):
-                if half:
-                    return (3 + g) % 6
-                return 1 + g % 2
-
             def weight(unit):
                 g, m = divmod(unit, MT)
                 half, c = divmod(m, MT // 2)
                 if c == 0:
-                    v1_staged[(g, half)] = staging("v1_staged%d_%d" % (g, half), v1_buffer(g, half))
+                    v1_staged[(g, half)] = staging("v1_staged%d_%d" % (g, half), (3 + g) % 6 if half else 1 + g % 2)
                 nc.vector.tensor_tensor(
-                    out=v1_staged[(g, half)][:, 512 * c : 512 * c + 512].rearrange("p (a b t) -> p a t b", b=2, t=SLOTS),
+                    out=v1_staged[(g, half)][:, PASS * c : PASS * (c + 1)].rearrange("p (a e t) -> p a t e", e=2, t=SLOTS),
                     in0=turned_bank[unit][:],
                     in1=s_neg[:, g, :].unsqueeze(1).unsqueeze(3).to_broadcast([P, P // 2, SLOTS, 2]),
                     op=ALU.mult,
@@ -265,77 +241,74 @@ def tile_persistentmeanfieldisingrbmgradient_w4_kernel(
             def v1_quantise(g, half):
                 quantise(v1_mx, g, HALF * half, HALF, v1_staged[(g, half)][:])
 
-            def interleave(copy, dst, src):
-                copy(
-                    out=dst.rearrange("p (c i t) -> p c t i", i=4, t=SLOTS),
-                    in_=src.rearrange("p t (c i) -> p c t i", i=4),
-                )
+            def interleaved(dst):
+                return dst.rearrange("p (c i t) -> p c t i", i=RUN, t=SLOTS)
+
+            def by_runs(src):
+                return src.rearrange("p t (c i) -> p c t i", i=RUN)
 
             def gpsimd_share(g):
+                rest = H_REST if g + 2 >= G else 0
                 nc.gpsimd.tensor_scalar(
-                    out=h_place(g, H_REST, 2 * H - H_REST).rearrange("p (c i t) -> p c t i", i=4, t=SLOTS),
-                    in0=h_rows[g][:, :, H_REST : 2 * H - H_REST].rearrange("p t (c i) -> p c t i", i=4),
+                    out=interleaved(h_place(g, rest, 2 * H - rest)),
+                    in0=by_runs(h_rows[g][:, :, rest : 2 * H - rest]),
                     scalar1=1.0,
                     scalar2=0.0,
                     op0=ALU.mult,
                     op1=ALU.add,
                 )
 
-            def h_rest(g, a, copy):
-                first = (H - H_REST) * a
-                rows = h_source(g, a)
-                interleave(copy, h_place(g, H * a + first, H * a + first + H_REST), rows[:, :, first : first + H_REST])
+            def h_rest(g, which):
+                first = (H - H_REST) * which
+                nc.scalar.copy(
+                    out=interleaved(h_place(g, H * which + first, H * which + first + H_REST)),
+                    in_=by_runs(h_source(g, which)[:, :, first : first + H_REST]),
+                )
 
             def hp_quantise(g):
                 quantise(hp_mx, g, 0, H, h_place(g, H, 2 * H))
 
-            def widen_columns(dst, src, scale, on_vector):
-                if on_vector:
-                    nc.vector.tensor_scalar(out=dst, in0=src.bitcast(E4M3), scalar1=scale, scalar2=None, op0=ALU.mult)
-                else:
-                    nc.scalar.activation(dst, src.bitcast(E4M3), ACT.Copy, scale=scale)
-
             def widen_first(t, half, on_vector):
-                src = v_rows_first[t // 2][:, t % 2, HALF * half : HALF * half + HALF]
-                widen_columns(v_wide[(half, 0)][:, t, :], src, scale_first[:, t : t + 1], on_vector)
+                dst = v_wide[(half, 0)][:, t, :]
+                src = v_rows_first[t // 2][:, t % 2, HALF * half : HALF * half + HALF].bitcast(E4M3)
+                scale = scale_first[:, t : t + 1]
+                if on_vector:
+                    nc.vector.tensor_scalar(out=dst, in0=src, scalar1=scale, scalar2=None, op0=ALU.mult)
+                else:
+                    nc.scalar.activation(dst, src, ACT.Copy, scale=scale)
 
-            def widen(half, g, t, on_vector):
+            def widen(half, g, t):
                 if (half, g) not in v_wide:
                     v_wide[(half, g)] = reused("v_wide1_%d" % g, [P, SLOTS, HALF], BF16, "rows%d" % g)
                 if g == 1:
                     src = v_rows_second[half][:, t, :]
                 else:
                     src = v_rows[g][:, t, HALF * half : HALF * half + HALF]
-                widen_columns(v_wide[(half, g)][:, t, :], src, scale_later[:, g - 1, t : t + 1], on_vector)
+                nc.scalar.activation(
+                    v_wide[(half, g)][:, t, :], src.bitcast(E4M3), ACT.Copy, scale=scale_later[:, g - 1, t : t + 1]
+                )
 
             v_staged = {}
 
-            def v_interleave(job, on_vector=True):
+            def v_interleave(job, place, copy):
                 m0, tiles, g = job
-                name = "v_staged%d_%d" % (m0, g)
-                if job == (2, 2, 0):
-                    v_staged[job] = h_place(0, 2 * P, 4 * P)
-                elif tiles == 4:
-                    v_staged[job] = staging(name, 5)
-                elif on_vector:
-                    v_staged[job] = reused(name, [P, 512 * tiles], BF16, "v_staged", 5)
-                else:
-                    v_staged[job] = staging(name, (1, 2, 3, 4, 5)[(SCALAR_LIST + [job]).index(job) if job[2] else 0])[:, 0 : 512 * tiles]
                 half, first = divmod(P * m0, HALF)
-                interleave(
-                    nc.vector.tensor_copy if on_vector else nc.scalar.copy,
-                    v_staged[job][:],
-                    v_wide[(half, g)][:, :, first : first + P * tiles],
-                )
+                v_staged[job] = place
+                copy(out=interleaved(place), in_=by_runs(v_wide[(half, g)][:, :, first : first + P * tiles]))
+
+            def on_scalar(job, number):
+                place = staging("v_staged%d_%d" % (job[0], job[2]), number)
+                v_interleave(job, place[:, 0 : PASS * job[1]], nc.scalar.copy)
+
+            def on_vector(job):
+                place = reused("v_staged%d_%d" % (job[0], job[2]), [P, PASS * job[1]], BF16, "v_staged", 5)
+                v_interleave(job, place[:], nc.vector.tensor_copy)
 
             def v_quantise(job):
                 m0, tiles, g = job
-                quantise(v_mx, g, P * m0, P * tiles, v_staged[job][:])
+                quantise(v_mx, g, P * m0, P * tiles, v_staged[job])
 
             acc = []
-
-            def open_acc(kind):
-                acc.append(next_bank(kind, [P, H], True))
 
             def correlate(m, vis_mx, hid_mx, g, first=False, last=False):
                 nc.tensor.matmul_mx(
@@ -348,30 +321,23 @@ def tile_persistentmeanfieldisingrbmgradient_w4_kernel(
                     stop=last,
                 )
 
-            def open_with_early_groups(kind):
-                open_acc(kind)
+            def open_early():
+                acc.append(next_bank("field", [P, H], True))
                 for g in range(G - 1):
                     correlate(len(acc) - 1, v1_mx, hn_mx, g, first=g == 0)
 
-            def store(m, on_vector, parts=1):
+            def store(m):
                 result = float_tile("result%d" % m, [P, H])
-                for part in range(parts):
-                    cols = slice(H // parts * part, H // parts * (part + 1))
-                    if on_vector:
-                        nc.vector.tensor_scalar(
-                            out=result[:, cols], in0=acc[m][:, cols], scalar1=float(B) ** -0.5, scalar2=None, op0=ALU.mult
-                        )
-                    else:
-                        nc.scalar.activation(result[:, cols], acc[m][:, cols], ACT.Copy, scale=float(B) ** -0.5)
-                    nc.sync.dma_start(out=out[P * m : P * (m + 1), cols], in_=result[:, cols])
+                nc.scalar.activation(result[:], acc[m][:], ACT.Copy, scale=float(B) ** -0.5)
+                nc.sync.dma_start(out=out[P * m : P * (m + 1), :], in_=result[:])
 
-            warm_bank = psum.tile([P, 512], F32, name="warm_bank", tag="bank7")
+            warm_bank = psum.tile([P, PASS], F32, name="warm_bank", tag="bank7")
 
-            def warm_up():
-                nc.tensor.matmul(warm_bank[:], lhsT=zeros[:, 0:P], rhs=zeros[:], start=True, stop=True)
+            def warm_up(count):
+                for i in range(count):
+                    nc.tensor.matmul(warm_bank[:], lhsT=zeros[:, 0:P], rhs=zeros[:], start=True, stop=True)
 
-            for i in range(WARM):
-                warm_up()
+            warm_up(WARM_FRONT)
             widen_first(0, 1, False)
             widen_first(0, 0, False)
             widen_first(3, 0, False)
@@ -380,98 +346,102 @@ def tile_persistentmeanfieldisingrbmgradient_w4_kernel(
             widen_first(2, 1, True)
             widen_first(3, 1, True)
             widen_first(2, 0, True)
+            second_half, first_pair, second_pair = (MT // 2, MT // 2, 0), (0, 2, 0), (2, 2, 0)
             hf_turn(0, 0, "turn")
-            last_banks = [hf_turn_slot(0, t) for t in (2, 3)]
-            v_interleave((4, 4, 0))
+            last_banks = []
+            for t in range(2, SLOTS):
+                last_banks.append(next_bank("field", [P, P, 2]))
+                turn_slot(last_banks[-1][:], 0, t)
+            v_interleave(second_half, staging("v_staged_half", 5)[:], nc.vector.tensor_copy)
             bias_bank = next_bank("turn", [P, P], dtype=BF16)
             nc.tensor.transpose(bias_bank[:], b_rows[:], ident16[:])
-            warm_up()
-            warm_up()
+            warm_up(WARM_MID)
             hf_turn(1, 0, "turn")
             hf_turn(1, 1, "turn")
             hf_copy_out(0, 0, nc.scalar.copy)
-            for t in (2, 3):
-                nc.scalar.copy(out=hf_staged[0][:, 512 * t : 512 * t + 512].bitcast(F32), in_=last_banks[t - 2][:].rearrange("p r u -> p (r u)"))
-            quantise(hf_mx, 0, 0, 256, hf_staged[0][:, 0:1024])
-            quantise(hf_mx, 0, 256, 128, hf_staged[0][:, 1024:1536])
-            quantise(hf_mx, 0, 384, 128, hf_staged[0][:, 1536:2048])
-            v_quantise((4, 4, 0))
-            v_interleave((0, 2, 0), False)
+            for t in range(2, SLOTS):
+                nc.scalar.copy(
+                    out=hf_staged[0][:, PASS * t : PASS * (t + 1)].bitcast(F32),
+                    in_=last_banks[t - 2][:].rearrange("p r u -> p (r u)"),
+                )
+            quantise(hf_mx, 0, 0, 2 * P, hf_staged[0][:, 0 : 2 * PASS])
+            for t in range(2, SLOTS):
+                quantise(hf_mx, 0, P * t, P, hf_staged[0][:, PASS * t : PASS * (t + 1)])
+            v_quantise(second_half)
+            on_scalar(first_pair, 1)
             nc.scalar.copy(out=bias[:], in_=bias_bank[:, 0:MT])
-            v_interleave((2, 2, 0))
+            v_interleave(second_pair, h_place(0, 2 * P, 4 * P), nc.vector.tensor_copy)
             hf_copy_out(1, 0, nc.vector.tensor_copy)
             for unit in range(QUAD):
                 field(unit)
             hf_turn(2, 0, "turn")
             hf_copy_out(1, 1, nc.vector.tensor_copy)
-            v_quantise((0, 2, 0))
-            for unit in range(2):
+            v_quantise(first_pair)
+            for unit in range(LEAD - QUAD):
                 tanh(unit)
                 field(unit + QUAD)
             nc.scalar.activation(s_neg[:], s_rows[:], ACT.Copy, scale=-1.0)
             hf_copy_out(2, 0, nc.vector.tensor_copy)
-            v_quantise((2, 2, 0))
-            quantise(hf_mx, 1, 0, 512, hf_staged[1][:])
+            v_quantise(second_pair)
+            quantise(hf_mx, 1, 0, PASS, hf_staged[1][:])
 
             to_widen = [(half, g, t) for half in range(2) for g in range(1, G) for t in range(SLOTS)]
-            widened = [0]
 
-            def widen_some(count):
-                for item in to_widen[widened[0] : widened[0] + count]:
-                    widen(*item, False)
-                widened.append(widened.pop() + count)
+            def widen_next(count):
+                for item in to_widen[:count]:
+                    widen(*item)
+                    to_widen.remove(item)
 
             def stretch(g):
                 if g + 2 < G:
-                    h_rest(g, 0, nc.vector.tensor_copy)
-                    quantise(hf_mx, g + 2, 0, 512, hf_staged[g + 2][:])
+                    quantise(hf_mx, g + 2, 0, PASS, hf_staged[g + 2][:])
                 elif g == G - 1:
                     v1_quantise(0, 1)
                 quantise(hn_mx, g, 0, H, h_place(g, 0, H))
                 v1_quantise(g, 0)
 
             units = G * MT
-            hf_in_quad = {HF_QUAD: (2, 1), 2: (3, 0), 3: (3, 1)}
+            hf_left = [(2, 1), (3, 0), (3, 1)]
             for q in range(QUADS):
                 g, second = divmod(q, 2)
                 first = QUAD * q
+                turns_hf = 1 <= q <= len(hf_left)
+                fields_left = [unit for unit in range(first + LEAD, first + LEAD + QUAD) if unit < units]
                 if not second:
                     gpsimd_share(g)
-                for unit in range(first + 2, min(first + 6, units)):
+                for unit in range(first + LEAD - QUAD, min(first + LEAD, units)):
                     tanh(unit)
                 for unit in range(first, first + QUAD):
                     turn(unit)
-                    if q in hf_in_quad and unit == first + 1:
-                        hf_turn(*hf_in_quad[q], "field")
-                    if q in SPLIT and unit == first + 1:
-                        for ahead in range(first + 6, first + 6 + SPLIT_N):
-                            field(ahead)
-                if q in hf_in_quad:
-                    hf_copy_out(*hf_in_quad[q], nc.scalar.copy)
+                    if unit == first + 1:
+                        if turns_hf:
+                            hf_turn(*hf_left[q - 1], "field")
+                        elif q:
+                            for ahead in fields_left[:2]:
+                                field(ahead)
+                if turns_hf:
+                    hf_copy_out(*hf_left[q - 1], nc.scalar.copy)
                 if second and g + 2 >= G:
-                    h_rest(g, 0, nc.scalar.copy)
-                    h_rest(g, 1, nc.scalar.copy)
-                widen_some(WIDEN_PER_QUAD[q])
-                for unit in range(first + 6, first + 10):
-                    if unit in field_bank:
-                        continue
-                    if unit < units:
+                    h_rest(g, 0)
+                    h_rest(g, 1)
+                elif q:
+                    widen_next(1)
+                for unit in fields_left:
+                    if unit not in field_bank:
                         field(unit)
-                    elif unit == units:
-                        open_with_early_groups("field")
+                if q == QUADS - 2:
+                    open_early()
                 if q == QUADS - 1:
                     for m in range(1, MT // 2):
-                        open_with_early_groups("field")
+                        open_early()
                 for unit in range(first, first + QUAD):
                     weight(unit)
                 if second:
                     stretch(g)
 
-            h_rest(0, 1, nc.vector.tensor_copy)
-            h_rest(1, 1, nc.vector.tensor_copy)
             hp_quantise(0)
             for m in range(MT // 2, MT):
-                open_acc("turn")
+                acc.append(next_bank("turn", [P, H], True))
                 correlate(m, v1_mx, hn_mx, 0, first=True)
             for m in range(MT // 2):
                 correlate(m, v1_mx, hn_mx, G - 1)
@@ -480,33 +450,38 @@ def tile_persistentmeanfieldisingrbmgradient_w4_kernel(
 
             jobs = [(m0, 2, g) for m0 in range(0, MT - 2, 2) for g in range(1, G)]
             jobs = jobs + [(m, 1, g) for m in range(MT - 2, MT) for g in range(1, G)]
-            scalar_jobs = SCALAR_LIST
-            widen_some(len(to_widen) // 2 + EARLY_AT - widened[0])
-            for late in scalar_jobs[:EARLY]:
-                v_interleave(late, False)
-            widen_some(len(to_widen))
+            early = [(2, 2, g) for g in range(1, 1 + EARLY_JOBS)]
+            late = [(m, 1, LATE_GROUP) for m in range(MT - 2, MT)]
+            widen_next(len([item for item in to_widen if item[0] == 0]))
+            for number, job in enumerate(early):
+                on_scalar(job, 1 + number)
+            widen_next(len(to_widen))
 
-            v_interleave(jobs[0])
+            on_vector(jobs[0])
             for index, job in enumerate(jobs):
                 m0, tiles, g = job
                 if m0 == 0:
                     hp_quantise(g)
-                later = [
-                    other for other in jobs[index + 1 : index + 1 + AHEAD] if other not in v_staged and other not in scalar_jobs
-                ]
-                if later:
-                    v_interleave(later[0])
+                ahead = [other for other in jobs[index + 1 : index + 3] if other not in list(v_staged) + late]
+                if ahead:
+                    on_vector(ahead[0])
                 v_quantise(job)
                 for m in range(m0, m0 + tiles):
                     correlate(m, v_mx, hp_mx, g, last=g == G - 1)
-                if index in V1_AFTER:
-                    late = V1_AFTER.index(index) + 1
-                    v1_quantise(late, 1)
+                if index % 2 == 0 and index // 2 + 1 < G:
+                    v1_quantise(index // 2 + 1, 1)
                     for m in range(MT // 2, MT):
-                        correlate(m, v1_mx, hn_mx, late)
+                        correlate(m, v1_mx, hn_mx, index // 2 + 1)
                 if g == G - 1 and m0 < MT - 1:
                     for m in range(m0, m0 + tiles):
-                        store(m, False)
-                    if m0 < 4:
-                        v_interleave(scalar_jobs[EARLY + m0 // 2], False)
-            store(MT - 1, True, 2)
+                        store(m)
+                    if m0 // 2 < len(late):
+                        on_scalar(late[m0 // 2], 1 + EARLY_JOBS + m0 // 2)
+
+            result = float_tile("result_last", [P, H])
+            for part in range(2):
+                cols = slice(H // 2 * part, H // 2 * (part + 1))
+                nc.vector.tensor_scalar(
+                    out=result[:, cols], in0=acc[MT - 1][:, cols], scalar1=float(B) ** -0.5, scalar2=None, op0=ALU.mult
+                )
+                nc.sync.dma_start(out=out[P * (MT - 1) :, cols], in_=result[:, cols])

@@ -248,7 +248,7 @@ def tile_persistentmeanfieldisingrbmgradient_w4_kernel(
                 return src.rearrange("p t (c i) -> p c t i", i=RUN)
 
             def gpsimd_share(g):
-                rest = H_REST if g + 2 >= G else 0
+                rest = 0 if g == 1 else H_REST
                 nc.gpsimd.tensor_scalar(
                     out=interleaved(h_place(g, rest, 2 * H - rest)),
                     in0=by_runs(h_rows[g][:, :, rest : 2 * H - rest]),
@@ -258,9 +258,9 @@ def tile_persistentmeanfieldisingrbmgradient_w4_kernel(
                     op1=ALU.add,
                 )
 
-            def h_rest(g, which):
+            def h_rest(g, which, copy):
                 first = (H - H_REST) * which
-                nc.scalar.copy(
+                copy(
                     out=interleaved(h_place(g, H * which + first, H * which + first + H_REST)),
                     in_=by_runs(h_source(g, which)[:, :, first : first + H_REST]),
                 )
@@ -396,6 +396,7 @@ def tile_persistentmeanfieldisingrbmgradient_w4_kernel(
                 if g + 2 < G:
                     quantise(hf_mx, g + 2, 0, PASS, hf_staged[g + 2][:])
                 elif g == G - 1:
+                    h_rest(0, 1, nc.vector.tensor_copy)
                     v1_quantise(0, 1)
                 quantise(hn_mx, g, 0, H, h_place(g, 0, H))
                 v1_quantise(g, 0)
@@ -421,10 +422,12 @@ def tile_persistentmeanfieldisingrbmgradient_w4_kernel(
                                 field(ahead)
                 if turns_hf:
                     hf_copy_out(*hf_left[q - 1], nc.scalar.copy)
-                if second and g + 2 >= G:
-                    h_rest(g, 0)
-                    h_rest(g, 1)
-                elif q:
+                if q == 0:
+                    h_rest(g, 0, nc.scalar.copy)
+                elif second and g + 2 >= G:
+                    h_rest(g, 0, nc.scalar.copy)
+                    h_rest(g, 1, nc.scalar.copy)
+                else:
                     widen_next(1)
                 for unit in fields_left:
                     if unit not in field_bank:

from contextlib import ExitStack

import concourse.mybir as mybir
from concourse.masks import make_identity

B, V, H = 2048, 1024, 512
FLOPS = 3 * 2 * B * V * H

F32 = mybir.dt.float32
BF16 = mybir.dt.bfloat16
U32 = mybir.dt.uint32
I32 = mybir.dt.int32
U8 = mybir.dt.uint8
E4M3 = mybir.dt.float8_e4m3fn
E4M3X4 = mybir.dt.float8_e4m3fn_x4
E2M1X4 = mybir.dt.float4_e2m1fn_x4
ACT = mybir.ActivationFunctionType
ALU = mybir.AluOpType

P = 128
SLOTS = 4
PASS = P * SLOTS
G = B // PASS
MT = V // P
HALF = V // 2
QUAD = 4
QUADS = G * MT // QUAD
LEAD = 6
RUN = 4

H_REST = 40
WARM_FRONT = 7
WARM_MID = 2
EARLY_JOBS = 2
LATE_GROUP = 2


def tile_persistentmeanfieldisingrbmgradient_w4_kernel(
    tc, v_bytes, v_scale, hp, hf, hn, w_words, w_scales, b, s, out
):
    nc = tc.nc
    with ExitStack() as ctx:
        keep = ctx.enter_context(tc.tile_pool(name="keep", bufs=1))
        ring = ctx.enter_context(tc.tile_pool(name="ring", bufs=1))
        psum = ctx.enter_context(tc.psum_pool(name="psum", bufs=1))

        def kept(name, shape, dtype, align=64):
            return keep.tile(shape, dtype, name=name, align_bytes=align)

        def reused(name, shape, dtype, tag, bufs=1):
            return ring.tile(shape, dtype, name=name, tag=tag, bufs=bufs, align_bytes=256)

        def mx_operand(name, width):
            codes = kept("%s_codes" % name, [P, G * width], U32, 256)
            scales = kept("%s_scales" % name, [P, G * width], U8, 256)
            groups = [slice(width * g, width * g + width) for g in range(G)]
            return [codes[:, cols] for cols in groups], [scales[:, cols] for cols in groups]

        turns = {
            "turn": ["bank%d" % i for i in range(QUAD)],
            "field": ["bank%d" % i for i in range(QUAD, 2 * QUAD)],
        }

        def next_bank(kind, shape, for_good=False, dtype=F32):
            name = turns[kind][0]
            turns[kind].remove(name)
            if not for_good:
                turns[kind].append(name)
            return psum.tile(shape, dtype, name=name, tag=name)

        hf_rows = [reused("hf_rows%d" % g, [P, SLOTS * H], BF16, "rows%d" % g) for g in range(G)]
        h_rows = [kept("h_rows%d" % g, [P, SLOTS, 2 * H], BF16) for g in range(G)]
        h_staged = kept("h_staged", [P, SLOTS * (G + 1) * H], BF16, 256)
        v_rows = {g: kept("v_rows%d" % g, [P, SLOTS, V], U8) for g in range(2, G)}
        v_rows_second = [kept("v_rows_second%d" % half, [P, SLOTS, HALF], U8) for half in range(2)]
        v_rows_first = [kept("v_rows_first%d" % pair, [P, 2, V], U8) for pair in range(2)]
        v_wide = {(0, g): kept("v_wide0_%d" % g, [P, SLOTS, HALF], BF16) for g in range(G)}
        v_wide[(1, 0)] = kept("v_wide1_0", [P, SLOTS, HALF], BF16)
        hf_mx = mx_operand("hf", PASS)
        hn_mx = mx_operand("hn", H)
        hp_mx = mx_operand("hp", H)
        v1_mx = mx_operand("v1", V)
        v_mx = mx_operand("v", V)
        w_codes = kept("w_codes", [P, 2 * V], U8, 256)
        w_plane = kept("w_plane", [P, V], U8, 256)
        ident = kept("ident", [P, P], F32)
        b_rows = kept("b_rows", [P, P], BF16)
        ident16 = kept("ident16", [P, P], BF16)
        bias = kept("bias", [P, MT], BF16)
        s_neg = kept("s_neg", [P, G, SLOTS], F32)
        s_rows = kept("s_rows", [P, G, SLOTS], BF16)
        scale_later = kept("scale_later", [P, G - 1, SLOTS], F32)
        scale_first = kept("scale_first", [P, SLOTS], F32)
        zeros = kept("zeros", [P, PASS], BF16)
        table_warm = kept("table_warm", [P, 1], F32)

        with tc.manual_schedule():
            nc.vector.memset(table_warm[:], 0.0)
            nc.vector.memset(b_rows[:], 0.0)
            nc.vector.memset(zeros[:], 0.0)
            nc.vector.memset(w_plane[:].bitcast(I32), 0)
            make_identity(nc, ident[:])
            make_identity(nc, ident16[:])
            scale_view = v_scale.rearrange("(g p t) o -> p g (t o)", p=P, t=SLOTS)
            nc.scalar.dma_start(out=scale_first[:], in_=scale_view[:, 0, :])
            nc.scalar.activation(table_warm[:], table_warm[:], ACT.Tanh)

            def group_rows(x, g):
                return x.rearrange("(g p t) c -> g p t c", p=P, t=SLOTS)[g]

            def h_source(g, which):
                return h_rows[g][:, :, H * which : H * (which + 1)]

            def load_h(g, which):
                nc.sync.dma_start(out=h_source(g, which), in_=group_rows((hn, hp)[which], g))

            def load_hf(g, pair):
                nc.sync.dma_start(
                    out=hf_rows[g][:, 2 * H * pair : 2 * H * (pair + 1)],
                    in_=group_rows(hf, g)[:, 2 * pair : 2 * pair + 2, :].rearrange("p t c -> p (t c)"),
                )

            def load_v_second(half):
                cols = slice(HALF * half, HALF * half + HALF)
                nc.sync.dma_start(out=v_rows_second[half][:], in_=group_rows(v_bytes, 1)[:, :, cols])

            for pair in range(2):
                nc.sync.dma_start(out=v_rows_first[pair][:], in_=group_rows(v_bytes, 0)[:, 2 * pair : 2 * pair + 2, :])
            load_hf(0, 0)
            load_hf(0, 1)
            nc.sync.dma_start(out=b_rows[0:MT, :], in_=b.rearrange("(m c) -> m c", c=P))
            load_hf(1, 0)
            load_hf(1, 1)
            nc.sync.dma_start(out=w_codes[:], in_=w_words[0])
            for q in range(4):
                nc.sync.dma_start(
                    out=w_plane[32 * q : 32 * q + 4, :].bitcast(I32),
                    in_=w_scales[0][4 * q : 4 * q + 4, :].bitcast(I32),
                )
            nc.sync.dma_start(out=s_rows[:], in_=s.rearrange("(g p t) -> p g t", p=P, t=SLOTS))
            load_hf(2, 0)
            load_h(0, 0)
            load_h(0, 1)
            load_hf(2, 1)
            nc.sync.dma_start(out=scale_later[:], in_=scale_view[:, 1:G, :])
            load_v_second(0)
            for part in range(2):
                load_h(1, part)
                load_hf(3, part)
            load_v_second(1)
            for g in range(2, G):
                nc.sync.dma_start(out=v_rows[g][:], in_=group_rows(v_bytes, g))
                load_h(g, 0)
                load_h(g, 1)

            def quantise(operand, g, col, width, src):
                codes, scales = operand
                nc.vector.quantize_mx(
                    out=codes[g][:, col : col + width].bitcast(E4M3X4),
                    scales=scales[g][:, col : col + width],
                    in_=src,
                )

            def staging(name, number):
                return reused(name, [P, SLOTS * PASS], BF16, "staging%d" % number)

            def h_place(g, first, last):
                base = SLOTS * H * (G - 1 - g)
                return h_staged[:, base + SLOTS * first : base + SLOTS * last]

            hf_staged = {}
            hf_bank = {}

            def turn_slot(place, g, t):
                words = hf_rows[g][:].bitcast(F32)
                for u in range(2):
                    nc.tensor.transpose(place[:, :, u], words[:, H // 2 * t + u : H // 2 * (t + 1) : 2], ident[:])

            def hf_turn(g, pair, kind):
                if pair == 0:
                    hf_staged[g] = staging("hf_staged%d" % g, (0, 3, 2, 0)[g])
                hf_bank[(g, pair)] = next_bank(kind, [P, 2, P, 2])
                for i in range(2):
                    turn_slot(hf_bank[(g, pair)][:, i, :, :], g, 2 * pair + i)

            def hf_copy_out(g, pair, copy):
                copy(
                    out=hf_staged[g][:, 2 * PASS * pair : 2 * PASS * (pair + 1)].bitcast(F32),
                    in_=hf_bank[(g, pair)][:].rearrange("p i r u -> p (i r u)"),
                )

            ident_pairs = ident[:].rearrange("p (a e) -> p a e", e=2)
            field_bank = {}
            tanh_tile = {}
            turned_bank = {}
            v1_staged = {}

            def field(unit):
                g, m = divmod(unit, MT)
                field_bank[unit] = next_bank("field", [P, PASS])
                nc.tensor.matmul_mx(
                    out=field_bank[unit][:],
                    lhsT=w_codes[:, 2 * P * m : 2 * P * (m + 1)].bitcast(E2M1X4),
                    lhsT_scale=w_plane[:, P * m : P * (m + 1)],
                    rhs=hf_mx[0][g][:].bitcast(E4M3X4),
                    rhs_scale=hf_mx[1][g][:],
                    start=True,
                    stop=True,
                )

            def float_tile(name, shape):
                return reused(name, shape, F32, "float_tile", 2 * QUAD)

            def tanh(unit):
                m = unit % MT
                tanh_tile[unit] = float_tile("tanh%d" % unit, [P, SLOTS, P])
                nc.scalar.activation(
                    tanh_tile[unit][:].rearrange("p t r -> p (t r)"),
                    field_bank[unit][:],
                    ACT.Tanh,
                    bias=bias[:, m : m + 1],
                )

            def turn(unit):
                turned_bank[unit] = next_bank("turn", [P, P // 2, SLOTS, 2])
                for t in range(SLOTS):
                    nc.tensor.transpose(turned_bank[unit][:, :, t, :], tanh_tile[unit][:, t, :], ident_pairs)

            def weight(unit):
                g, m = divmod(unit, MT)
                half, c = divmod(m, MT // 2)
                if c == 0:
                    v1_staged[(g, half)] = staging("v1_staged%d_%d" % (g, half), (3 + g) % 6 if half else 1 + g % 2)
                nc.vector.tensor_tensor(
                    out=v1_staged[(g, half)][:, PASS * c : PASS * (c + 1)].rearrange("p (a e t) -> p a t e", e=2, t=SLOTS),
                    in0=turned_bank[unit][:],
                    in1=s_neg[:, g, :].unsqueeze(1).unsqueeze(3).to_broadcast([P, P // 2, SLOTS, 2]),
                    op=ALU.mult,
                )

            def v1_quantise(g, half):
                quantise(v1_mx, g, HALF * half, HALF, v1_staged[(g, half)][:])

            def interleaved(dst):
                return dst.rearrange("p (c i t) -> p c t i", i=RUN, t=SLOTS)

            def by_runs(src):
                return src.rearrange("p t (c i) -> p c t i", i=RUN)

            def gpsimd_share(g):
                rest = 0 if g == 1 else H_REST
                nc.gpsimd.tensor_scalar(
                    out=interleaved(h_place(g, rest, 2 * H - rest)),
                    in0=by_runs(h_rows[g][:, :, rest : 2 * H - rest]),
                    scalar1=1.0,
                    scalar2=0.0,
                    op0=ALU.mult,
                    op1=ALU.add,
                )

            def h_rest(g, which, copy):
                first = (H - H_REST) * which
                copy(
                    out=interleaved(h_place(g, H * which + first, H * which + first + H_REST)),
                    in_=by_runs(h_source(g, which)[:, :, first : first + H_REST]),
                )

            def hp_quantise(g):
                quantise(hp_mx, g, 0, H, h_place(g, H, 2 * H))

            def widen_first(t, half, on_vector):
                dst = v_wide[(half, 0)][:, t, :]
                src = v_rows_first[t // 2][:, t % 2, HALF * half : HALF * half + HALF].bitcast(E4M3)
                scale = scale_first[:, t : t + 1]
                if on_vector:
                    nc.vector.tensor_scalar(out=dst, in0=src, scalar1=scale, scalar2=None, op0=ALU.mult)
                else:
                    nc.scalar.activation(dst, src, ACT.Copy, scale=scale)

            def widen(half, g, t):
                if (half, g) not in v_wide:
                    v_wide[(half, g)] = reused("v_wide1_%d" % g, [P, SLOTS, HALF], BF16, "rows%d" % g)
                if g == 1:
                    src = v_rows_second[half][:, t, :]
                else:
                    src = v_rows[g][:, t, HALF * half : HALF * half + HALF]
                nc.scalar.activation(
                    v_wide[(half, g)][:, t, :], src.bitcast(E4M3), ACT.Copy, scale=scale_later[:, g - 1, t : t + 1]
                )

            v_staged = {}

            def v_interleave(job, place, copy):
                m0, tiles, g = job
                half, first = divmod(P * m0, HALF)
                v_staged[job] = place
                copy(out=interleaved(place), in_=by_runs(v_wide[(half, g)][:, :, first : first + P * tiles]))

            def on_scalar(job, number):
                place = staging("v_staged%d_%d" % (job[0], job[2]), number)
                v_interleave(job, place[:, 0 : PASS * job[1]], nc.scalar.copy)

            def on_vector(job):
                place = reused("v_staged%d_%d" % (job[0], job[2]), [P, PASS * job[1]], BF16, "v_staged", 5)
                v_interleave(job, place[:], nc.vector.tensor_copy)

            def v_quantise(job):
                m0, tiles, g = job
                quantise(v_mx, g, P * m0, P * tiles, v_staged[job])

            acc = []

            def correlate(m, vis_mx, hid_mx, g, first=False, last=False):
                nc.tensor.matmul_mx(
                    out=acc[m][:],
                    lhsT=vis_mx[0][g][:, P * m : P * (m + 1)].bitcast(E4M3X4),
                    lhsT_scale=vis_mx[1][g][:, P * m : P * (m + 1)],
                    rhs=hid_mx[0][g][:].bitcast(E4M3X4),
                    rhs_scale=hid_mx[1][g][:],
                    start=first,
                    stop=last,
                )

            def open_early():
                acc.append(next_bank("field", [P, H], True))
                for g in range(G - 1):
                    correlate(len(acc) - 1, v1_mx, hn_mx, g, first=g == 0)

            def store(m):
                result = float_tile("result%d" % m, [P, H])
                nc.scalar.activation(result[:], acc[m][:], ACT.Copy, scale=float(B) ** -0.5)
                nc.sync.dma_start(out=out[P * m : P * (m + 1), :], in_=result[:])

            warm_bank = psum.tile([P, PASS], F32, name="warm_bank", tag="bank7")

            def warm_up(count):
                for i in range(count):
                    nc.tensor.matmul(warm_bank[:], lhsT=zeros[:, 0:P], rhs=zeros[:], start=True, stop=True)

            warm_up(WARM_FRONT)
            widen_first(0, 1, False)
            widen_first(0, 0, False)
            widen_first(3, 0, False)
            widen_first(1, 1, True)
            widen_first(1, 0, True)
            widen_first(2, 1, True)
            widen_first(3, 1, True)
            widen_first(2, 0, True)
            second_half, first_pair, second_pair = (MT // 2, MT // 2, 0), (0, 2, 0), (2, 2, 0)
            hf_turn(0, 0, "turn")
            last_banks = []
            for t in range(2, SLOTS):
                last_banks.append(next_bank("field", [P, P, 2]))
                turn_slot(last_banks[-1][:], 0, t)
            v_interleave(second_half, staging("v_staged_half", 5)[:], nc.vector.tensor_copy)
            bias_bank = next_bank("turn", [P, P], dtype=BF16)
            nc.tensor.transpose(bias_bank[:], b_rows[:], ident16[:])
            warm_up(WARM_MID)
            hf_turn(1, 0, "turn")
            hf_turn(1, 1, "turn")
            hf_copy_out(0, 0, nc.scalar.copy)
            for t in range(2, SLOTS):
                nc.scalar.copy(
                    out=hf_staged[0][:, PASS * t : PASS * (t + 1)].bitcast(F32),
                    in_=last_banks[t - 2][:].rearrange("p r u -> p (r u)"),
                )
            quantise(hf_mx, 0, 0, 2 * P, hf_staged[0][:, 0 : 2 * PASS])
            for t in range(2, SLOTS):
                quantise(hf_mx, 0, P * t, P, hf_staged[0][:, PASS * t : PASS * (t + 1)])
            v_quantise(second_half)
            on_scalar(first_pair, 1)
            nc.scalar.copy(out=bias[:], in_=bias_bank[:, 0:MT])
            v_interleave(second_pair, h_place(0, 2 * P, 4 * P), nc.vector.tensor_copy)
            hf_copy_out(1, 0, nc.vector.tensor_copy)
            for unit in range(QUAD):
                field(unit)
            hf_turn(2, 0, "turn")
            hf_copy_out(1, 1, nc.vector.tensor_copy)
            v_quantise(first_pair)
            for unit in range(LEAD - QUAD):
                tanh(unit)
                field(unit + QUAD)
            nc.scalar.activation(s_neg[:], s_rows[:], ACT.Copy, scale=-1.0)
            hf_copy_out(2, 0, nc.vector.tensor_copy)
            v_quantise(second_pair)
            quantise(hf_mx, 1, 0, PASS, hf_staged[1][:])

            to_widen = [(half, g, t) for half in range(2) for g in range(1, G) for t in range(SLOTS)]

            def widen_next(count):
                for item in to_widen[:count]:
                    widen(*item)
                    to_widen.remove(item)

            def stretch(g):
                if g + 2 < G:
                    quantise(hf_mx, g + 2, 0, PASS, hf_staged[g + 2][:])
                elif g == G - 1:
                    h_rest(0, 1, nc.vector.tensor_copy)
                    v1_quantise(0, 1)
                quantise(hn_mx, g, 0, H, h_place(g, 0, H))
                v1_quantise(g, 0)

            units = G * MT
            hf_left = [(2, 1), (3, 0), (3, 1)]
            for q in range(QUADS):
                g, second = divmod(q, 2)
                first = QUAD * q
                turns_hf = 1 <= q <= len(hf_left)
                fields_left = [unit for unit in range(first + LEAD, first + LEAD + QUAD) if unit < units]
                if not second:
                    gpsimd_share(g)
                for unit in range(first + LEAD - QUAD, min(first + LEAD, units)):
                    tanh(unit)
                for unit in range(first, first + QUAD):
                    turn(unit)
                    if unit == first + 1:
                        if turns_hf:
                            hf_turn(*hf_left[q - 1], "field")
                        elif q:
                            for ahead in fields_left[:2]:
                                field(ahead)
                if turns_hf:
                    hf_copy_out(*hf_left[q - 1], nc.scalar.copy)
                if q == 0:
                    h_rest(g, 0, nc.scalar.copy)
                elif second and g + 2 >= G:
                    h_rest(g, 0, nc.scalar.copy)
                    h_rest(g, 1, nc.scalar.copy)
                else:
                    widen_next(1)
                for unit in fields_left:
                    if unit not in field_bank:
                        field(unit)
                if q == QUADS - 2:
                    open_early()
                if q == QUADS - 1:
                    for m in range(1, MT // 2):
                        open_early()
                for unit in range(first, first + QUAD):
                    weight(unit)
                if second:
                    stretch(g)

            hp_quantise(0)
            for m in range(MT // 2, MT):
                acc.append(next_bank("turn", [P, H], True))
                correlate(m, v1_mx, hn_mx, 0, first=True)
            for m in range(MT // 2):
                correlate(m, v1_mx, hn_mx, G - 1)
            for m in range(MT):
                correlate(m, v_mx, hp_mx, 0)

            jobs = [(m0, 2, g) for m0 in range(0, MT - 2, 2) for g in range(1, G)]
            jobs = jobs + [(m, 1, g) for m in range(MT - 2, MT) for g in range(1, G)]
            early = [(2, 2, g) for g in range(1, 1 + EARLY_JOBS)]
            late = [(m, 1, LATE_GROUP) for m in range(MT - 2, MT)]
            widen_next(len([item for item in to_widen if item[0] == 0]))
            for number, job in enumerate(early):
                on_scalar(job, 1 + number)
            widen_next(len(to_widen))

            on_vector(jobs[0])
            for index, job in enumerate(jobs):
                m0, tiles, g = job
                if m0 == 0:
                    hp_quantise(g)
                ahead = [other for other in jobs[index + 1 : index + 3] if other not in list(v_staged) + late]
                if ahead:
                    on_vector(ahead[0])
                v_quantise(job)
                for m in range(m0, m0 + tiles):
                    correlate(m, v_mx, hp_mx, g, last=g == G - 1)
                if index % 2 == 0 and index // 2 + 1 < G:
                    v1_quantise(index // 2 + 1, 1)
                    for m in range(MT // 2, MT):
                        correlate(m, v1_mx, hn_mx, index // 2 + 1)
                if g == G - 1 and m0 < MT - 1:
                    for m in range(m0, m0 + tiles):
                        store(m)
                    if m0 // 2 < len(late):
                        on_scalar(late[m0 // 2], 1 + EARLY_JOBS + m0 // 2)

            result = float_tile("result_last", [P, H])
            for part in range(2):
                cols = slice(H // 2 * part, H // 2 * (part + 1))
                nc.vector.tensor_scalar(
                    out=result[:, cols], in0=acc[MT - 1][:, cols], scalar1=float(B) ** -0.5, scalar2=None, op0=ALU.mult
                )
                nc.sync.dma_start(out=out[P * (MT - 1) :, cols], in_=result[:, cols])
